import numpy as np, ml_dtypes
CORES = [2,6,10,14,18,22,26,30]
N = 8
BF = ml_dtypes.bfloat16
def f(rng, *shape):
    return (rng.standard_normal(shape, dtype=np.float32) * np.exp2(rng.integers(-2, 3, shape[:-1] + (1,)))).astype(BF)
def wide(rng, *shape):
    v = f(rng, *shape).astype(np.float32); k = shape[:-2] + (1, shape[-1])
    return (v * np.exp2(rng.integers(-6, 7, k)) * (rng.random(k) > 0.0625)).astype(BF)
def gentries(a):
    return np.ascontiguousarray(a.reshape(8, 16, -1).transpose(0, 2, 1)).reshape(8, -1)
def gtable(e):
    e = np.asarray(e); return np.ascontiguousarray(e.reshape(8, -1, 16).transpose(0, 2, 1)).reshape(128, -1).astype(np.int32)
WAY = "abcd"; W = len(WAY)
IC, CG, CAPP, TOT, S = 2048, 256, 256, 2048, 512
def numbers(a):
    return np.stack([gentries(u) for u in a])
def slots(a):
    return np.stack([gentries(u) for u in a]).reshape(N, N, CAPP)
def columns(t, a):
    e = slots(a); t = t.astype(np.float64)
    return np.stack([np.concatenate([t[q][:, e[q, r]] for q in range(N)], axis=1) for r in range(N)])
def sums(t, x):
    return np.stack([np.bincount(x, weights=t[o], minlength=TOT) for o in range(16)])
def home(p, a):
    e = slots(a); y = np.zeros((N, 16, IC), np.float64)
    for q in range(N):
        for r in range(N):
            y[q][:, e[q, r]] += p[r][:, q * CAPP:(q + 1) * CAPP]
    return y
def anyslots(rng):
    return np.argsort(rng.random((W, N, N, IC)), axis=-1)[..., :CAPP]
def anynumbers(rng):
    x = rng.integers(0, TOT, (W, N, 8, S)); few = rng.integers(0, TOT, (W, N, 8, 32))
    return np.where(rng.random(x.shape) < 0.5, np.take_along_axis(few, rng.integers(0, 32, x.shape), axis=-1), x)
def make(rng, x, e):
    o = np.argsort(x[0], axis=-1, kind="stable"); x = np.stack([np.take_along_axis(u, o, axis=-1) for u in x])
    ob = np.lexsort((rng.random(x[1].shape), x[1]), axis=-1)
    d = {"f" + c: f(rng, N, 16, IC) for c in WAY}
    d["v"] = (rng.standard_normal((N, 8, S)) * np.exp2(rng.integers(-1, 2, (N, 8, 1)))).astype(np.float32)
    for w, c in enumerate(WAY): d["x" + c] = np.stack([gtable(u) for u in x[w]])
    d["ob"] = np.stack([gtable(u) for u in ob])
    for w, c in enumerate(WAY): d["l" + c] = np.stack([gtable(u.reshape(8, CG)) for u in e[w]])
    return d
def setup_inputs(rng):
    return make(rng, anynumbers(rng), anyslots(rng))
def setup_inputs_runs(rng):
    x = anynumbers(rng); h = rng.integers(0, TOT, (W, N, 8, 1))
    for w in range(W): x[w, :, :, w * S // 8:w * S // 8 + S // 2] = h[w]
    x[0, :, 0:2] = h[0, :, 0:1]; x[1, :, 1:3] = h[1, :, 1:2]
    return make(rng, x, anyslots(rng))
def setup_inputs_apart(rng):
    x = np.argsort(rng.random((W, N, 8 * S // TOT, TOT)), axis=-1).reshape(W, N, 8, S)
    return make(rng, x, anyslots(rng))
def setup_inputs_ends(rng):
    x = rng.integers(0, N, (W, N, 8, S)) * CAPP + rng.integers(0, 2, (W, N, 8, S)) * (CAPP - 1)
    x = np.where(rng.random(x.shape) < 0.75, x, rng.integers(0, TOT, x.shape)); x[..., 0] = 0; x[..., 1] = TOT - 1
    e = 1 + np.argsort(rng.random((W, N, N, IC - 2)), axis=-1)[..., :CAPP]; e[..., 0] = IC - 1; e[..., -1] = 0
    return make(rng, x, e)
def setup_inputs_alike(rng):
    x = anynumbers(rng); x[:, :, 1:] = x[:, :, :1].copy()
    e = np.repeat(np.argsort(rng.random((W, N, 1, IC)), axis=-1)[..., :CAPP], N, axis=2)
    return make(rng, x, e)
def setup_inputs_spread(rng):
    d = setup_inputs(rng)
    for c in WAY[1:]: d["f" + c] = wide(rng, N, 16, IC)
    return d
def check_inputs(d):
    bad = []
    for c in WAY:
        x = numbers(d["x" + c]); e = slots(d["l" + c])
        if not np.isfinite(d["f" + c].astype(np.float32)).all(): bad.append("finite_f" + c)
        if x.min() < 0 or x.max() >= TOT: bad.append("range_x" + c)
        if e.min() < 0 or e.max() >= IC: bad.append("range_l" + c)
        if (np.diff(np.sort(e, axis=-1), axis=-1) == 0).any(): bad.append("different_l" + c)
    if not np.isfinite(d["v"]).all(): bad.append("finite_v")
    if (np.diff(numbers(d["xa"]), axis=-1) < 0).any(): bad.append("sorted_xa")
    o = numbers(d["ob"])
    if not (np.sort(o, axis=-1) == np.arange(S)).all(): bad.append("places_ob")
    elif (np.diff(np.take_along_axis(numbers(d["xb"]), o, axis=-1), axis=-1) < 0).any(): bad.append("sorted_xb_by_ob")
    return bad
def reference(fa, fb, fc, fd, v, xa, xb, xc, xd, ob, la, lb, lc, ld):
    xi = numbers(xa).reshape(N, 8 * S); xj = numbers(xb).reshape(N, 8 * S)
    w = np.repeat(v.astype(np.float64).reshape(N, 1, 8 * S), 16, axis=1)
    for t, x, a in ((fc, xc, lc), (fd, xd, ld),):
        u = columns(t, a); x = numbers(x).reshape(N, 8 * S)
        w = w * np.stack([u[r][:, x[r]] for r in range(N)])
    u = columns(fb, lb)
    ya = fa.astype(np.float64) * home([sums(w[r] * u[r][:, xj[r]], xi[r]) for r in range(N)], la)
    u = columns(ya, la)
    yb = home([sums(w[r] * u[r][:, xi[r]], xj[r]) for r in range(N)], lb)
    return {"ya": ya.astype(np.float32), "yb": yb.astype(np.float32)}

@@ -1,0 +1,382 @@
+from concourse.bass import DstId, RemoteDMATransfer
+from concourse.mybir import AluOpType as OP, ActivationFunctionType as AF
+
+F, B, I, U = "float32", "bfloat16", "int32", "uint16"
+SCRATCH = {
+    "din": ("sbuf", [128, 2048], B), "bin": ("sbuf", [128, 2048], B), "frc": ("sbuf", [128, 2048], B),
+    "frd": ("sbuf", [128, 2048], B), "frb": ("sbuf", [128, 2048], B), "fra": ("sbuf", [128, 2048], B),
+    "lt": ("sbuf", [128, 64], I), "lu": ("sbuf", [128, 64], U),
+    "xt": ("sbuf", [128, 128], I), "xr": ("sbuf", [128, 128], I), "xo": ("sbuf", [128, 128], I), "xu": ("sbuf", [128, 128], U),
+    "obt": ("sbuf", [128, 32], I), "obu": ("sbuf", [128, 32], U),
+    "vin": ("sbuf", [128, 512], F), "vr": ("sbuf", [128, 512], F),
+    "pc": ("sbuf", [128, 8], I), "dj": ("sbuf", [128, 256], I), "gm": ("sbuf", [128, 128], I), "jt": ("sbuf", [128, 32], I),
+    "pi": ("sbuf", [128, 8], I), "pg": ("sbuf", [128, 8], I), "col": ("sbuf", [128, 8], F),
+    "di": ("sbuf", [128, 128], I), "dk": ("sbuf", [128, 256], I), "d16": ("sbuf", [128, 512], F), "e2": ("sbuf", [128, 64], F),
+    "eb": ("sbuf", [128, 128], B), "i2f": ("sbuf", [128, 256], F), "i2b": ("sbuf", [128, 256], B),
+    "sh1": ("sbuf", [128, 128], F), "sh2": ("sbuf", [128, 128], F), "b8": ("sbuf", [128, 128], F),
+    "gf": ("sbuf", [128, 128], F), "jf": ("sbuf", [128, 32], F),
+    "xf": ("sbuf", [128, 66], F), "y1": ("sbuf", [128, 1056], F), "fla": ("sbuf", [128, 512], F),
+    "flb": ("sbuf", [128, 512], F), "fbp": ("sbuf", [128, 512], F),
+    "ma": ("sbuf", [128, 512], F), "mb": ("sbuf", [128, 512], F),
+    "sa1": ("sbuf", [128, 32], F), "sa2": ("sbuf", [128, 32], F), "sau": ("sbuf", [128, 32], U), "sbu": ("sbuf", [128, 32], U),
+    "ba": ("sbuf", [128, 1024], F), "t1": ("sbuf", [128, 512], F), "t2": ("sbuf", [128, 256], F),
+    "t3": ("sbuf", [128, 128], F), "t4": ("sbuf", [128, 64], F), "xg": ("sbuf", [128, 40], F),
+    "ai": ("sbuf", [128, 32], I), "aj": ("sbuf", [128, 32], I), "au": ("sbuf", [128, 32], U),
+    "gd": ("sbuf", [128, 256], B), "gk": ("sbuf", [128, 256], B), "gb": ("sbuf", [128, 256], B),
+    "sndd": ("dram", [1024, 32], B), "landd": ("dram", [1024, 32], B),
+    "sndc": ("dram", [1024, 32], B), "landc": ("dram", [1024, 32], B),
+    "sndb": ("dram", [1024, 32], B), "landb": ("dram", [1024, 32], B),
+    "snda": ("dram", [1024, 32], F), "landa": ("dram", [1024, 32], F),
+    "td": ("sbuf", [128, 2048], B), "tc": ("sbuf", [128, 2048], B), "tb": ("sbuf", [128, 2048], B), "ta": ("sbuf", [128, 2048], F),
+    "w1": ("sbuf", [128, 512], F), "w2": ("sbuf", [128, 512], F), "wp": ("sbuf", [128, 512], F),
+    "pr1": ("sbuf", [128, 512], F), "pr2": ("sbuf", [128, 512], F), "sg1": ("sbuf", [128, 512], F), "sg2": ("sbuf", [128, 512], F),
+    "P1": ("sbuf", [128, 2560], F), "P2": ("sbuf", [128, 2560], F), "Z1": ("sbuf", [128, 2048], F), "Z2": ("sbuf", [128, 2048], F),
+    "r1": ("sbuf", [128, 256], F), "r2": ("sbuf", [128, 256], F), "u3": ("sbuf", [128, 256], F), "r3": ("sbuf", [128, 256], F),
+    "lp1": ("sbuf", [128, 256], F), "lq1": ("sbuf", [128, 256], F), "lp2": ("sbuf", [128, 256], F), "lq2": ("sbuf", [128, 256], F),
+    "yar": ("sbuf", [128, 2048], F), "ga": ("sbuf", [128, 256], F),
+    "ps0": ("psum", [128, 512], F), "ps1": ("psum", [128, 512], F), "ps2": ("psum", [128, 512], F), "ps3": ("psum", [128, 512], F),
+    "ps4": ("psum", [128, 512], F), "ps5": ("psum", [128, 512], F), "ps6": ("psum", [128, 512], F), "ps7": ("psum", [128, 512], F),
+}
+EXCH = ["d", "c", "b", "a"]
+SEMAPHORES = (["c_g", "c_v", "c_s", "c_p", "ldd", "ldl1", "ldl2", "ldl3", "ldc", "ldb", "lda", "ldx", "ldo", "ldv", "oya", "oyb"]
+              + [k + x for x in EXCH for k in ("snd", "self", "arr", "loc", "cmp", "rot")]
+              + [k + x for x in ("p1", "p2") for k in ("arr", "loc")])
+
+
+def ways(src, cores, topo):
+    off = [d for d in cores if topo.chip(d) != topo.chip(src)]
+    on = [d for d in cores if d != src and topo.chip(d) == topo.chip(src)]
+    far = [d for d in off if not topo.mates(topo.chip(src), topo.chip(d)) and not topo.same_plane(topo.chip(src), topo.chip(d))]
+    return far, [d for d in off if d not in far], on
+
+
+def send_engines(src, cores, topo):
+    far, near, on = ways(src, cores, topo)
+    e = topo.engines(src, near[0])
+    one, two = e[0::2], e[1::2]
+    n = len(two) // len(far)
+    p = {d: [one[i]] for i, d in enumerate(near)}
+    p.update({d: two[i * n:(i + 1) * n] for i, d in enumerate(far)})
+    for i, d in enumerate(on):
+        p[d] = [x for x in topo.engines(src, d) if x not in e][i:i + 1]
+    return p
+
+
+def sum_calls(src, cores, topo):
+    far, near, on = ways(src, cores, topo)
+    off = far + near
+    e = topo.engines(src, off[0])
+    n = len(e) // 2
+    calls = [[(off[2 * k], e[0:n]), (off[2 * k + 1], e[n:2 * n])] for k in range(len(off) // 2)]
+    for d in on:
+        calls[-1].append((d, [x for x in topo.engines(src, d) if x not in e][0:n]))
+    return calls
+
+
+def rank_program(g, core, T, topo):
+    me = T.rank_of(core)
+    if me is None:
+        return
+    cores = list(T.cores)
+    eng = {"g": g, "v": g.vector, "s": g.scalar, "p": g.tensor, "y": g.sync}
+    seen = {q: {} for q in eng}
+    cnt, WR, RD = {}, {}, {}
+
+    def need(q, toks):
+        m = {}
+        for s, n in toks:
+            n = cnt[s] if n is None else n
+            m[s] = max(m.get(s, 0), n)
+        for s in m:
+            if seen[q].get(s, 0) < m[s]:
+                eng[q].wait_ge(T.sem[s], m[s])
+                seen[q][s] = m[s]
+
+    def before(q, rd, wr, own=None):
+        own = own or q
+        toks = []
+        for k in rd:
+            toks += [t for _, t in WR.get(k, [])]
+        for k in wr:
+            toks += [t for o, t in WR.get(k, []) + RD.get(k, []) if o != own]
+        need(q, toks)
+
+    def after(o, tok, rd, wr):
+        for k in rd:
+            RD.setdefault(k, []).append((o, tok))
+        for k in wr:
+            WR.setdefault(k, []).append((o, tok))
+
+    def run(q, fn, rd, wr, *a, **k):
+        before(q, rd, wr)
+        s = "c_" + q
+        cnt[s] = cnt.get(s, 0) + 1
+        fn(*a, **k).then_inc(T.sem[s], 1)
+        after(q, (s, cnt[s]), rd, wr)
+
+    def dma(q, sem, rd, wr, out, in_):
+        before(q, rd, wr, "d" + sem)
+        cnt[sem] = cnt.get(sem, 0) + 16
+        eng[q].dma_start(out, in_).then_inc(T.sem[sem], 16)
+        after("d" + sem, (sem, None), rd, wr)
+
+    V, S, P = g.vector, g.scalar, g.tensor
+
+    def ts(rd, wr, out, in0, s1, op0, s2=None, op1=None):
+        if op1 is None:
+            run("v", V.tensor_scalar, rd, wr, out, in0, s1, None, op0)
+        else:
+            run("v", V.tensor_scalar, rd, wr, out, in0, s1, s2, op0, op1)
+
+    def tt(rd, wr, out, a, b, op):
+        run("v", V.tensor_tensor, rd, wr, out, a, b, op)
+
+    def vcopy(rd, wr, out, in_):
+        run("v", V.tensor_copy, rd, wr, out, in_)
+
+    def scopy(rd, wr, out, in_):
+        run("s", S.activation, rd, wr, out, in_, AF.Copy)
+
+    def mm(rd, wr, out, lhsT, rhs):
+        run("p", P.matmul, rd, wr, out, lhsT, rhs, True, True)
+
+    def bank(i):
+        return T["ps%d" % i]
+
+    dma("y", "ldd", [], ["din"], T.din[0:16, :], T.fd[:, :])
+    dma("s", "ldl1", [], ["lt1"], T.lt[:, 16:32], T.ld[:, :])
+    dma("y", "ldl1", [], ["lt1"], T.lt[:, 0:16], T.lc[:, :])
+    for k in range(8):
+        dma("s" if k % 2 else "y", "ldc", [], ["frc"], T.frc[16 * k:16 * k + 16, :], T.fc[:, :])
+    dma("y", "ldb", [], ["bin"], T.bin[0:16, :], T.fb[:, :])
+    dma("s", "ldl2", [], ["lt2"], T.lt[:, 32:48], T.lb[:, :])
+
+    def zeros(z, c0, c1):
+        run("g", g.iota, [], [z], T[z][:, c0:c1], [[0, c1 - c0]], 0, 0, allow_small_or_imprecise_dtypes=True)
+
+    run("g", g.iota, [], ["dj"], T.dj[:, :], [[1, 256]], 128, -1)
+    run("g", g.iota, [], ["pc"], T.pc[:, 0:1], [[1, 1]], 0, 1)
+    run("g", g.iota, [], ["gm"], T.gm[:, :], [[1, 8], [0, 16]], 0, 0)
+    run("g", g.iota, [], ["jt"], T.jt[:, :], [[16, 32]], 2048, 1)
+    zeros("P1", 0, 1024)
+    ts(["dj"], ["di"], T.di[:, :], T.dj[:, 0:128], 15, OP.bitwise_and)
+    ts(["di"], ["eb"], T.eb[:, :], T.di[:, :], 0.0, OP.is_equal)
+    ts(["di"], ["d16"], T.d16[:, 0:128], T.di[:, :], 0.0, OP.is_equal)
+    ts(["pc"], ["pi"], T.pi[:, 0:1], T.pc[:, 0:1], 15, OP.bitwise_and)
+    ts(["pc"], ["pg"], T.pg[:, 0:1], T.pc[:, 0:1], 4, OP.logical_shift_right)
+    vcopy(["pg"], ["pgf"], T.col[:, 2:3], T.pg[:, 0:1])
+    vcopy(["pc"], ["pf"], T.col[:, 3:4], T.pc[:, 0:1])
+    run("v", V.memset, [], ["xf"], T.xf[:, 32:33], -1.0)
+    run("v", V.memset, [], ["xf"], T.xf[:, 65:66], -1.0)
+    ts(["gm", "pf"], ["b8"], T.b8[:, :], T.gm[:, :], T.col[:, 3:4], OP.is_equal)
+    vcopy(["lt1"], ["lu1"], T.lu[:, 0:32], T.lt[:, 0:32])
+
+    def spread(src, skey, dst, dkey):
+        for k in range(4):
+            mm(["eb", skey], ["ps%d" % k], bank(k)[:, :], T.eb[0:16, :], src[0:16, 512 * k:512 * k + 512])
+            (scopy if k % 2 == 0 else vcopy)(["ps%d" % k], ["%s%d" % (dkey, k)], dst[:, 512 * k:512 * k + 512], bank(k)[:, :])
+        return ["%s%d" % (dkey, k) for k in range(4)]
+
+    def pick(keys, out, okey, src, c):
+        scopy(keys, [okey + "S"], out[:, 0:128], src[:, :].indirect(T.lu[:, c:c + 8]))
+        vcopy(keys, [okey + "V"], out[:, 128:256], src[:, :].indirect(T.lu[:, c + 8:c + 16]))
+        return [okey + "S", okey + "V"]
+
+    plans = {c: send_engines(c, cores, topo) for c in cores}
+
+    def transfer(src, dst, d, es, x):
+        rid, pid, _ = topo.addr(d)
+        mask = 0
+        for e in es:
+            mask |= 1 << e
+        return RemoteDMATransfer(dst_ids=[DstId(rid=rid, pnc=pid)], dma_engine_mask=mask, remote_sem=T.sem["arr" + x], src=src, dst=dst)
+
+    def exchange(x, src, keys):
+        snd, land = T["snd" + x], T["land" + x]
+        dma("y", "snd" + x, keys, ["snd" + x], snd[:, :], src[:, :])
+        dma("y", "self" + x, keys, ["land" + x], land[128 * me:128 * me + 128, :], src[16 * me:16 * me + 16, :])
+        before("g", ["snd" + x], [])
+        g.remote_dma_fused([transfer(snd[128 * cores.index(d):128 * cores.index(d) + 128, :], land[128 * me:128 * me + 128, :], d, es, x)
+                            for d, es in plans[core].items()], local_sem=T.sem["loc" + x])
+        cnt["loc" + x] = sum(len(es) for es in plans[core].values())
+        cnt["arr" + x] = sum(len(plans[c][core]) for c in cores if c != core)
+        after("remote", ("arr" + x, None), [], ["land" + x])
+
+    kd = spread(T.din, "din", T.frd, "frd")
+    exchange("d", T.gd, pick(kd + ["lu1"], T.gd, "gd", T.frd, 16))
+    exchange("c", T.gk, pick(["frc", "lu1"], T.gk, "gk", T.frc, 0))
+    dma("y", "ldl3", [], ["lt3"], T.lt[:, 48:64], T.la[:, :])
+    dma("y", "ldv", [], ["vin"], T.vin[0:8, :], T.v[:, :])
+    for k, x in enumerate((T.xa, T.xb, T.xc, T.xd)):
+        dma("y", "ldx", [], ["xt"], T.xt[:, 32 * k:32 * k + 32], x[:, :])
+    dma("y", "ldo", [], ["obt"], T.obt[:, :], T.ob[:, :])
+    ts(["pi"], ["nz"], T.col[:, 0:1], T.pi[:, 0:1], 0.0, OP.not_equal)
+    ts(["pi"], ["zf"], T.col[:, 1:2], T.pi[:, 0:1], 0.0, OP.is_equal)
+    ts(["pg"], ["g16"], T.col[:, 4:5], T.pg[:, 0:1], 16.0, OP.mult)
+    ts(["pg"], ["rc"], T.col[:, 5:6], T.pg[:, 0:1], -256.0, OP.mult, 2048.0, OP.add)
+    kbi = spread(T.bin, "bin", T.frb, "frb")
+    vcopy(["lt2"], ["lu2"], T.lu[:, 32:48], T.lt[:, 32:48])
+    exchange("b", T.gb, pick(kbi + ["lu2"], T.gb, "gb", T.frb, 32))
+    mm(["b8", "vin"], ["ps6"], bank(6)[:, :], T.b8[0:8, :], T.vin[0:8, :])
+    zeros("P1", 1024, 2048)
+    zeros("Z1", 0, 2048)
+
+    ts(["dj"], ["dk"], T.dk[:, :], T.dj[:, :], 127, OP.bitwise_and)
+    ts(["dk"], ["i2b"], T.i2b[:, :], T.dk[:, :], 0.0, OP.is_equal)
+    ts(["gm", "pgf"], ["gf"], T.gf[:, :], T.gm[:, :], T.col[:, 2:3], OP.is_equal)
+    ts(["jt", "g16"], ["jf"], T.jf[:, :], T.jt[:, :], T.col[:, 4:5], OP.subtract)
+    ts(["dj", "nz"], ["sh1"], T.sh1[:, :], T.dj[:, 0:128], 127.0, OP.is_equal, T.col[:, 0:1], OP.mult)
+    ts(["dj", "zf"], ["sh2"], T.sh2[:, :], T.dj[:, 0:128], 143.0, OP.is_equal, T.col[:, 1:2], OP.mult)
+    run("v", V.memset, [], ["e2"], T.e2[:, :], 0.0)
+    vcopy(["d16", "e2"], ["e2a"], T.e2[:, 0:32:2], T.d16[:, 0:16])
+    vcopy(["d16", "e2"], ["e2b"], T.e2[:, 33:64:2], T.d16[:, 0:16])
+    ts(["xt", "rc"], ["xr"], T.xr[:, 32:128], T.xt[:, 32:128], T.col[:, 5:6], OP.add)
+    ts(["xr"], ["xo"], T.xo[:, 32:128], T.xr[:, 32:128], 2047, OP.bitwise_and)
+    vcopy(["xo"], ["xu"], T.xu[:, 32:128], T.xo[:, 32:128])
+    vcopy(["xt"], ["xf"], T.xf[:, 0:32], T.xt[:, 0:32])
+    vcopy(["xt"], ["xf"], T.xf[:, 33:65], T.xt[:, 32:64])
+    vcopy(["lt3"], ["lu3"], T.lu[:, 48:64], T.lt[:, 48:64])
+    scopy(["ps6"], ["vr"], T.vr[:, :], bank(6)[:, :])
+    for i in range(16):
+        if i % 2:
+            run("s", S.activation, ["xf", "d16"], ["y1s"], T.y1[:, i::16], T.xf[:, :], AF.Copy, scale=T.d16[:, i:i + 1])
+        else:
+            ts(["xf", "d16"], ["y1v"], T.y1[:, i::16], T.xf[:, :], T.d16[:, i:i + 1], OP.mult)
+    mm(["gf", "y1s", "y1v"], ["ps5"], bank(5)[:, :], T.gf[:, :], T.y1[:, 0:512])
+    scopy(["ps5"], ["fla"], T.fla[:, :], bank(5)[:, :])
+
+    def scatter_places(xkey, x, b, outkey, out):
+        k = "ps%d" % b
+        before("p", [xkey, "sh1", "sh2"], [k])
+        run("p", P.matmul, [xkey, "sh1"], [k], bank(b)[:, 0:32], T.sh1[:, :], x[:, 0:32], True, False)
+        run("p", P.matmul, [xkey, "sh2"], [k], bank(b)[:, 0:32], T.sh2[:, :], x[:, 1:33], False, True)
+        tt([xkey, k], [outkey + "e"], T.sa1[:, :], x[:, 0:32], bank(b)[:, 0:32], OP.not_equal)
+        tt([xkey, "jf"], [outkey + "d"], T.sa2[:, :], x[:, 0:32], T.jf[:, :], OP.subtract)
+        tt([outkey + "e", outkey + "d"], [outkey + "f"], T.sa2[:, :], T.sa2[:, :], T.sa1[:, :], OP.mult)
+        tt([outkey + "f", "jf"], [outkey + "h"], T.sa1[:, :], T.sa2[:, :], T.jf[:, :], OP.add)
+        vcopy([outkey + "h"], [outkey], out[:, :], T.sa1[:, :])
+
+    scatter_places("xf", T.xf, 7, "sau", T.sau)
+    run("v", V.memset, [], ["ma"], T.ma[:, 0:1], 0.0)
+    tt(["fla", "ps5"], ["ma"], T.ma[:, 1:512], T.fla[:, 1:512], bank(5)[:, 0:511], OP.is_equal)
+
+    def table(x, t, ident, ikey, groups, queues):
+        land, key, w = T["land" + x], "land" + x, 256
+        dma("y", "cmp" + x, [key], [x + "0"], t[:, 0:w], land[:, :])
+        byp = [d for _, ds, _ in groups for d in ds]
+        for d in range(1, 8):
+            if d not in byp:
+                q = queues[d % len(queues)]
+                dma(q, "rot" + x, [key], ["%s%d" % (x, d)], t[0:128 - 16 * d, d * w:(d + 1) * w], land[128 * d:1024, :])
+                dma(q, "rot" + x, [key], ["%s%d" % (x, d)], t[128 - 16 * d:128, d * w:(d + 1) * w], land[0:128 * d, :])
+        for b, ds, q in groups:
+            n = len(ds)
+            for i, d in enumerate(ds):
+                mm([ikey, x + "0"], ["ps%d" % b], bank(b)[:, i * w:(i + 1) * w], ident[:, 16 * d:16 * d + 128], t[:, 0:w])
+            (vcopy if q == "v" else scopy)(["ps%d" % b], ["%s%d" % (x, d) for d in ds], t[:, ds[0] * w:(ds[0] + n) * w], bank(b)[:, 0:n * w])
+        return ["%s%d" % (x, d) for d in range(8)]
+
+    kd = table("d", T.td, T.i2b, "i2b", ((0, (1, 2), "s"), (1, (3, 4), "v"), (2, (5,), "s"), (4, (6,), "v")), "y")
+    tt(kd + ["xu", "vr"], ["w1"], T.w1[:, :], T.td[:, :].indirect(T.xu[:, 96:128]), T.vr[:, :], OP.mult)
+    kc = table("c", T.tc, T.i2b, "i2b", ((3, (1, 2), "s"), (7, (3, 4), "s"), (6, (5,), "v")), "y")
+    tt(kc + ["xu", "w1"], ["w2"], T.w2[:, :], T.tc[:, :].indirect(T.xu[:, 64:96]), T.w1[:, :], OP.mult)
+    kb = table("b", T.tb, T.i2b, "i2b", ((0, (1, 2), "s"), (1, (3, 4), "s")), "y")
+    for k in range(8):
+        dma("y", "lda", [], ["fra"], T.fra[16 * k:16 * k + 16, :], T.fa[:, :])
+    tt(kb + ["xu", "w2"], ["pr1"], T.pr1[:, :], T.tb[:, :].indirect(T.xu[:, 32:64]), T.w2[:, :], OP.mult)
+    mm(["gf", "y1s", "y1v"], ["ps4"], bank(4)[:, :], T.gf[:, :], T.y1[:, 528:1040])
+    scopy(["ps4"], ["flb"], T.flb[:, :], bank(4)[:, :])
+    for k in range(1, 4):
+        scopy(["d16"], ["d16t"], T.d16[:, 128 * k:128 * k + 128], T.d16[:, 0:128])
+    vcopy(["obt"], ["obu"], T.obu[:, :], T.obt[:, :])
+
+    def segsum(mkey, m, pkey, p, skey, s, ukey, u, zkey, z):
+        run("v", V.tensor_tensor_scan, [mkey, pkey], [skey], s[:, :], m[:, :], p[:, :], 0.0, OP.mult, OP.add)
+        vcopy([skey, ukey, zkey], [zkey + "s"], z[:, :].indirect(u[:, :]), s[:, :])
+
+    calls = {c: sum_calls(c, cores, topo) for c in cores}
+
+    def sums_out(x, keys, z, r, lp):
+        def add(q, b, c):
+            for h in range(2):
+                run("p", P.matmul, keys + ["d16", "e2a", "e2b"], ["ps%d" % b], bank(b)[:, c:c + 32],
+                    z[:, 256 * q + 128 * h:256 * q + 128 * h + 128], T.e2[:, 32 * h:32 * h + 32], h == 0, h == 1)
+        pos = 0
+        for k, call in enumerate(calls[core]):
+            n = 32 * len(call)
+            for j, (d, _) in enumerate(call):
+                add(cores.index(d), k, 32 * j)
+            (vcopy if k % 2 else scopy)(["ps%d" % k], ["%sr%d" % (x, k)], r[:, pos:pos + n], bank(k)[:, 0:n])
+            before("g", ["%sr%d" % (x, k)], [])
+            g.remote_dma_fused([transfer(r[:, pos + 32 * j:pos + 32 * j + 32], lp[:, 32 * me:32 * me + 32], d, es, x)
+                                for j, (d, es) in enumerate(call)], local_sem=T.sem["loc" + x])
+            pos += n
+        add(me, 4, 0)
+        vcopy(["ps4"], [x + "me"], lp[:, 32 * me:32 * me + 32], bank(4)[:, 0:32])
+        cnt["loc" + x] = sum(len(es) for call in calls[core] for _, es in call)
+        cnt["arr" + x] = sum(len(es) for c in cores if c != core for call in calls[c] for d, es in call if d == core)
+        after("remote", ("arr" + x, None), [], ["land" + x])
+
+    def sums_in(x, lp, lq, c, zkey, z):
+        for h in range(2):
+            mm(["land" + x, x + "me", "i2f"], ["ps%d" % (5 + h)], bank(5 + h)[:, 0:128], lp[:, h::2], T.i2f[:, 0:128])
+            scopy(["ps%d" % (5 + h)], ["%st%d" % (x, h)], lq[:, 128 * h:128 * h + 128], bank(5 + h)[:, 0:128])
+        for h in range(2):
+            vcopy(["%st%d" % (x, h), "lu2", "lu3", zkey] + [zkey + "s0"] * h, ["%ss%d" % (zkey, h)],
+                  z[:, :].indirect(T.lu[:, c + 8 * h:c + 8 * h + 8]), lq[:, 128 * h:128 * h + 128])
+        return [zkey, zkey + "s0", zkey + "s1"]
+
+    segsum("ma", T.ma, "pr1", T.pr1, "sg1", T.sg1, "sau", T.sau, "P1", T.P1)
+    sums_out("p1", ["P1", "P1s"], T.P1, T.r1, T.lp1)
+    ts(["dk"], ["i2f"], T.i2f[:, :], T.dk[:, :], 0.0, OP.is_equal)
+    zeros("P2", 0, 2048)
+
+    scopy(["flb", "obu"], ["fbp"], T.fbp[:, :], T.flb[:, :].indirect(T.obu[:, :]))
+    scopy(["w2", "obu"], ["wp"], T.wp[:, :], T.w2[:, :].indirect(T.obu[:, :]))
+    tt(["flb", "obu", "d16", "d16t"], ["ba"], T.ba[:, 0:512], T.flb[:, :].indirect(T.obu[:, :]), T.d16[:, :], OP.mult)
+    tt(["fla", "obu", "d16", "d16t"], ["ba"], T.ba[:, 512:1024], T.fla[:, :].indirect(T.obu[:, :]), T.d16[:, :], OP.mult)
+    tt(["ba"], ["t1"], T.t1[:, :], T.ba[:, 0::2], T.ba[:, 1::2], OP.add)
+
+    kz = sums_in("p1", T.lp1, T.lq1, 48, "Z1", T.Z1)
+    for k, (c0, c1) in enumerate(((0, 512), (512, 1024), (1024, 1536), (1536, 1792), (1792, 2048))):
+        c = slice(c0, c1)
+        mm(["d16"] + kz, ["ps%d" % k], bank(k)[:, 0:c1 - c0], T.d16[:, 0:128], T.Z1[:, c])
+        tt(["ps%d" % k, "fra"], ["yar"], T.yar[:, c], bank(k)[:, 0:c1 - c0], T.fra[:, c], OP.mult)
+    scopy(["yar", "lu3"], ["gaS"], T.ga[:, 128:256], T.yar[:, :].indirect(T.lu[:, 56:64]))
+    vcopy(["yar", "lu3"], ["gaV"], T.ga[:, 0:128], T.yar[:, :].indirect(T.lu[:, 48:56]))
+    exchange("a", T.ga, ["gaS", "gaV"])
+    zeros("Z2", 0, 2048)
+    dma("y", "oya", ["yar"], [], T.ya[:, :], T.yar[0:16, :])
+
+    tt(["t1"], ["t2"], T.t2[:, :], T.t1[:, 0::2], T.t1[:, 1::2], OP.add)
+    tt(["t2"], ["t3"], T.t3[:, :], T.t2[:, 0::2], T.t2[:, 1::2], OP.add)
+    tt(["t3"], ["t4"], T.t4[:, :], T.t3[:, 0::2], T.t3[:, 1::2], OP.add)
+    run("v", V.memset, [], ["xg"], T.xg[:, 32:33], -1.0)
+    vcopy(["t4"], ["xg"], T.xg[:, 0:32], T.t4[:, 0:32])
+    ts(["t4", "rc"], ["ai"], T.ai[:, :], T.t4[:, 32:64], T.col[:, 5:6], OP.add)
+    ts(["ai"], ["aj"], T.aj[:, :], T.ai[:, :], 2047, OP.bitwise_and)
+    vcopy(["aj"], ["au"], T.au[:, :], T.aj[:, :])
+    scatter_places("xg", T.xg, 7, "sbu", T.sbu)
+    run("v", V.memset, [], ["mb"], T.mb[:, 0:1], 0.0)
+    tt(["fbp"], ["mb"], T.mb[:, 1:512], T.fbp[:, 1:512], T.fbp[:, 0:511], OP.is_equal)
+
+    ka = table("a", T.ta, T.i2f, "i2f", ((0, (1,), "s"), (1, (2,), "v"), (2, (3,), "s")), "y")
+    tt(ka + ["au", "wp"], ["pr2"], T.pr2[:, :], T.ta[:, :].indirect(T.au[:, :]), T.wp[:, :], OP.mult)
+    segsum("mb", T.mb, "pr2", T.pr2, "sg2", T.sg2, "sbu", T.sbu, "P2", T.P2)
+    sums_out("p2", ["P2", "P2s"], T.P2, T.r2, T.lp2)
+
+    kz = sums_in("p2", T.lp2, T.lq2, 32, "Z2", T.Z2)
+    kr = []
+    for h in range(2):
+        for q in range(8):
+            c = 256 * q + 128 * h
+            mm(kz + ["d16"], ["ps%d" % h], bank(h)[:, 16 * q:16 * q + 16], T.Z2[:, c:c + 128], T.d16[:, 0:16])
+        (vcopy if h else scopy)(["ps%d" % h], ["u3%d" % h], T.u3[:, 128 * h:128 * h + 128], bank(h)[:, 0:128])
+    for h in range(2):
+        run("p", P.transpose, ["u3%d" % h, "i2f"], ["ps%d" % (2 + h)], bank(2 + h)[:, 0:128], T.u3[:, 128 * h:128 * h + 128], T.i2f[:, 0:128])
+        (vcopy if h else scopy)(["ps%d" % (2 + h)], ["r3%d" % h], T.r3[:, 128 * h:128 * h + 128], bank(2 + h)[:, 0:128])
+        kr.append("r3%d" % h)
+    for q in range(8):
+        dma("s" if q % 2 else "y", "oyb", kr, [], T.yb[:, 256 * q:256 * q + 256], T.r3[16 * q:16 * q + 16, :])
+
+    need("g", [(s, cnt[s]) for s in cnt])

@@ -2,45 +2,43 @@ from concourse.bass import DstId, RemoteDMATransfer
 from concourse.mybir import AluOpType as OP, ActivationFunctionType as AF
 
 F, B, I, U = "float32", "bfloat16", "int32", "uint16"
+
+
+def sb(n, d=F):
+    return ("sbuf", [128, n], d)
+
+
 SCRATCH = {
-    "din": ("sbuf", [128, 2048], B), "bin": ("sbuf", [128, 2048], B), "frc": ("sbuf", [128, 2048], B),
-    "frd": ("sbuf", [128, 2048], B), "frb": ("sbuf", [128, 2048], B), "fra": ("sbuf", [128, 2048], B),
-    "lt": ("sbuf", [128, 64], I), "lu": ("sbuf", [128, 64], U),
-    "xt": ("sbuf", [128, 128], I), "xr": ("sbuf", [128, 128], I), "xo": ("sbuf", [128, 128], I), "xu": ("sbuf", [128, 128], U),
-    "obt": ("sbuf", [128, 32], I), "obu": ("sbuf", [128, 32], U),
-    "vin": ("sbuf", [128, 512], F), "vr": ("sbuf", [128, 512], F),
-    "pc": ("sbuf", [128, 8], I), "dj": ("sbuf", [128, 256], I), "gm": ("sbuf", [128, 128], I), "jt": ("sbuf", [128, 32], I),
-    "pi": ("sbuf", [128, 8], I), "pg": ("sbuf", [128, 8], I), "col": ("sbuf", [128, 8], F),
-    "di": ("sbuf", [128, 128], I), "dk": ("sbuf", [128, 256], I), "d16": ("sbuf", [128, 512], F), "e2": ("sbuf", [128, 64], F),
-    "eb": ("sbuf", [128, 128], B), "i2f": ("sbuf", [128, 256], F), "i2b": ("sbuf", [128, 256], B),
-    "sh1": ("sbuf", [128, 128], F), "sh2": ("sbuf", [128, 128], F), "b8": ("sbuf", [128, 128], F),
-    "gf": ("sbuf", [128, 128], F), "jf": ("sbuf", [128, 32], F),
-    "xf": ("sbuf", [128, 66], F), "y1": ("sbuf", [128, 1056], F), "fla": ("sbuf", [128, 512], F),
-    "flb": ("sbuf", [128, 512], F), "fbp": ("sbuf", [128, 512], F),
-    "ma": ("sbuf", [128, 512], F), "mb": ("sbuf", [128, 512], F),
-    "sa1": ("sbuf", [128, 32], F), "sa2": ("sbuf", [128, 32], F), "sau": ("sbuf", [128, 32], U), "sbu": ("sbuf", [128, 32], U),
-    "ba": ("sbuf", [128, 1024], F), "t1": ("sbuf", [128, 512], F), "t2": ("sbuf", [128, 256], F),
-    "t3": ("sbuf", [128, 128], F), "t4": ("sbuf", [128, 64], F), "xg": ("sbuf", [128, 40], F),
-    "ai": ("sbuf", [128, 32], I), "aj": ("sbuf", [128, 32], I), "au": ("sbuf", [128, 32], U),
-    "gd": ("sbuf", [128, 256], B), "gk": ("sbuf", [128, 256], B), "gb": ("sbuf", [128, 256], B),
+    "win": sb(2048, B), "lt": sb(64, I), "lu": sb(64, U), "g0": sb(1024, B), "fra": sb(2048, B), "fas": sb(256),
+    "xt": sb(160, I), "xr": sb(96, I), "xo": sb(96, I), "xu": sb(96, U),
+    "obt": sb(32, I), "obu": sb(32, U), "vin": sb(512), "vr": sb(512),
+    "pc": sb(8, I), "dj": sb(128, I), "jt": sb(32, I), "pi": sb(8, I), "pg": sb(8, I), "col": sb(16),
+    "di": sb(128, I), "d16": sb(128), "one": sb(256), "i2f": sb(128), "i2b": sb(256, B),
+    "sh0": sb(128), "gf0": sb(128), "sh1": sb(128), "sh2": sb(128), "b8": sb(128), "gf": sb(128), "jf": sb(32), "pos": sb(512),
+    "ki": sb(16, I), "kt": sb(32, I), "ru": sb(16, U), "pu": sb(8, U), "tu": sb(32, U), "mw": sb(8), "fl1": sb(128), "fl2": sb(128),
+    "xf": sb(104), "xq": sb(64, I), "xs": sb(64), "xc1": sb(64), "lsu": sb(32, U), "lnu": sb(16, U),
+    "eq1": sb(32), "eq2": sb(32), "equ1": sb(32, U), "equ2": sb(32, U), "dm": sb(32), "of": sb(32), "su1": sb(32, U), "su2": sb(32, U),
+    "ma": sb(520), "mb": sb(520), "W1": sb(2688), "W2": sb(2688), "W3": sb(2048),
+    "ef1": sb(128), "ef2": sb(128), "ef3": sb(128), "eu1": sb(128, U), "eu2": sb(128, U), "eu3": sb(128, U),
+    "ly": sb(128), "lru": sb(128, U),
+    "oq": sb(32, I), "os1": sb(32), "oc": sb(32), "otu": sb(32, U), "wx": sb(512), "q1": sb(512), "q2": sb(512),
+    "xal": sb(32), "xbl": sb(40), "au": sb(32, U), "bi": sb(32, I), "bq": sb(32, I), "bs": sb(32), "bc": sb(32),
     "sndd": ("dram", [1024, 32], B), "landd": ("dram", [1024, 32], B),
     "sndc": ("dram", [1024, 32], B), "landc": ("dram", [1024, 32], B),
     "sndb": ("dram", [1024, 32], B), "landb": ("dram", [1024, 32], B),
-    "snda": ("dram", [1024, 32], F), "landa": ("dram", [1024, 32], F),
-    "td": ("sbuf", [128, 2048], B), "tc": ("sbuf", [128, 2048], B), "tb": ("sbuf", [128, 2048], B), "ta": ("sbuf", [128, 2048], F),
-    "w1": ("sbuf", [128, 512], F), "w2": ("sbuf", [128, 512], F), "wp": ("sbuf", [128, 512], F),
-    "pr1": ("sbuf", [128, 512], F), "pr2": ("sbuf", [128, 512], F), "sg1": ("sbuf", [128, 512], F), "sg2": ("sbuf", [128, 512], F),
-    "P1": ("sbuf", [128, 2560], F), "P2": ("sbuf", [128, 2560], F), "Z1": ("sbuf", [128, 2048], F), "Z2": ("sbuf", [128, 2048], F),
-    "r1": ("sbuf", [128, 256], F), "r2": ("sbuf", [128, 256], F), "u3": ("sbuf", [128, 256], F), "r3": ("sbuf", [128, 256], F),
-    "lp1": ("sbuf", [128, 256], F), "lq1": ("sbuf", [128, 256], F), "lp2": ("sbuf", [128, 256], F), "lq2": ("sbuf", [128, 256], F),
-    "yar": ("sbuf", [128, 2048], F), "ga": ("sbuf", [128, 256], F),
+    "td": sb(2048, B), "tc": sb(2048, B), "tb": sb(2048, B), "ta": sb(2048),
+    "w1": sb(512), "w2": sb(512), "wp": sb(512), "pr1": sb(512), "pr2": sb(512), "sg1": sb(520), "sg2": sb(520),
+    "G1": sb(2048), "G2": sb(2048), "Z1": sb(2048), "rp": sb(2048),
+    "r1": sb(256), "r2": sb(256), "ra": sb(256), "ua": sb(256), "ub": sb(256), "ya3": sb(256), "yb3": sb(256),
+    "lp1": sb(256), "lq1": sb(256), "lp2": sb(256), "lq2": sb(264), "lpa": sb(256),
     "ps0": ("psum", [128, 512], F), "ps1": ("psum", [128, 512], F), "ps2": ("psum", [128, 512], F), "ps3": ("psum", [128, 512], F),
     "ps4": ("psum", [128, 512], F), "ps5": ("psum", [128, 512], F), "ps6": ("psum", [128, 512], F), "ps7": ("psum", [128, 512], F),
 }
-EXCH = ["d", "c", "b", "a"]
-SEMAPHORES = (["c_g", "c_v", "c_s", "c_p", "ldd", "ldl1", "ldl2", "ldl3", "ldc", "ldb", "lda", "ldx", "ldo", "ldv", "oya", "oyb"]
+EXCH = ["d", "c", "b"]
+SEMAPHORES = (["c_g", "c_v", "c_s", "c_p", "ldw", "ldl", "ldx", "ldn", "ldo", "ldv", "ldy", "ldz", "fas", "fil1", "fil2", "fil3",
+               "ef1", "ef2", "ef3", "wx", "xal", "xbl", "oya", "oyb"]
               + [k + x for x in EXCH for k in ("snd", "self", "arr", "loc", "cmp", "rot")]
-              + [k + x for x in ("p1", "p2") for k in ("arr", "loc")])
+              + [k + x for x in ("p1", "p2") for k in ("arr", "loc")] + ["loca", "arra0", "arra1", "arra2", "arra3"])
 
 
 def ways(src, cores, topo):
@@ -62,14 +60,14 @@ def send_engines(src, cores, topo):
     return p
 
 
-def sum_calls(src, cores, topo):
+def sum_calls(src, cores, topo, last):
     far, near, on = ways(src, cores, topo)
-    off = far + near
+    off = far + sorted(near, key=lambda d: not topo.mates(topo.chip(src), topo.chip(d)))
     e = topo.engines(src, off[0])
     n = len(e) // 2
     calls = [[(off[2 * k], e[0:n]), (off[2 * k + 1], e[n:2 * n])] for k in range(len(off) // 2)]
     for d in on:
-        calls[-1].append((d, [x for x in topo.engines(src, d) if x not in e][0:n]))
+        calls[-1 if last else 0].append((d, [x for x in topo.engines(src, d) if x not in e][0:n]))
     return calls
 
 
@@ -97,6 +95,8 @@ def rank_program(g, core, T, topo):
         toks = []
         for k in rd:
             toks += [t for _, t in WR.get(k, [])]
+            if k[:2] == "ps":
+                toks += [t for o, t in RD.get(k, []) if o != own]
         for k in wr:
             toks += [t for o, t in WR.get(k, []) + RD.get(k, []) if o != own]
         need(q, toks)
@@ -137,246 +137,342 @@ def rank_program(g, core, T, topo):
     def scopy(rd, wr, out, in_):
         run("s", S.activation, rd, wr, out, in_, AF.Copy)
 
-    def mm(rd, wr, out, lhsT, rhs):
-        run("p", P.matmul, rd, wr, out, lhsT, rhs, True, True)
+    def copy(q, rd, wr, out, in_):
+        (vcopy if q == "v" else scopy)(rd, wr, out, in_)
+
+    def fill(key, ap, c):
+        run("v", V.memset, [], [key], ap, c)
+
+    def mm(rd, wr, out, lhsT, rhs, start=True, stop=True):
+        run("p", P.matmul, rd, wr, out, lhsT, rhs, start, stop)
 
     def bank(i):
         return T["ps%d" % i]
 
-    dma("y", "ldd", [], ["din"], T.din[0:16, :], T.fd[:, :])
-    dma("s", "ldl1", [], ["lt1"], T.lt[:, 16:32], T.ld[:, :])
-    dma("y", "ldl1", [], ["lt1"], T.lt[:, 0:16], T.lc[:, :])
-    for k in range(8):
-        dma("s" if k % 2 else "y", "ldc", [], ["frc"], T.frc[16 * k:16 * k + 16, :], T.fc[:, :])
-    dma("y", "ldb", [], ["bin"], T.bin[0:16, :], T.fb[:, :])
-    dma("s", "ldl2", [], ["lt2"], T.lt[:, 32:48], T.lb[:, :])
+    def iota(key, out, pattern, base, cm):
+        if out.dtype == T.pos.dtype:
+            run("g", g.iota, [], [key], out[:, :], pattern, base, cm, allow_small_or_imprecise_dtypes=True)
+        else:
+            run("g", g.iota, [], [key], out[:, :], pattern, base, cm)
 
-    def zeros(z, c0, c1):
-        run("g", g.iota, [], [z], T[z][:, c0:c1], [[0, c1 - c0]], 0, 0, allow_small_or_imprecise_dtypes=True)
+    for f, x in enumerate((T.fd, T.fc, T.fb)):
+        for e in range(2):
+            dma("ys"[e], "ldw", [], ["win"], T.win[32 * f + 16 * e:32 * f + 16 * e + 16, :], x[:, :])
+    for f, l in enumerate((T.ld, T.lc, T.lb)):
+        for u in range(4):
+            dma("ys"[u % 2], "ldl", [], ["lt"], T.lt[32 * f:32 * f + 32, 16 * u:16 * u + 16], l[32 * u:32 * u + 32, :])
+    dma("y", "ldx", [], ["xta"], T.xt[:, 0:32], T.xa[:, :])
+    dma("s", "ldy", [], ["xtb"], T.xt[:, 64:96], T.xb[:, :])
+    fill("win0", T.win[96:128, :], 0.0)
+    fill("lt0", T.lt[96:128, :], 0)
 
-    run("g", g.iota, [], ["dj"], T.dj[:, :], [[1, 256]], 128, -1)
-    run("g", g.iota, [], ["pc"], T.pc[:, 0:1], [[1, 1]], 0, 1)
-    run("g", g.iota, [], ["gm"], T.gm[:, :], [[1, 8], [0, 16]], 0, 0)
-    run("g", g.iota, [], ["jt"], T.jt[:, :], [[16, 32]], 2048, 1)
-    zeros("P1", 0, 1024)
-    ts(["dj"], ["di"], T.di[:, :], T.dj[:, 0:128], 15, OP.bitwise_and)
-    ts(["di"], ["eb"], T.eb[:, :], T.di[:, :], 0.0, OP.is_equal)
-    ts(["di"], ["d16"], T.d16[:, 0:128], T.di[:, :], 0.0, OP.is_equal)
+    def select(key, out, src, skey, pattern, op, base, cm):
+        run("g", g.affine_select, [skey], [key], out, src, pattern, op, 0.0, base, cm)
+
+    fill("one", T.one[:, :], 1.0)
+    iota("pos", T.pos, [[1, 512]], 0, 0)
+    iota("pc", T.pc, [[0, 8]], 0, 1)
+    iota("jt", T.jt, [[16, 32]], 2048, 1)
+    select("sh0", T.sh0[:, :], T.one[:, 0:128], "one", [[-1, 128]], OP.is_equal, -1, 1)
+    select("sh2", T.sh2[:, :], T.one[:, 0:128], "one", [[-16, 8], [256, 16]], OP.is_equal, -256 * 15, 1)
+    select("sh1", T.sh1[:, :], T.sh0[:, :], "sh0", [[0, 8], [1, 16]], OP.not_equal, -15, 0)
+    select("b8", T.b8[:, :], T.one[:, 0:128], "one", [[-1, 8], [0, 16]], OP.is_equal, 0, 1)
+    iota("kt", T.kt, [[1, 16], [256, 2]], 0, 0)
+    fill("fl1", T.fl1[:, :], 512.0)
+    fill("xf", T.xf[:, 32:33], -1.0)
+    fill("mw", T.mw[:, 0:1], 0.0)
+    fill("mw", T.mw[:, 1:8], 1.0)
     ts(["pc"], ["pi"], T.pi[:, 0:1], T.pc[:, 0:1], 15, OP.bitwise_and)
     ts(["pc"], ["pg"], T.pg[:, 0:1], T.pc[:, 0:1], 4, OP.logical_shift_right)
-    vcopy(["pg"], ["pgf"], T.col[:, 2:3], T.pg[:, 0:1])
-    vcopy(["pc"], ["pf"], T.col[:, 3:4], T.pc[:, 0:1])
-    run("v", V.memset, [], ["xf"], T.xf[:, 32:33], -1.0)
-    run("v", V.memset, [], ["xf"], T.xf[:, 65:66], -1.0)
-    ts(["gm", "pf"], ["b8"], T.b8[:, :], T.gm[:, :], T.col[:, 3:4], OP.is_equal)
-    vcopy(["lt1"], ["lu1"], T.lu[:, 0:32], T.lt[:, 0:32])
+    ts(["jt"], ["jf"], T.jf[:, :], T.jt[:, :], 1.0 / 128, OP.mult)
+    ts(["pg"], ["rc"], T.col[:, 5:6], T.pg[:, 0:1], -256.0, OP.mult, 2048.0, OP.add)
+    ts(["pi"], ["p16"], T.col[:, 7:8], T.pi[:, 0:1], 16.0, OP.mult)
+    vcopy(["pi"], ["pif"], T.col[:, 6:7], T.pi[:, 0:1])
+    fill("wx", T.wx[:, :], 0.0)
+    vcopy(["lt", "lt0"], ["lu"], T.lu[:, :], T.lt[:, :])
 
-    def spread(src, skey, dst, dkey):
-        for k in range(4):
-            mm(["eb", skey], ["ps%d" % k], bank(k)[:, :], T.eb[0:16, :], src[0:16, 512 * k:512 * k + 512])
-            (scopy if k % 2 == 0 else vcopy)(["ps%d" % k], ["%s%d" % (dkey, k)], dst[:, 512 * k:512 * k + 512], bank(k)[:, :])
-        return ["%s%d" % (dkey, k) for k in range(4)]
+    def blank(k, q):
+        dma(q, "fil%d" % k, ["fl1", "fl2"], ["W%d" % k], T["W%d" % k][0::16, 0:2048], (T.fl2 if k == 3 else T.fl1)[:, :])
 
-    def pick(keys, out, okey, src, c):
-        scopy(keys, [okey + "S"], out[:, 0:128], src[:, :].indirect(T.lu[:, c:c + 8]))
-        vcopy(keys, [okey + "V"], out[:, 128:256], src[:, :].indirect(T.lu[:, c + 8:c + 16]))
-        return [okey + "S", okey + "V"]
+    blank(1, "y")
+    dma("y", "ldo", [], ["obt"], T.obt[:, :], T.ob[:, :])
+    dma("y", "ldv", [], ["vin"], T.vin[0:8, :], T.v[:, :])
+
+    for u in range(4):
+        copy("vs"[u % 2], ["win", "win0", "lu"], ["g0%d" % u], T.g0[:, 256 * u:256 * u + 256], T.win[:, :].indirect(T.lu[:, 16 * u:16 * u + 16]))
 
     plans = {c: send_engines(c, cores, topo) for c in cores}
 
-    def transfer(src, dst, d, es, x):
+    def transfer(src, dst, d, es, sem):
         rid, pid, _ = topo.addr(d)
         mask = 0
         for e in es:
             mask |= 1 << e
-        return RemoteDMATransfer(dst_ids=[DstId(rid=rid, pnc=pid)], dma_engine_mask=mask, remote_sem=T.sem["arr" + x], src=src, dst=dst)
+        return RemoteDMATransfer(dst_ids=[DstId(rid=rid, pnc=pid)], dma_engine_mask=mask, remote_sem=T.sem[sem], src=src, dst=dst)
 
-    def exchange(x, src, keys):
+    def stage(x, f, q):
         snd, land = T["snd" + x], T["land" + x]
-        dma("y", "snd" + x, keys, ["snd" + x], snd[:, :], src[:, :])
-        dma("y", "self" + x, keys, ["land" + x], land[128 * me:128 * me + 128, :], src[16 * me:16 * me + 16, :])
+        for u in range(4):
+            dma(q, "snd" + x, ["g0%d" % u], ["snd" + x], snd[256 * u:256 * u + 256, :], T.g0[32 * f:32 * f + 32, 256 * u:256 * u + 256])
+        p, u = 32 * f + 16 * (me % 2), me // 2
+        dma(q, "self" + x, ["g0%d" % u], ["land" + x], land[128 * me:128 * me + 128, :], T.g0[p:p + 16, 256 * u:256 * u + 256])
+
+    def exchange(x):
+        snd, land = T["snd" + x], T["land" + x]
         before("g", ["snd" + x], [])
-        g.remote_dma_fused([transfer(snd[128 * cores.index(d):128 * cores.index(d) + 128, :], land[128 * me:128 * me + 128, :], d, es, x)
+        g.remote_dma_fused([transfer(snd[128 * cores.index(d):128 * cores.index(d) + 128, :], land[128 * me:128 * me + 128, :], d, es, "arr" + x)
                             for d, es in plans[core].items()], local_sem=T.sem["loc" + x])
         cnt["loc" + x] = sum(len(es) for es in plans[core].values())
         cnt["arr" + x] = sum(len(plans[c][core]) for c in cores if c != core)
         after("remote", ("arr" + x, None), [], ["land" + x])
 
-    kd = spread(T.din, "din", T.frd, "frd")
-    exchange("d", T.gd, pick(kd + ["lu1"], T.gd, "gd", T.frd, 16))
-    exchange("c", T.gk, pick(["frc", "lu1"], T.gk, "gk", T.frc, 0))
-    dma("y", "ldl3", [], ["lt3"], T.lt[:, 48:64], T.la[:, :])
-    dma("y", "ldv", [], ["vin"], T.vin[0:8, :], T.v[:, :])
-    for k, x in enumerate((T.xa, T.xb, T.xc, T.xd)):
-        dma("y", "ldx", [], ["xt"], T.xt[:, 32 * k:32 * k + 32], x[:, :])
-    dma("y", "ldo", [], ["obt"], T.obt[:, :], T.ob[:, :])
-    ts(["pi"], ["nz"], T.col[:, 0:1], T.pi[:, 0:1], 0.0, OP.not_equal)
-    ts(["pi"], ["zf"], T.col[:, 1:2], T.pi[:, 0:1], 0.0, OP.is_equal)
-    ts(["pg"], ["g16"], T.col[:, 4:5], T.pg[:, 0:1], 16.0, OP.mult)
-    ts(["pg"], ["rc"], T.col[:, 5:6], T.pg[:, 0:1], -256.0, OP.mult, 2048.0, OP.add)
-    kbi = spread(T.bin, "bin", T.frb, "frb")
-    vcopy(["lt2"], ["lu2"], T.lu[:, 32:48], T.lt[:, 32:48])
-    exchange("b", T.gb, pick(kbi + ["lu2"], T.gb, "gb", T.frb, 32))
-    mm(["b8", "vin"], ["ps6"], bank(6)[:, :], T.b8[0:8, :], T.vin[0:8, :])
-    zeros("P1", 1024, 2048)
-    zeros("Z1", 0, 2048)
+    stage("d", 0, "y")
+    stage("c", 1, "s")
+    stage("b", 2, "y")
+    for x in EXCH:
+        exchange(x)
+    select("i2b", T.i2b[:, :], T.one[:, :], "one", [[0, 2], [-1, 128]], OP.is_equal, 0, 1)
+    iota("dj", T.dj, [[1, 128]], 128, -1)
+    select("gf0", T.gf0[:, :], T.one[:, 0:128], "one", [[-16, 8], [0, 16]], OP.is_ge, 0, 1)
+    iota("ki", T.ki, [[0, 8], [16, 2]], 0, 0)
+    select("gf", T.gf[:, :], T.gf0[:, :], "gf0", [[16, 8], [0, 16]], OP.is_ge, 15, -1)
+    select("i2f", T.i2f[:, :], T.one[:, 0:128], "one", [[-1, 128]], OP.is_equal, 0, 1)
+    iota("Z1", T.Z1, [[0, 2048]], 0, 0)
 
-    ts(["dj"], ["dk"], T.dk[:, :], T.dj[:, :], 127, OP.bitwise_and)
-    ts(["dk"], ["i2b"], T.i2b[:, :], T.dk[:, :], 0.0, OP.is_equal)
-    ts(["gm", "pgf"], ["gf"], T.gf[:, :], T.gm[:, :], T.col[:, 2:3], OP.is_equal)
-    ts(["jt", "g16"], ["jf"], T.jf[:, :], T.jt[:, :], T.col[:, 4:5], OP.subtract)
-    ts(["dj", "nz"], ["sh1"], T.sh1[:, :], T.dj[:, 0:128], 127.0, OP.is_equal, T.col[:, 0:1], OP.mult)
-    ts(["dj", "zf"], ["sh2"], T.sh2[:, :], T.dj[:, 0:128], 143.0, OP.is_equal, T.col[:, 1:2], OP.mult)
-    run("v", V.memset, [], ["e2"], T.e2[:, :], 0.0)
-    vcopy(["d16", "e2"], ["e2a"], T.e2[:, 0:32:2], T.d16[:, 0:16])
-    vcopy(["d16", "e2"], ["e2b"], T.e2[:, 33:64:2], T.d16[:, 0:16])
-    ts(["xt", "rc"], ["xr"], T.xr[:, 32:128], T.xt[:, 32:128], T.col[:, 5:6], OP.add)
-    ts(["xr"], ["xo"], T.xo[:, 32:128], T.xr[:, 32:128], 2047, OP.bitwise_and)
-    vcopy(["xo"], ["xu"], T.xu[:, 32:128], T.xo[:, 32:128])
-    vcopy(["xt"], ["xf"], T.xf[:, 0:32], T.xt[:, 0:32])
-    vcopy(["xt"], ["xf"], T.xf[:, 33:65], T.xt[:, 32:64])
-    vcopy(["lt3"], ["lu3"], T.lu[:, 48:64], T.lt[:, 48:64])
-    scopy(["ps6"], ["vr"], T.vr[:, :], bank(6)[:, :])
-    for i in range(16):
-        if i % 2:
-            run("s", S.activation, ["xf", "d16"], ["y1s"], T.y1[:, i::16], T.xf[:, :], AF.Copy, scale=T.d16[:, i:i + 1])
-        else:
-            ts(["xf", "d16"], ["y1v"], T.y1[:, i::16], T.xf[:, :], T.d16[:, i:i + 1], OP.mult)
-    mm(["gf", "y1s", "y1v"], ["ps5"], bank(5)[:, :], T.gf[:, :], T.y1[:, 0:512])
-    scopy(["ps5"], ["fla"], T.fla[:, :], bank(5)[:, :])
+    vcopy(["xta"], ["xf"], T.xf[:, 0:32], T.xt[:, 0:32])
+    vcopy(["xtb"], ["xfb"], T.xf[:, 40:72], T.xt[:, 64:96])
+    dma("s", "wx", ["xf"], ["wx"], T.wx[1::16, :], T.xf[:, 0:32])
+    dma("s", "wx", ["xfb"], ["wx"], T.wx[2::16, :], T.xf[:, 40:72])
+    dma("y", "ldn", [], ["xtc"], T.xt[:, 96:128], T.xc[:, :])
+    dma("y", "ldn", [], ["xtc"], T.xt[:, 128:160], T.xd[:, :])
+    dma("y", "ldz", [], ["xtl"], T.xt[:, 32:48], T.la[:, :])
+    dma("y", "ldz", [], ["xtl"], T.xt[:, 48:64], T.lb[:, :])
 
-    def scatter_places(xkey, x, b, outkey, out):
+    def following(xkey, x, b):
         k = "ps%d" % b
-        before("p", [xkey, "sh1", "sh2"], [k])
-        run("p", P.matmul, [xkey, "sh1"], [k], bank(b)[:, 0:32], T.sh1[:, :], x[:, 0:32], True, False)
-        run("p", P.matmul, [xkey, "sh2"], [k], bank(b)[:, 0:32], T.sh2[:, :], x[:, 1:33], False, True)
-        tt([xkey, k], [outkey + "e"], T.sa1[:, :], x[:, 0:32], bank(b)[:, 0:32], OP.not_equal)
-        tt([xkey, "jf"], [outkey + "d"], T.sa2[:, :], x[:, 0:32], T.jf[:, :], OP.subtract)
-        tt([outkey + "e", outkey + "d"], [outkey + "f"], T.sa2[:, :], T.sa2[:, :], T.sa1[:, :], OP.mult)
-        tt([outkey + "f", "jf"], [outkey + "h"], T.sa1[:, :], T.sa2[:, :], T.jf[:, :], OP.add)
-        vcopy([outkey + "h"], [outkey], out[:, :], T.sa1[:, :])
+        mm(xkey + ["sh1"], [k], bank(b)[:, 0:32], T.sh1[:, :], x[:, 0:32], True, False)
+        mm(xkey + ["sh2"], [k], bank(b)[:, 0:32], T.sh2[:, :], x[:, 1:33], False, True)
 
-    scatter_places("xf", T.xf, 7, "sau", T.sau)
-    run("v", V.memset, [], ["ma"], T.ma[:, 0:1], 0.0)
-    tt(["fla", "ps5"], ["ma"], T.ma[:, 1:512], T.fla[:, 1:512], bank(5)[:, 0:511], OP.is_equal)
+    def turned(key, x, xq, xs, xc, out, m):
+        ts([key], [out + "q"], xq, x, 4, OP.logical_shift_right)
+        ts([out + "q"], [out + "s"], xs, xq, 1.0 / m - 16, OP.mult)
+        tt([key, out + "s"], [out], xc, x, xs, OP.add)
 
-    def table(x, t, ident, ikey, groups, queues):
+    def ends(n, xkey, x, b, ckey, c, m):
+        eq, equ, su, W = T["eq" + n], T["equ" + n], T["su" + n], T["W" + n]
+        tt(xkey + ["ps%d" % b], ["eq" + n], eq[:, :], x[:, 0:32], bank(b)[:, 0:32], OP.is_equal)
+        tt(["eq" + n, "jf"], ["dm"], T.dm[:, :], eq[:, :], T.jf[:, :], OP.mult)
+        vcopy(["eq" + n], ["equ" + n], equ[:, :], eq[:, :])
+        tt(["dm", ckey], ["of"], T.of[:, :], T.dm[:, :], c, OP.max)
+        ts(["of"], ["su" + n], su[:, :], T.of[:, :], 128.0, OP.mult)
+
+    def invert(n, su, c0, c1):
+        vcopy(["pos", "su" + n, "W" + n], ["W" + n + "s"], T["W" + n][:, :].indirect(su[:, c0:c1]), T.pos[:, 16 * c0:16 * c1])
+
+    def relist(n):
+        dma("y", "ef" + n, ["W" + n, "W" + n + "s"], ["ef" + n], T["ef" + n][:, :], T["W" + n][0::16, 0:2048])
+
+    def same(n, m):
+        scopy(["mw", "equ" + n], ["m" + n], m[:, 1:513], T.mw[:, :].indirect(T["equ" + n][:, :]))
+
+    following(["xf"], T.xf, 7)
+    mm(["b8", "vin"], ["ps6"], bank(6)[:, :], T.b8[0:8, :], T.vin[0:8, :])
+    turned("xta", T.xt[:, 0:32], T.xq[:, 0:32], T.xs[:, 0:32], T.xc1[:, 0:32], "xc1", 128)
+    ends("1", ["xf"], T.xf, 7, "xc1", T.xc1[:, 0:32], T.ma)
+    invert("1", T.su1, 0, 32)
+    relist("1")
+    same("1", T.ma)
+    turned("obt", T.obt[:, :], T.oq[:, :], T.os1[:, :], T.oc[:, :], "oc", 32)
+    ts(["oc"], ["otu"], T.otu[:, :], T.oc[:, :], 32.0, OP.mult)
+    ts(["kt", "p16"], ["tu"], T.tu[:, :], T.kt[:, :], T.col[:, 7:8], OP.add)
+    scopy(["ps6"], ["vr"], T.vr[:, :], bank(6)[:, :])
+    scopy(["wx", "otu"], ["q1"], T.q1[:, :], T.wx[:, :].indirect(T.otu[:, :]))
+    scopy(["q1", "tu"], ["q2"], T.q2[:, :], T.q1[:, :].indirect(T.tu[:, :]))
+    ts(["xtb", "xtc", "rc"], ["xr"], T.xr[:, :], T.xt[:, 64:160], T.col[:, 5:6], OP.add)
+    fill("ma0", T.ma[:, 0:1], 0.0)
+    ts(["xr"], ["xo"], T.xo[:, :], T.xr[:, :], 2047, OP.bitwise_and)
+    fill("sg10", T.sg1[:, 512:520], 0.0)
+    vcopy(["xo"], ["xu"], T.xu[:, :], T.xo[:, :])
+    ts(["dj"], ["di"], T.di[:, :], T.dj[:, :], 15, OP.bitwise_and)
+    fill("fl2", T.fl2[:, :], 256.0)
+    ts(["di"], ["d16"], T.d16[:, :], T.di[:, :], 0.0, OP.is_equal)
+    vcopy(["xtl"], ["lnu"], T.lnu[:, :], T.xt[:, 32:48])
+    vcopy(["obt"], ["obu"], T.obu[:, :], T.obt[:, :])
+    fill("xbl1", T.xbl[:, 32:33], -1.0)
+
+    def table(x, t, groups):
         land, key, w = T["land" + x], "land" + x, 256
         dma("y", "cmp" + x, [key], [x + "0"], t[:, 0:w], land[:, :])
         byp = [d for _, ds, _ in groups for d in ds]
         for d in range(1, 8):
             if d not in byp:
-                q = queues[d % len(queues)]
-                dma(q, "rot" + x, [key], ["%s%d" % (x, d)], t[0:128 - 16 * d, d * w:(d + 1) * w], land[128 * d:1024, :])
-                dma(q, "rot" + x, [key], ["%s%d" % (x, d)], t[128 - 16 * d:128, d * w:(d + 1) * w], land[0:128 * d, :])
+                dma("y", "rot" + x, [key], ["%s%d" % (x, d)], t[0:128 - 16 * d, d * w:(d + 1) * w], land[128 * d:1024, :])
+                dma("y", "rot" + x, [key], ["%s%d" % (x, d)], t[128 - 16 * d:128, d * w:(d + 1) * w], land[0:128 * d, :])
         for b, ds, q in groups:
             n = len(ds)
             for i, d in enumerate(ds):
-                mm([ikey, x + "0"], ["ps%d" % b], bank(b)[:, i * w:(i + 1) * w], ident[:, 16 * d:16 * d + 128], t[:, 0:w])
-            (vcopy if q == "v" else scopy)(["ps%d" % b], ["%s%d" % (x, d) for d in ds], t[:, ds[0] * w:(ds[0] + n) * w], bank(b)[:, 0:n * w])
+                mm(["i2b", x + "0"], ["ps%d" % b], bank(b)[:, i * w:(i + 1) * w], T.i2b[:, 16 * d:16 * d + 128], t[:, 0:w])
+            copy(q, ["ps%d" % b], ["%s%d" % (x, d) for d in ds], t[:, ds[0] * w:(ds[0] + n) * w], bank(b)[:, 0:n * w])
         return ["%s%d" % (x, d) for d in range(8)]
 
-    kd = table("d", T.td, T.i2b, "i2b", ((0, (1, 2), "s"), (1, (3, 4), "v"), (2, (5,), "s"), (4, (6,), "v")), "y")
-    tt(kd + ["xu", "vr"], ["w1"], T.w1[:, :], T.td[:, :].indirect(T.xu[:, 96:128]), T.vr[:, :], OP.mult)
-    kc = table("c", T.tc, T.i2b, "i2b", ((3, (1, 2), "s"), (7, (3, 4), "s"), (6, (5,), "v")), "y")
-    tt(kc + ["xu", "w1"], ["w2"], T.w2[:, :], T.tc[:, :].indirect(T.xu[:, 64:96]), T.w1[:, :], OP.mult)
-    kb = table("b", T.tb, T.i2b, "i2b", ((0, (1, 2), "s"), (1, (3, 4), "s")), "y")
+    kd = table("d", T.td, ((0, (1, 2), "s"), (1, (3, 4), "v"), (2, (5,), "s"), (4, (6,), "v")))
+    tt(kd + ["xu", "vr"], ["w1"], T.w1[:, :], T.td[:, :].indirect(T.xu[:, 64:96]), T.vr[:, :], OP.mult)
+    kc = table("c", T.tc, ((3, (1, 2), "s"), (7, (3, 4), "s")))
+    vcopy(["ef1"], ["eu1"], T.eu1[:, :], T.ef1[:, :])
+    tt(kc + ["xu", "w1"], ["w2"], T.w2[:, :], T.tc[:, :].indirect(T.xu[:, 32:64]), T.w1[:, :], OP.mult)
+    kb = table("b", T.tb, ((0, (1, 2), "s"), (1, (3, 4), "s")))
+    dma("y", "xal", ["q2"], ["xal"], T.xal[:, :], T.q2[1::16, :])
+    dma("y", "xbl", ["q2"], ["xbl"], T.xbl[:, 0:32], T.q2[2::16, :])
+    blank(2, "y")
+    blank(3, "y")
     for k in range(8):
-        dma("y", "lda", [], ["fra"], T.fra[16 * k:16 * k + 16, :], T.fa[:, :])
-    tt(kb + ["xu", "w2"], ["pr1"], T.pr1[:, :], T.tb[:, :].indirect(T.xu[:, 32:64]), T.w2[:, :], OP.mult)
-    mm(["gf", "y1s", "y1v"], ["ps4"], bank(4)[:, :], T.gf[:, :], T.y1[:, 528:1040])
-    scopy(["ps4"], ["flb"], T.flb[:, :], bank(4)[:, :])
-    for k in range(1, 4):
-        scopy(["d16"], ["d16t"], T.d16[:, 128 * k:128 * k + 128], T.d16[:, 0:128])
-    vcopy(["obt"], ["obu"], T.obu[:, :], T.obt[:, :])
+        dma("y", "fas", [], ["fra"], T.fra[16 * k:16 * k + 16, :], T.fa[:, :])
+    tt(kb + ["xu", "w2"], ["pr1"], T.pr1[:, :], T.tb[:, :].indirect(T.xu[:, 0:32]), T.w2[:, :], OP.mult)
 
-    def segsum(mkey, m, pkey, p, skey, s, ukey, u, zkey, z):
-        run("v", V.tensor_tensor_scan, [mkey, pkey], [skey], s[:, :], m[:, :], p[:, :], 0.0, OP.mult, OP.add)
-        vcopy([skey, ukey, zkey], [zkey + "s"], z[:, :].indirect(u[:, :]), s[:, :])
+    def sums_out(x, keys, src, lst, G, r, lp, calls, sem, own, mid=None):
+        def pick(q, h):
+            c = 256 * q + 128 * h
+            copy("vs"[h], keys, ["%sG%d" % (x, c)], G[:, c:c + 128], src.indirect(lst[:, c // 16:c // 16 + 8]))
 
-    calls = {c: sum_calls(c, cores, topo) for c in cores}
-
-    def sums_out(x, keys, z, r, lp):
         def add(q, b, c):
             for h in range(2):
-                run("p", P.matmul, keys + ["d16", "e2a", "e2b"], ["ps%d" % b], bank(b)[:, c:c + 32],
-                    z[:, 256 * q + 128 * h:256 * q + 128 * h + 128], T.e2[:, 32 * h:32 * h + 32], h == 0, h == 1)
+                mm(["%sG%d" % (x, 256 * q + 128 * h), "d16"], ["ps%d" % b], bank(b)[:, c + h:c + 32:2],
+                   G[:, 256 * q + 128 * h:256 * q + 128 * h + 128], T.d16[:, 0:16])
+        order = [[cores.index(d) for d, _ in call] for call in calls[core]] + [[me]]
+        for q in order[0]:
+            pick(q, 0)
+            pick(q, 1)
         pos = 0
         for k, call in enumerate(calls[core]):
             n = 32 * len(call)
-            for j, (d, _) in enumerate(call):
-                add(cores.index(d), k, 32 * j)
-            (vcopy if k % 2 else scopy)(["ps%d" % k], ["%sr%d" % (x, k)], r[:, pos:pos + n], bank(k)[:, 0:n])
+            for j, q in enumerate(order[k]):
+                add(q, k, 32 * j)
+            for h in range(2):
+                pick(order[k + 1][0], h)
+            copy("vs"[k % 2], ["ps%d" % k], ["%sr%d" % (x, k)], r[:, pos:pos + n], bank(k)[:, 0:n])
+            for q in order[k + 1][1:]:
+                pick(q, 0)
+                pick(q, 1)
             before("g", ["%sr%d" % (x, k)], [])
-            g.remote_dma_fused([transfer(r[:, pos + 32 * j:pos + 32 * j + 32], lp[:, 32 * me:32 * me + 32], d, es, x)
+            g.remote_dma_fused([transfer(r[:, pos + 32 * j:pos + 32 * j + 32], lp[:, 32 * me:32 * me + 32], d, es, sem(core, d, k))
                                 for j, (d, es) in enumerate(call)], local_sem=T.sem["loc" + x])
             pos += n
+        own()
+        cnt["loc" + x] = sum(len(es) for call in calls[core] for _, es in call)
+        got = {}
+        for c in cores:
+            for k, call in enumerate(calls[c]):
+                for d, es in call:
+                    if d == core:
+                        s = sem(c, d, k)
+                        cnt[s] = cnt.get(s, 0) + len(es)
+                        got.setdefault(s, []).append(cores.index(c))
+        for s in got:
+            after("remote", (s, None), [], ["land" + s])
+        return add, got
+
+    late = {c: sum_calls(c, cores, topo, True) for c in cores}
+    early = {c: sum_calls(c, cores, topo, False) for c in cores}
+
+    def slot_sums(x, n, m, pr, sg, G, r, lp):
+        run("v", V.tensor_tensor_scan, ["m" + n, {"1": "ma0", "2": "mb0"}[n], "pr" + n], ["sg" + n], sg[:, 0:512], m[:, 0:512], pr[:, :], 0.0, OP.mult, OP.add)
+        add, _ = sums_out(x, ["sg" + n, "sg" + n + "0", "eu" + n], sg[:, :], T["eu" + n], G, r, lp, late, lambda c, d, k: "arr" + x, lambda: None)
         add(me, 4, 0)
         vcopy(["ps4"], [x + "me"], lp[:, 32 * me:32 * me + 32], bank(4)[:, 0:32])
-        cnt["loc" + x] = sum(len(es) for call in calls[core] for _, es in call)
-        cnt["arr" + x] = sum(len(es) for c in cores if c != core for call in calls[c] for d, es in call if d == core)
-        after("remote", ("arr" + x, None), [], ["land" + x])
 
-    def sums_in(x, lp, lq, c, zkey, z):
+    def sums_in(x, lp, lq, qs):
         for h in range(2):
-            mm(["land" + x, x + "me", "i2f"], ["ps%d" % (5 + h)], bank(5 + h)[:, 0:128], lp[:, h::2], T.i2f[:, 0:128])
-            scopy(["ps%d" % (5 + h)], ["%st%d" % (x, h)], lq[:, 128 * h:128 * h + 128], bank(5 + h)[:, 0:128])
-        for h in range(2):
-            vcopy(["%st%d" % (x, h), "lu2", "lu3", zkey] + [zkey + "s0"] * h, ["%ss%d" % (zkey, h)],
-                  z[:, :].indirect(T.lu[:, c + 8 * h:c + 8 * h + 8]), lq[:, 128 * h:128 * h + 128])
-        return [zkey, zkey + "s0", zkey + "s1"]
+            mm(["landarr" + x, x + "me", "i2f"], ["ps%d" % (5 + h)], bank(5 + h)[:, 0:128], lp[:, h::2], T.i2f[:, :])
+            copy(qs[h], ["ps%d" % (5 + h)], ["%st%d" % (x, h)], lq[:, 128 * h:128 * h + 128], bank(5 + h)[:, 0:128])
 
-    segsum("ma", T.ma, "pr1", T.pr1, "sg1", T.sg1, "sau", T.sau, "P1", T.P1)
-    sums_out("p1", ["P1", "P1s"], T.P1, T.r1, T.lp1)
-    ts(["dk"], ["i2f"], T.i2f[:, :], T.dk[:, :], 0.0, OP.is_equal)
-    zeros("P2", 0, 2048)
+    def columns(x, keys, z, h, b):
+        for j in range(8):
+            c = 1024 * h + 128 * j
+            mm(keys(c) + ["d16"], ["ps%d" % b], bank(b)[:, j:128:8], z[:, c:c + 128], T.d16[:, 0:16])
 
-    scopy(["flb", "obu"], ["fbp"], T.fbp[:, :], T.flb[:, :].indirect(T.obu[:, :]))
+    def store(x, h, b, b2, q, u, y3, y, sem, dq):
+        c = slice(128 * h, 128 * h + 128)
+        copy(q, ["ps%d" % b], ["%su%d" % (x, h)], u[:, c], bank(b)[:, 0:128])
+        mm(["%su%d" % (x, h), "i2f"], ["ps%d" % b2], bank(b2)[:, 0:128], u[:, c], T.i2f[:, :])
+        copy(q, ["ps%d" % b2], ["%sy%d" % (x, h)], y3[:, c], bank(b2)[:, 0:128])
+        dma(dq, sem, ["%sy%d" % (x, h)], [], y[:, 1024 * h:1024 * h + 1024], y3[:, c])
+
+    slot_sums("p1", "1", T.ma, T.pr1, T.sg1, T.G1, T.r1, T.lp1)
+
+    following(["xbl", "xbl1"], T.xbl, 7)
+    scopy(["fra", "lnu"], ["fas"], T.fas[:, :], T.fra[:, :].indirect(T.lnu[:, :]))
     scopy(["w2", "obu"], ["wp"], T.wp[:, :], T.w2[:, :].indirect(T.obu[:, :]))
-    tt(["flb", "obu", "d16", "d16t"], ["ba"], T.ba[:, 0:512], T.flb[:, :].indirect(T.obu[:, :]), T.d16[:, :], OP.mult)
-    tt(["fla", "obu", "d16", "d16t"], ["ba"], T.ba[:, 512:1024], T.fla[:, :].indirect(T.obu[:, :]), T.d16[:, :], OP.mult)
-    tt(["ba"], ["t1"], T.t1[:, :], T.ba[:, 0::2], T.ba[:, 1::2], OP.add)
+    ts(["ki", "pif"], ["pu"], T.pu[:, :], T.ki[:, 0:16:2], T.col[:, 6:7], OP.add)
+    vcopy(["xtl"], ["laf"], T.xf[:, 72:88], T.xt[:, 32:48])
+    vcopy(["xbl"], ["bi"], T.bi[:, :], T.xbl[:, 0:32])
+    tt(["laf", "pu", "gf"], ["ly"], T.ly[:, :], T.xf[:, 72:88].indirect(T.pu[:, :]), T.gf[:, :], OP.mult)
+    mm(["d16", "ly"], ["ps3"], bank(3)[:, 0:128], T.d16[:, :], T.ly[:, :])
+    turned("bi", T.bi[:, :], T.bq[:, :], T.bs[:, :], T.bc[:, :], "bc", 128)
+    vcopy(["ps3"], ["lru"], T.lru[:, :], bank(3)[:, 0:128])
+    ends("2", ["xbl", "xbl1"], T.xbl, 7, "bc", T.bc[:, :], T.mb)
+    ts(["ki", "pif"], ["ru"], T.ru[:, :], T.ki[:, :], T.col[:, 6:7], OP.add)
+    invert("2", T.su2, 0, 16)
 
-    kz = sums_in("p1", T.lp1, T.lq1, 48, "Z1", T.Z1)
-    for k, (c0, c1) in enumerate(((0, 512), (512, 1024), (1024, 1536), (1536, 1792), (1792, 2048))):
-        c = slice(c0, c1)
-        mm(["d16"] + kz, ["ps%d" % k], bank(k)[:, 0:c1 - c0], T.d16[:, 0:128], T.Z1[:, c])
-        tt(["ps%d" % k, "fra"], ["yar"], T.yar[:, c], bank(k)[:, 0:c1 - c0], T.fra[:, c], OP.mult)
-    scopy(["yar", "lu3"], ["gaS"], T.ga[:, 128:256], T.yar[:, :].indirect(T.lu[:, 56:64]))
-    vcopy(["yar", "lu3"], ["gaV"], T.ga[:, 0:128], T.yar[:, :].indirect(T.lu[:, 48:56]))
-    exchange("a", T.ga, ["gaS", "gaV"])
-    zeros("Z2", 0, 2048)
-    dma("y", "oya", ["yar"], [], T.ya[:, :], T.yar[0:16, :])
-
-    tt(["t1"], ["t2"], T.t2[:, :], T.t1[:, 0::2], T.t1[:, 1::2], OP.add)
-    tt(["t2"], ["t3"], T.t3[:, :], T.t2[:, 0::2], T.t2[:, 1::2], OP.add)
-    tt(["t3"], ["t4"], T.t4[:, :], T.t3[:, 0::2], T.t3[:, 1::2], OP.add)
-    run("v", V.memset, [], ["xg"], T.xg[:, 32:33], -1.0)
-    vcopy(["t4"], ["xg"], T.xg[:, 0:32], T.t4[:, 0:32])
-    ts(["t4", "rc"], ["ai"], T.ai[:, :], T.t4[:, 32:64], T.col[:, 5:6], OP.add)
-    ts(["ai"], ["aj"], T.aj[:, :], T.ai[:, :], 2047, OP.bitwise_and)
-    vcopy(["aj"], ["au"], T.au[:, :], T.aj[:, :])
-    scatter_places("xg", T.xg, 7, "sbu", T.sbu)
-    run("v", V.memset, [], ["mb"], T.mb[:, 0:1], 0.0)
-    tt(["fbp"], ["mb"], T.mb[:, 1:512], T.fbp[:, 1:512], T.fbp[:, 0:511], OP.is_equal)
-
-    ka = table("a", T.ta, T.i2f, "i2f", ((0, (1,), "s"), (1, (2,), "v"), (2, (3,), "s")), "y")
-    tt(ka + ["au", "wp"], ["pr2"], T.pr2[:, :], T.ta[:, :].indirect(T.au[:, :]), T.wp[:, :], OP.mult)
-    segsum("mb", T.mb, "pr2", T.pr2, "sg2", T.sg2, "sbu", T.sbu, "P2", T.P2)
-    sums_out("p2", ["P2", "P2s"], T.P2, T.r2, T.lp2)
-
-    kz = sums_in("p2", T.lp2, T.lq2, 32, "Z2", T.Z2)
-    kr = []
+    sums_in("p1", T.lp1, T.lq1, "ss")
     for h in range(2):
-        for q in range(8):
-            c = 256 * q + 128 * h
-            mm(kz + ["d16"], ["ps%d" % h], bank(h)[:, 16 * q:16 * q + 16], T.Z2[:, c:c + 128], T.d16[:, 0:16])
-        (vcopy if h else scopy)(["ps%d" % h], ["u3%d" % h], T.u3[:, 128 * h:128 * h + 128], bank(h)[:, 0:128])
+        tt(["p1t%d" % h, "fas", "lnu", "Z1"] + ["Z1s0"] * h, ["Z1s%d" % h], T.Z1[:, :].indirect(T.lnu[:, 8 * h:8 * h + 8]),
+           T.lq1[:, 128 * h:128 * h + 128], T.fas[:, 128 * h:128 * h + 128], OP.mult)
+    kz = ["Z1", "Z1s0", "Z1s1"]
+
+    def own_a():
+        c = 256 * me
+        mm(["aG%d" % c, "aG%d" % (c + 128), "d16"], ["ps4"], bank(4)[:, 0:256], T.d16[:, :], T.G2[:, c:c + 256])
+
+    _, got = sums_out("a", kz + ["lru"], T.Z1[:, :], T.lru, T.G2, T.ra, T.lpa, early,
+                      lambda c, d, k: "arra%d" % (3 if topo.chip(c) == topo.chip(d) else k), own_a)
+    scopy(["ps4"], ["ta%d" % me], T.ta[:, 256 * me:256 * me + 256], bank(4)[:, 0:256])
+    invert("2", T.su2, 16, 32)
+    relist("2")
+    same("2", T.mb)
+    vcopy(["xal"], ["au"], T.au[:, :], T.xal[:, :])
+
+    landing = [(s, q) for s in ("arra3", "arra0", "arra1", "arra2") for q in got[s]]
+
+    def widen(i):
+        s, q = landing[i]
+        copy("vs"[i % 2], ["land" + s, "ru"], ["rp%d" % q], T.rp[:, 256 * q:256 * q + 256], T.lpa[:, 32 * q:32 * q + 32].indirect(T.ru[:, :]))
+
+    widen(0)
+    widen(1)
+    for i, (s, q) in enumerate(landing):
+        for h in range(2):
+            mm(["rp%d" % q, "i2f"], ["ps%d" % (i % 4)], bank(i % 4)[:, 128 * h:128 * h + 128], T.rp[:, 256 * q + h:256 * q + 256:2], T.i2f[:, :])
+        if i + 2 < len(landing):
+            widen(i + 2)
+        if i == 1:
+            turned("xtl", T.xt[:, 48:64], T.xq[:, 48:64], T.xs[:, 48:64], T.xc1[:, 48:64], "xc3", 128)
+            ts(["xc3"], ["su3"], T.lsu[:, 0:16], T.xc1[:, 48:64], 128.0, OP.mult)
+        if i == 3:
+            fill("mb0", T.mb[:, 0:1], 0.0)
+            fill("sg20", T.sg2[:, 512:520], 0.0)
+            fill("lq20", T.lq2[:, 256:264], 0.0)
+        if i == 5:
+            vcopy(["ef2"], ["eu2"], T.eu2[:, :], T.ef2[:, :])
+        copy("vs"[i % 2], ["ps%d" % (i % 4)], ["ta%d" % q], T.ta[:, 256 * q:256 * q + 256], bank(i % 4)[:, 0:256])
+
+    tt(["ta%d" % q for q in range(8)] + ["au", "wp"], ["pr2"], T.pr2[:, :], T.ta[:, :].indirect(T.au[:, :]), T.wp[:, :], OP.mult)
+    columns("ya", lambda c: kz, T.Z1, 0, 5)
+    store("ya", 0, 5, 6, "s", T.ua, T.ya3, T.ya, "oya", "y")
+    slot_sums("p2", "2", T.mb, T.pr2, T.sg2, T.G1, T.r2, T.lp2)
+    columns("ya", lambda c: kz, T.Z1, 1, 7)
+    invert("3", T.lsu, 0, 16)
+    relist("3")
+    store("ya", 1, 7, 6, "s", T.ua, T.ya3, T.ya, "oya", "y")
+    vcopy(["ef3"], ["eu3"], T.eu3[:, :], T.ef3[:, :])
+
+    sums_in("p2", T.lp2, T.lq2, "vs")
     for h in range(2):
-        run("p", P.transpose, ["u3%d" % h, "i2f"], ["ps%d" % (2 + h)], bank(2 + h)[:, 0:128], T.u3[:, 128 * h:128 * h + 128], T.i2f[:, 0:128])
-        (vcopy if h else scopy)(["ps%d" % (2 + h)], ["r3%d" % h], T.r3[:, 128 * h:128 * h + 128], bank(2 + h)[:, 0:128])
-        kr.append("r3%d" % h)
-    for q in range(8):
-        dma("s" if q % 2 else "y", "oyb", kr, [], T.yb[:, 256 * q:256 * q + 256], T.r3[16 * q:16 * q + 16, :])
+        for j in range(8):
+            c = 1024 * h + 128 * j
+            copy("vs"[j % 2], ["p2t0", "p2t1", "lq20", "eu3"], ["bG%d" % c, "aG%d" % c], T.G2[:, c:c + 128], T.lq2[:, :].indirect(T.eu3[:, c // 16:c // 16 + 8]))
+    columns("yb", lambda c: ["bG%d" % c], T.G2, 0, 0)
+    columns("yb", lambda c: ["bG%d" % c], T.G2, 1, 1)
+    store("yb", 0, 0, 2, "s", T.ub, T.yb3, T.yb, "oyb", "y")
+    store("yb", 1, 1, 3, "v", T.ub, T.yb3, T.yb, "oyb", "y")
 
     need("g", [(s, cnt[s]) for s in cnt])

@@ -9,65 +9,67 @@ def sb(n, d=F):
 
 
 SCRATCH = {
-    "win": sb(2048, B), "lt": sb(64, I), "lu": sb(64, U), "g0": sb(1024, B), "fra": sb(2048, B), "fas": sb(256),
+    "win": sb(2048, B), "lt": sb(64, I), "lu": sb(64, U), "g0": sb(1024, B), "fas": sb(256, B),
     "xt": sb(160, I), "xr": sb(96, I), "xo": sb(96, I), "xu": sb(96, U),
     "obt": sb(32, I), "obu": sb(32, U), "vin": sb(512), "vr": sb(512),
-    "pc": sb(8, I), "dj": sb(128, I), "jt": sb(32, I), "pi": sb(8, I), "pg": sb(8, I), "col": sb(16),
-    "di": sb(128, I), "d16": sb(128), "one": sb(256), "i2f": sb(128), "i2b": sb(256, B),
-    "sh0": sb(128), "gf0": sb(128), "sh1": sb(128), "sh2": sb(128), "b8": sb(128), "gf": sb(128), "jf": sb(32), "pos": sb(512),
-    "ki": sb(16, I), "kt": sb(32, I), "ru": sb(16, U), "pu": sb(8, U), "tu": sb(32, U), "mw": sb(8), "fl1": sb(128), "fl2": sb(128),
+    "sndd": ("dram", [1024, 32], B), "landd": ("dram", [1024, 32], B),
+    "sndc": ("dram", [1024, 32], B), "landc": ("dram", [1024, 32], B),
+    "sndb": ("dram", [1024, 32], B), "landb": ("dram", [1024, 32], B),
+    "pc": sb(8, I), "dj": sb(16, I), "jt": sb(32, I), "pi": sb(8, I), "pg": sb(8, I), "col": sb(16),
+    "di": sb(16, I), "d16": sb(16), "one": sb(256), "i2f": sb(256), "i2b": sb(256, B),
+    "sh0": sb(128), "gf0": sb(128), "sh1": sb(128), "sh2": sb(128), "b8": sb(128), "gf": sb(128), "jf": sb(32), "pos": sb(512), "pos0": sb(256),
+    "kt": sb(32, I), "pu": sb(8, U), "tu": sb(32, U), "mw": sb(8), "fl1": sb(128), "fl3": sb(128, B),
+    "W4": sb(2048, B), "cf": sb(256), "ef4": sb(128), "eu4": sb(128, U), "lnt": sb(16, U),
+    "ai": sb(32, I), "aw": sb(320, I),
     "xf": sb(104), "xq": sb(64, I), "xs": sb(64), "xc1": sb(64), "lsu": sb(32, U), "lnu": sb(16, U),
     "eq1": sb(32), "eq2": sb(32), "equ1": sb(32, U), "equ2": sb(32, U), "dm": sb(32), "of": sb(32), "su1": sb(32, U), "su2": sb(32, U),
     "ma": sb(520), "mb": sb(520), "W1": sb(2688), "W2": sb(2688), "W3": sb(2048),
     "ef1": sb(128), "ef2": sb(128), "ef3": sb(128), "eu1": sb(128, U), "eu2": sb(128, U), "eu3": sb(128, U),
-    "ly": sb(128), "lru": sb(128, U),
+    "ly": sb(128),
     "oq": sb(32, I), "os1": sb(32), "oc": sb(32), "otu": sb(32, U), "wx": sb(512), "q1": sb(512), "q2": sb(512),
     "xal": sb(32), "xbl": sb(40), "au": sb(32, U), "bi": sb(32, I), "bq": sb(32, I), "bs": sb(32), "bc": sb(32),
-    "sndd": ("dram", [1024, 32], B), "landd": ("dram", [1024, 32], B),
-    "sndc": ("dram", [1024, 32], B), "landc": ("dram", [1024, 32], B),
-    "sndb": ("dram", [1024, 32], B), "landb": ("dram", [1024, 32], B),
     "td": sb(2048, B), "tc": sb(2048, B), "tb": sb(2048, B), "ta": sb(2048),
     "w1": sb(512), "w2": sb(512), "wp": sb(512), "pr1": sb(512), "pr2": sb(512), "sg1": sb(520), "sg2": sb(520),
-    "G1": sb(2048), "G2": sb(2048), "Z1": sb(2048), "rp": sb(2048),
+    "G1": sb(2048), "G2": sb(2048), "Z1": sb(2048),
     "r1": sb(256), "r2": sb(256), "ra": sb(256), "ua": sb(256), "ub": sb(256), "ya3": sb(256), "yb3": sb(256),
-    "lp1": sb(256), "lq1": sb(256), "lp2": sb(256), "lq2": sb(264), "lpa": sb(256),
+    "lp1": sb(256), "lq1": sb(264), "lp2": sb(256), "lq2": sb(520), "lpa": sb(256),
     "ps0": ("psum", [128, 512], F), "ps1": ("psum", [128, 512], F), "ps2": ("psum", [128, 512], F), "ps3": ("psum", [128, 512], F),
     "ps4": ("psum", [128, 512], F), "ps5": ("psum", [128, 512], F), "ps6": ("psum", [128, 512], F), "ps7": ("psum", [128, 512], F),
 }
-EXCH = ["d", "c", "b"]
 SEMAPHORES = (["c_g", "c_v", "c_s", "c_p", "ldw", "ldl", "ldx", "ldn", "ldo", "ldv", "ldy", "ldz", "fas", "fil1", "fil2", "fil3",
-               "ef1", "ef2", "ef3", "wx", "xal", "xbl", "oya", "oyb"]
-              + [k + x for x in EXCH for k in ("snd", "self", "arr", "loc", "cmp", "rot")]
-              + [k + x for x in ("p1", "p2") for k in ("arr", "loc")] + ["loca", "arra0", "arra1", "arra2", "arra3"])
+               "ef1", "ef2", "ef3", "wx", "xal", "xbl", "oya", "oyb", "arrp1", "arrp2", "fil4", "ef4", "inv",
+               "rota0", "rota1", "rota2", "rota3"]
+              + [k + x for x in "dcb" for k in ("snd", "self", "arr", "loc", "cmp", "rot")]
+              + ["loc" + x for x in ("p1", "a", "p2")] + ["arra%d" % k for k in range(7)])
+LATE, EARLY = ((2, 2, 1, 1), 2), ((2, 2, 2), 0)
+AHEAD = 2
+LIFT = 32
+BY_PE = (2, 4, 4, 7)
 
 
-def ways(src, cores, topo):
+def long_call(src, cores, topo):
     off = [d for d in cores if topo.chip(d) != topo.chip(src)]
-    on = [d for d in cores if d != src and topo.chip(d) == topo.chip(src)]
     far = [d for d in off if not topo.mates(topo.chip(src), topo.chip(d)) and not topo.same_plane(topo.chip(src), topo.chip(d))]
-    return far, [d for d in off if d not in far], on
-
-
-def send_engines(src, cores, topo):
-    far, near, on = ways(src, cores, topo)
+    near = [d for d in off if d not in far]
     e = topo.engines(src, near[0])
     one, two = e[0::2], e[1::2]
     n = len(two) // len(far)
-    p = {d: [one[i]] for i, d in enumerate(near)}
-    p.update({d: two[i * n:(i + 1) * n] for i, d in enumerate(far)})
-    for i, d in enumerate(on):
-        p[d] = [x for x in topo.engines(src, d) if x not in e][i:i + 1]
-    return p
+    call = [(d, [one[i]]) for i, d in enumerate(near)] + [(d, two[i * n:(i + 1) * n]) for i, d in enumerate(far)]
+    on = [d for d in cores if d != src and d not in off]
+    return call + [(d, [x for x in topo.engines(src, d) if x not in e][i:i + 1]) for i, d in enumerate(on)]
 
 
-def sum_calls(src, cores, topo, last):
-    far, near, on = ways(src, cores, topo)
-    off = far + sorted(near, key=lambda d: not topo.mates(topo.chip(src), topo.chip(d)))
+def plan_calls(src, cores, topo, sizes, home):
+    off = [d for d in cores if topo.chip(d) != topo.chip(src)]
+    on = [d for d in cores if d != src and topo.chip(d) == topo.chip(src)]
+    off.sort(key=lambda d: (topo.same_plane(topo.chip(src), topo.chip(d)), topo.mates(topo.chip(src), topo.chip(d)), topo.die(d) != topo.die(src)))
     e = topo.engines(src, off[0])
-    n = len(e) // 2
-    calls = [[(off[2 * k], e[0:n]), (off[2 * k + 1], e[n:2 * n])] for k in range(len(off) // 2)]
+    calls = []
+    for m in sizes:
+        n = len(e) // max(m, 1)
+        calls.append([(off.pop(0), e[j * n:j * n + n]) for j in range(m)])
     for d in on:
-        calls[-1 if last else 0].append((d, [x for x in topo.engines(src, d) if x not in e][0:n]))
+        calls[home].append((d, [x for x in topo.engines(src, d) if x not in e][0:len(e) // 2]))
     return calls
 
 
@@ -155,153 +157,186 @@ def rank_program(g, core, T, topo):
         else:
             run("g", g.iota, [], [key], out[:, :], pattern, base, cm)
 
-    for f, x in enumerate((T.fd, T.fc, T.fb)):
+    def select(key, out, src, skey, pattern, op, base, cm):
+        run("g", g.affine_select, [skey], [key], out[:, :], src[:, 0:128], pattern, op, 0.0, base, cm)
+
+    def send(x, call, k, key, src, dst, sem):
+        trs = []
+        for j, (d, es) in enumerate(call):
+            rid, pid, _ = topo.addr(d)
+            trs.append(RemoteDMATransfer(dst_ids=[DstId(rid=rid, pnc=pid)], dma_engine_mask=sum(1 << e for e in es),
+                                         remote_sem=T.sem[sem(core, d, k)], src=src(j, cores.index(d)), dst=dst))
+        before("g", key, [])
+        g.remote_dma_fused(trs, local_sem=T.sem["loc" + x])
+        cnt["loc" + x] = cnt.get("loc" + x, 0) + sum(len(es) for _, es in call)
+
+    def arrivals(calls, sem):
+        got = {}
+        for c in cores:
+            for k, call in enumerate(calls[c]):
+                for d, es in call:
+                    if d == core:
+                        s = sem(c, d, k)
+                        cnt[s] = cnt.get(s, 0) + len(es)
+                        got.setdefault(s, []).append(cores.index(c))
+        for s in got:
+            after("remote", (s, None), [], ["land" + s])
+        return got
+
+    def by_call(x):
+        return lambda c, d, k: "arr%s%d" % (x, 0 if topo.chip(c) == topo.chip(d) else k + 1)
+
+    late, early = [{c: plan_calls(c, cores, topo, *p) for c in cores} for p in (LATE, EARLY)]
+
+    def factor(f, x):
         for e in range(2):
             dma("ys"[e], "ldw", [], ["win"], T.win[32 * f + 16 * e:32 * f + 16 * e + 16, :], x[:, :])
-    for f, l in enumerate((T.ld, T.lc, T.lb)):
+
+    factor(0, T.fd)
+    factor(1, T.fc)
+    factor(2, T.fb)
+    for f, l in enumerate((T.ld, T.lc, T.lb, T.la)):
         for u in range(4):
             dma("ys"[u % 2], "ldl", [], ["lt"], T.lt[32 * f:32 * f + 32, 16 * u:16 * u + 16], l[32 * u:32 * u + 32, :])
+    factor(3, T.fa)
     dma("y", "ldx", [], ["xta"], T.xt[:, 0:32], T.xa[:, :])
     dma("s", "ldy", [], ["xtb"], T.xt[:, 64:96], T.xb[:, :])
-    fill("win0", T.win[96:128, :], 0.0)
-    fill("lt0", T.lt[96:128, :], 0)
-
-    def select(key, out, src, skey, pattern, op, base, cm):
-        run("g", g.affine_select, [skey], [key], out, src, pattern, op, 0.0, base, cm)
 
     fill("one", T.one[:, :], 1.0)
-    iota("pos", T.pos, [[1, 512]], 0, 0)
+    iota("pos", T.pos, [[1, 512]], LIFT, 0)
     iota("pc", T.pc, [[0, 8]], 0, 1)
     iota("jt", T.jt, [[16, 32]], 2048, 1)
-    select("sh0", T.sh0[:, :], T.one[:, 0:128], "one", [[-1, 128]], OP.is_equal, -1, 1)
-    select("sh2", T.sh2[:, :], T.one[:, 0:128], "one", [[-16, 8], [256, 16]], OP.is_equal, -256 * 15, 1)
-    select("sh1", T.sh1[:, :], T.sh0[:, :], "sh0", [[0, 8], [1, 16]], OP.not_equal, -15, 0)
-    select("b8", T.b8[:, :], T.one[:, 0:128], "one", [[-1, 8], [0, 16]], OP.is_equal, 0, 1)
+    select("sh0", T.sh0, T.one, "one", [[-1, 128]], OP.is_equal, -1, 1)
+    select("sh2", T.sh2, T.one, "one", [[-16, 8], [256, 16]], OP.is_equal, -256 * 15, 1)
+    select("sh1", T.sh1, T.sh0, "sh0", [[0, 8], [1, 16]], OP.not_equal, -15, 0)
+    select("b8", T.b8, T.one, "one", [[-1, 8], [0, 16]], OP.is_equal, 0, 1)
     iota("kt", T.kt, [[1, 16], [256, 2]], 0, 0)
-    fill("fl1", T.fl1[:, :], 512.0)
+    fill("fl1", T.fl1[:, :], 512.0 + LIFT)
+    fill("fl3", T.fl3[:, :], 256.0)
     fill("xf", T.xf[:, 32:33], -1.0)
     fill("mw", T.mw[:, 0:1], 0.0)
     fill("mw", T.mw[:, 1:8], 1.0)
+    fill("wx", T.wx[:, :], 0.0)
+    fill("lq20", T.lq2[:, 256:520], 0.0)
     ts(["pc"], ["pi"], T.pi[:, 0:1], T.pc[:, 0:1], 15, OP.bitwise_and)
     ts(["pc"], ["pg"], T.pg[:, 0:1], T.pc[:, 0:1], 4, OP.logical_shift_right)
     ts(["jt"], ["jf"], T.jf[:, :], T.jt[:, :], 1.0 / 128, OP.mult)
     ts(["pg"], ["rc"], T.col[:, 5:6], T.pg[:, 0:1], -256.0, OP.mult, 2048.0, OP.add)
+    ts(["pg"], ["rc4"], T.col[:, 8:9], T.pg[:, 0:1], -64.0, OP.mult, 512.0, OP.add)
     ts(["pi"], ["p16"], T.col[:, 7:8], T.pi[:, 0:1], 16.0, OP.mult)
     vcopy(["pi"], ["pif"], T.col[:, 6:7], T.pi[:, 0:1])
-    fill("wx", T.wx[:, :], 0.0)
+    for key, ap in (("ma0", T.ma[:, 0:1]), ("mb0", T.mb[:, 0:1]), ("sg10", T.sg1[:, 512:520]), ("sg20", T.sg2[:, 512:520]), ("lq10", T.lq1[:, 256:264])):
+        fill(key, ap, 0.0)
+    fill("xbl1", T.xbl[:, 32:33], -1.0)
     vcopy(["lt", "lt0"], ["lu"], T.lu[:, :], T.lt[:, :])
 
-    def blank(k, q):
-        dma(q, "fil%d" % k, ["fl1", "fl2"], ["W%d" % k], T["W%d" % k][0::16, 0:2048], (T.fl2 if k == 3 else T.fl1)[:, :])
-
-    blank(1, "y")
+    dma("y", "fil1", ["fl1"], ["W1"], T.W1[0::16, 0:2048], T.fl1[:, :])
+    dma("y", "ldz", [], ["xtl"], T.xt[:, 32:48], T.la[:, :])
+    dma("y", "ldz", [], ["xtl"], T.xt[:, 48:64], T.lb[:, :])
     dma("y", "ldo", [], ["obt"], T.obt[:, :], T.ob[:, :])
     dma("y", "ldv", [], ["vin"], T.vin[0:8, :], T.v[:, :])
 
     for u in range(4):
         copy("vs"[u % 2], ["win", "win0", "lu"], ["g0%d" % u], T.g0[:, 256 * u:256 * u + 256], T.win[:, :].indirect(T.lu[:, 16 * u:16 * u + 16]))
 
-    plans = {c: send_engines(c, cores, topo) for c in cores}
-
-    def transfer(src, dst, d, es, sem):
-        rid, pid, _ = topo.addr(d)
-        mask = 0
-        for e in es:
-            mask |= 1 << e
-        return RemoteDMATransfer(dst_ids=[DstId(rid=rid, pnc=pid)], dma_engine_mask=mask, remote_sem=T.sem[sem], src=src, dst=dst)
+    wide = {c: [long_call(c, cores, topo)] for c in cores}
 
     def stage(x, f, q):
         snd, land = T["snd" + x], T["land" + x]
         for u in range(4):
             dma(q, "snd" + x, ["g0%d" % u], ["snd" + x], snd[256 * u:256 * u + 256, :], T.g0[32 * f:32 * f + 32, 256 * u:256 * u + 256])
         p, u = 32 * f + 16 * (me % 2), me // 2
-        dma(q, "self" + x, ["g0%d" % u], ["land" + x], land[128 * me:128 * me + 128, :], T.g0[p:p + 16, 256 * u:256 * u + 256])
-
-    def exchange(x):
-        snd, land = T["snd" + x], T["land" + x]
-        before("g", ["snd" + x], [])
-        g.remote_dma_fused([transfer(snd[128 * cores.index(d):128 * cores.index(d) + 128, :], land[128 * me:128 * me + 128, :], d, es, "arr" + x)
-                            for d, es in plans[core].items()], local_sem=T.sem["loc" + x])
-        cnt["loc" + x] = sum(len(es) for es in plans[core].values())
-        cnt["arr" + x] = sum(len(plans[c][core]) for c in cores if c != core)
-        after("remote", ("arr" + x, None), [], ["land" + x])
+        dma(q, "self" + x, ["g0%d" % u], ["landarr" + x], land[128 * me:128 * me + 128, :], T.g0[p:p + 16, 256 * u:256 * u + 256])
 
     stage("d", 0, "y")
     stage("c", 1, "s")
     stage("b", 2, "y")
-    for x in EXCH:
-        exchange(x)
-    select("i2b", T.i2b[:, :], T.one[:, :], "one", [[0, 2], [-1, 128]], OP.is_equal, 0, 1)
-    iota("dj", T.dj, [[1, 128]], 128, -1)
-    select("gf0", T.gf0[:, :], T.one[:, 0:128], "one", [[-16, 8], [0, 16]], OP.is_ge, 0, 1)
-    iota("ki", T.ki, [[0, 8], [16, 2]], 0, 0)
-    select("gf", T.gf[:, :], T.gf0[:, :], "gf0", [[16, 8], [0, 16]], OP.is_ge, 15, -1)
-    select("i2f", T.i2f[:, :], T.one[:, 0:128], "one", [[-1, 128]], OP.is_equal, 0, 1)
+    for x in "dcb":
+        send(x, wide[core][0], 0, ["snd" + x], lambda j, r: T["snd" + x][128 * r:128 * r + 128, :], T["land" + x][128 * me:128 * me + 128, :],
+             lambda c, d, k: "arr" + x)
+        arrivals(wide, lambda c, d, k: "arr" + x)
+    iota("pos0", T.pos0, [[1, 256]], 0, 0)
+    iota("dj", T.dj, [[1, 16]], 128, -1)
+    select("gf0", T.gf0, T.one, "one", [[-16, 8], [0, 16]], OP.is_ge, 0, 1)
+    run("g", g.affine_select, ["one"], ["i2b"], T.i2b[:, :], T.one[:, :], [[0, 2], [-1, 128]], OP.is_equal, 0.0, 0, 1)
+    select("gf", T.gf, T.gf0, "gf0", [[16, 8], [0, 16]], OP.is_ge, 15, -1)
+    run("g", g.affine_select, ["one"], ["i2f"], T.i2f[:, :], T.one[:, :], [[0, 2], [-1, 128]], OP.is_equal, 0.0, 0, 1)
     iota("Z1", T.Z1, [[0, 2048]], 0, 0)
-
-    vcopy(["xta"], ["xf"], T.xf[:, 0:32], T.xt[:, 0:32])
-    vcopy(["xtb"], ["xfb"], T.xf[:, 40:72], T.xt[:, 64:96])
-    dma("s", "wx", ["xf"], ["wx"], T.wx[1::16, :], T.xf[:, 0:32])
-    dma("s", "wx", ["xfb"], ["wx"], T.wx[2::16, :], T.xf[:, 40:72])
-    dma("y", "ldn", [], ["xtc"], T.xt[:, 96:128], T.xc[:, :])
-    dma("y", "ldn", [], ["xtc"], T.xt[:, 128:160], T.xd[:, :])
-    dma("y", "ldz", [], ["xtl"], T.xt[:, 32:48], T.la[:, :])
-    dma("y", "ldz", [], ["xtl"], T.xt[:, 48:64], T.lb[:, :])
 
     def following(xkey, x, b):
         k = "ps%d" % b
         mm(xkey + ["sh1"], [k], bank(b)[:, 0:32], T.sh1[:, :], x[:, 0:32], True, False)
         mm(xkey + ["sh2"], [k], bank(b)[:, 0:32], T.sh2[:, :], x[:, 1:33], False, True)
 
-    def turned(key, x, xq, xs, xc, out, m):
-        ts([key], [out + "q"], xq, x, 4, OP.logical_shift_right)
+    def turned(key, x, xq, xs, xc, out, m, more=()):
+        ts([key, *more], [out + "q"], xq, x, 4, OP.logical_shift_right)
         ts([out + "q"], [out + "s"], xs, xq, 1.0 / m - 16, OP.mult)
         tt([key, out + "s"], [out], xc, x, xs, OP.add)
 
-    def ends(n, xkey, x, b, ckey, c, m):
-        eq, equ, su, W = T["eq" + n], T["equ" + n], T["su" + n], T["W" + n]
+    def ends(n, xkey, x, b, ckey, c):
+        eq, equ, su = T["eq" + n], T["equ" + n], T["su" + n]
         tt(xkey + ["ps%d" % b], ["eq" + n], eq[:, :], x[:, 0:32], bank(b)[:, 0:32], OP.is_equal)
         tt(["eq" + n, "jf"], ["dm"], T.dm[:, :], eq[:, :], T.jf[:, :], OP.mult)
         vcopy(["eq" + n], ["equ" + n], equ[:, :], eq[:, :])
         tt(["dm", ckey], ["of"], T.of[:, :], T.dm[:, :], c, OP.max)
         ts(["of"], ["su" + n], su[:, :], T.of[:, :], 128.0, OP.mult)
 
-    def invert(n, su, c0, c1):
-        vcopy(["pos", "su" + n, "W" + n], ["W" + n + "s"], T["W" + n][:, :].indirect(su[:, c0:c1]), T.pos[:, 16 * c0:16 * c1])
+    def invert(q, n, su, c0, c1):
+        rd, wr, out, in_ = ["pos", "su" + n, "W" + n], ["W" + n + "s"], T["W" + n][:, :].indirect(su[:, c0:c1]), T.pos[:, 16 * c0:16 * c1]
+        if q == "v":
+            vcopy(rd, wr, out, in_)
+        else:
+            run("s", S.activation, rd, wr, out, in_, AF.Silu)
 
-    def relist(n):
-        dma("y", "ef" + n, ["W" + n, "W" + n + "s"], ["ef" + n], T["ef" + n][:, :], T["W" + n][0::16, 0:2048])
+    def relist(n, q="y"):
+        dma(q, "ef" + n, ["W" + n, "W" + n + "s"], ["ef" + n], T["ef" + n][:, :], T["W" + n][0::16, 0:2048])
+
+    def listed(n):
+        ts(["ef" + n], ["eu" + n], T["eu" + n][:, :], T["ef" + n][:, :], 0.25 - LIFT, OP.add)
 
     def same(n, m):
         scopy(["mw", "equ" + n], ["m" + n], m[:, 1:513], T.mw[:, :].indirect(T["equ" + n][:, :]))
 
+    vcopy(["xta"], ["xf"], T.xf[:, 0:32], T.xt[:, 0:32])
+    vcopy(["xtb"], ["xfb"], T.xf[:, 40:72], T.xt[:, 64:96])
+    dma("s", "wx", ["xf"], ["wx"], T.wx[1::16, :], T.xf[:, 0:32])
+    dma("s", "wx", ["xfb"], ["wx"], T.wx[2::16, :], T.xf[:, 40:72])
+    dma("y", "fil3", ["fl1"], ["W3"], T.W3[0::16, 0:2048], T.fl1[:, :])
+    dma("y", "ldn", [], ["xtc"], T.xt[:, 96:128], T.xc[:, :])
+    dma("y", "ldn", [], ["xtc"], T.xt[:, 128:160], T.xd[:, :])
+    dma("y", "fil4", ["fl3"], ["W4"], T.W4[0::16, :], T.fl3[:, :])
     following(["xf"], T.xf, 7)
     mm(["b8", "vin"], ["ps6"], bank(6)[:, :], T.b8[0:8, :], T.vin[0:8, :])
-    turned("xta", T.xt[:, 0:32], T.xq[:, 0:32], T.xs[:, 0:32], T.xc1[:, 0:32], "xc1", 128)
-    ends("1", ["xf"], T.xf, 7, "xc1", T.xc1[:, 0:32], T.ma)
-    invert("1", T.su1, 0, 32)
+    turned("xta", T.xt[:, 0:64], T.xq[:, :], T.xs[:, :], T.xc1[:, :], "xc1", 128, ["xtl"])
+    ends("1", ["xf"], T.xf, 7, "xc1", T.xc1[:, 0:32])
+    ts(["xc1"], ["su3"], T.lsu[:, 0:16], T.xc1[:, 48:64], 128.0, OP.mult)
+    invert("v", "1", T.su1, 0, 32)
     relist("1")
     same("1", T.ma)
+    scopy(["ps6"], ["vr"], T.vr[:, :], bank(6)[:, :])
+    invert("s", "3", T.lsu, 0, 16)
+    relist("3", "s")
     turned("obt", T.obt[:, :], T.oq[:, :], T.os1[:, :], T.oc[:, :], "oc", 32)
     ts(["oc"], ["otu"], T.otu[:, :], T.oc[:, :], 32.0, OP.mult)
     ts(["kt", "p16"], ["tu"], T.tu[:, :], T.kt[:, :], T.col[:, 7:8], OP.add)
-    scopy(["ps6"], ["vr"], T.vr[:, :], bank(6)[:, :])
     scopy(["wx", "otu"], ["q1"], T.q1[:, :], T.wx[:, :].indirect(T.otu[:, :]))
     scopy(["q1", "tu"], ["q2"], T.q2[:, :], T.q1[:, :].indirect(T.tu[:, :]))
     ts(["xtb", "xtc", "rc"], ["xr"], T.xr[:, :], T.xt[:, 64:160], T.col[:, 5:6], OP.add)
-    fill("ma0", T.ma[:, 0:1], 0.0)
-    ts(["xr"], ["xo"], T.xo[:, :], T.xr[:, :], 2047, OP.bitwise_and)
-    fill("sg10", T.sg1[:, 512:520], 0.0)
-    vcopy(["xo"], ["xu"], T.xu[:, :], T.xo[:, :])
-    ts(["dj"], ["di"], T.di[:, :], T.dj[:, :], 15, OP.bitwise_and)
-    fill("fl2", T.fl2[:, :], 256.0)
-    ts(["di"], ["d16"], T.d16[:, :], T.di[:, :], 0.0, OP.is_equal)
     vcopy(["xtl"], ["lnu"], T.lnu[:, :], T.xt[:, 32:48])
+    ts(["xr"], ["xo"], T.xo[:, :], T.xr[:, :], 2047, OP.bitwise_and)
+    ts(["dj"], ["di"], T.di[:, :], T.dj[:, 0:16], 15, OP.bitwise_and)
+    vcopy(["xo"], ["xu"], T.xu[:, :], T.xo[:, :])
+    ts(["di"], ["d16"], T.d16[:, :], T.di[:, :], 0.0, OP.is_equal)
+    vcopy(["pos0", "lnu", "W4"], ["W4s"], T.W4[:, :].indirect(T.lnu[:, :]), T.pos0[:, :])
+    ts(["one", "pif"], ["pu"], T.pu[:, :], T.one[:, 0:8], T.col[:, 6:7], OP.mult)
+    vcopy(["xtl"], ["laf"], T.xf[:, 72:88], T.xt[:, 32:48])
     vcopy(["obt"], ["obu"], T.obu[:, :], T.obt[:, :])
-    fill("xbl1", T.xbl[:, 32:33], -1.0)
+    tt(["laf", "pu", "gf"], ["ly"], T.ly[:, :], T.xf[:, 72:88].indirect(T.pu[:, :]), T.gf[:, :], OP.mult)
+    mm(["d16", "ly"], ["ps5"], bank(5)[:, 0:16], T.ly[:, :], T.d16[:, :])
+    vcopy(["ps5"], ["lnt"], T.lnt[:, :], bank(5)[:, 0:16])
 
     def table(x, t, groups):
-        land, key, w = T["land" + x], "land" + x, 256
+        land, key, w = T["land" + x], "landarr" + x, 256
         dma("y", "cmp" + x, [key], [x + "0"], t[:, 0:w], land[:, :])
         byp = [d for _, ds, _ in groups for d in ds]
         for d in range(1, 8):
@@ -315,75 +350,68 @@ def rank_program(g, core, T, topo):
             copy(q, ["ps%d" % b], ["%s%d" % (x, d) for d in ds], t[:, ds[0] * w:(ds[0] + n) * w], bank(b)[:, 0:n * w])
         return ["%s%d" % (x, d) for d in range(8)]
 
-    kd = table("d", T.td, ((0, (1, 2), "s"), (1, (3, 4), "v"), (2, (5,), "s"), (4, (6,), "v")))
+    kd = table("d", T.td, ((0, (1, 2), "s"), (1, (3, 4), "v"), (2, (5,), "s")))
     tt(kd + ["xu", "vr"], ["w1"], T.w1[:, :], T.td[:, :].indirect(T.xu[:, 64:96]), T.vr[:, :], OP.mult)
     kc = table("c", T.tc, ((3, (1, 2), "s"), (7, (3, 4), "s")))
-    vcopy(["ef1"], ["eu1"], T.eu1[:, :], T.ef1[:, :])
+    listed("1")
     tt(kc + ["xu", "w1"], ["w2"], T.w2[:, :], T.tc[:, :].indirect(T.xu[:, 32:64]), T.w1[:, :], OP.mult)
     kb = table("b", T.tb, ((0, (1, 2), "s"), (1, (3, 4), "s")))
     dma("y", "xal", ["q2"], ["xal"], T.xal[:, :], T.q2[1::16, :])
     dma("y", "xbl", ["q2"], ["xbl"], T.xbl[:, 0:32], T.q2[2::16, :])
-    blank(2, "y")
-    blank(3, "y")
     for k in range(8):
-        dma("y", "fas", [], ["fra"], T.fra[16 * k:16 * k + 16, :], T.fa[:, :])
+        dma("y", "inv", ["W4", "W4s"], ["win"], T.win[16 * k:16 * k + 8, :], T.W4[0::16, :])
+    for u in range(4):
+        dma("y", "fas", ["g0%d" % u], ["fas"], T.fas[32 * u:32 * u + 32, :], T.g0[96:128, 256 * u:256 * u + 256])
+    dma("y", "fil2", ["fl1"], ["W2"], T.W2[0::16, 0:2048], T.fl1[:, :])
     tt(kb + ["xu", "w2"], ["pr1"], T.pr1[:, :], T.tb[:, :].indirect(T.xu[:, 0:32]), T.w2[:, :], OP.mult)
+    scopy(["win", "lnt"], ["cf"], T.cf[:, :], T.win[:, :].indirect(T.lnt[:, :]))
+    for k in range(8):
+        dma("y", "ef4", ["cf"], ["ef4"], T.ef4[:, 16 * k:16 * k + 16], T.cf[16 * k:16 * k + 8, :])
 
-    def sums_out(x, keys, src, lst, G, r, lp, calls, sem, own, mid=None):
+    def sums_out(x, keys, src, lst, G, r, lp, calls, sem, cols, home):
         def pick(q, h):
             c = 256 * q + 128 * h
             copy("vs"[h], keys, ["%sG%d" % (x, c)], G[:, c:c + 128], src.indirect(lst[:, c // 16:c // 16 + 8]))
 
         def add(q, b, c):
             for h in range(2):
-                mm(["%sG%d" % (x, 256 * q + 128 * h), "d16"], ["ps%d" % b], bank(b)[:, c + h:c + 32:2],
+                mm(["%sG%d" % (x, 256 * q + 128 * h), "d16"], ["ps%d" % b], bank(b)[:, cols(c, h)],
                    G[:, 256 * q + 128 * h:256 * q + 128 * h + 128], T.d16[:, 0:16])
-        order = [[cores.index(d) for d, _ in call] for call in calls[core]] + [[me]]
+        steps = list(enumerate(calls[core]))
+        steps.insert(home, (None, [(core, [])]))
+        order = [[cores.index(d) for d, _ in call] for _, call in steps] + [[]]
         for q in order[0]:
             pick(q, 0)
             pick(q, 1)
         pos = 0
-        for k, call in enumerate(calls[core]):
+        for i, (k, call) in enumerate(steps):
             n = 32 * len(call)
-            for j, q in enumerate(order[k]):
-                add(q, k, 32 * j)
-            for h in range(2):
-                pick(order[k + 1][0], h)
-            copy("vs"[k % 2], ["ps%d" % k], ["%sr%d" % (x, k)], r[:, pos:pos + n], bank(k)[:, 0:n])
-            for q in order[k + 1][1:]:
+            for j, q in enumerate(order[i]):
+                add(q, i, 32 * j)
+            for q in order[i + 1][:AHEAD]:
                 pick(q, 0)
                 pick(q, 1)
-            before("g", ["%sr%d" % (x, k)], [])
-            g.remote_dma_fused([transfer(r[:, pos + 32 * j:pos + 32 * j + 32], lp[:, 32 * me:32 * me + 32], d, es, sem(core, d, k))
-                                for j, (d, es) in enumerate(call)], local_sem=T.sem["loc" + x])
-            pos += n
-        own()
-        cnt["loc" + x] = sum(len(es) for call in calls[core] for _, es in call)
-        got = {}
-        for c in cores:
-            for k, call in enumerate(calls[c]):
-                for d, es in call:
-                    if d == core:
-                        s = sem(c, d, k)
-                        cnt[s] = cnt.get(s, 0) + len(es)
-                        got.setdefault(s, []).append(cores.index(c))
-        for s in got:
-            after("remote", (s, None), [], ["land" + s])
-        return add, got
-
-    late = {c: sum_calls(c, cores, topo, True) for c in cores}
-    early = {c: sum_calls(c, cores, topo, False) for c in cores}
+            if k is None:
+                copy("vs"[i % 2], ["ps%d" % i], [x + "me"], lp[:, 32 * me:32 * me + 32], bank(i)[:, 0:32])
+            else:
+                copy("vs"[i % 2], ["ps%d" % i], ["%sr%d" % (x, k)], r[:, pos:pos + n], bank(i)[:, 0:n])
+            for q in order[i + 1][AHEAD:]:
+                pick(q, 0)
+                pick(q, 1)
+            if k is not None:
+                send(x, call, k, ["%sr%d" % (x, k)], lambda j, q: r[:, pos + 32 * j:pos + 32 * j + 32], lp[:, 32 * me:32 * me + 32], sem)
+                pos += n
+        return arrivals(calls, sem)
 
     def slot_sums(x, n, m, pr, sg, G, r, lp):
         run("v", V.tensor_tensor_scan, ["m" + n, {"1": "ma0", "2": "mb0"}[n], "pr" + n], ["sg" + n], sg[:, 0:512], m[:, 0:512], pr[:, :], 0.0, OP.mult, OP.add)
-        add, _ = sums_out(x, ["sg" + n, "sg" + n + "0", "eu" + n], sg[:, :], T["eu" + n], G, r, lp, late, lambda c, d, k: "arr" + x, lambda: None)
-        add(me, 4, 0)
-        vcopy(["ps4"], [x + "me"], lp[:, 32 * me:32 * me + 32], bank(4)[:, 0:32])
+        sums_out(x, ["sg" + n, "sg" + n + "0", "eu" + n], sg[:, :], T["eu" + n], G, r, lp, late, lambda c, d, k: "arr" + x,
+                 lambda c, h: slice(c + h, c + 32, 2), len(LATE[0]))
 
-    def sums_in(x, lp, lq, qs):
+    def sums_in(x, lp, out):
         for h in range(2):
-            mm(["landarr" + x, x + "me", "i2f"], ["ps%d" % (5 + h)], bank(5 + h)[:, 0:128], lp[:, h::2], T.i2f[:, :])
-            copy(qs[h], ["ps%d" % (5 + h)], ["%st%d" % (x, h)], lq[:, 128 * h:128 * h + 128], bank(5 + h)[:, 0:128])
+            mm(["landarr" + x, x + "me", "i2f"], ["ps%d" % (5 + h)], bank(5 + h)[:, 0:128], lp[:, h::2], T.i2f[:, 0:128])
+            out(h, "ps%d" % (5 + h), "%st%d" % (x, h), slice(128 * h, 128 * h + 128), bank(5 + h)[:, 0:128])
 
     def columns(x, keys, z, h, b):
         for j in range(8):
@@ -393,79 +421,70 @@ def rank_program(g, core, T, topo):
     def store(x, h, b, b2, q, u, y3, y, sem, dq):
         c = slice(128 * h, 128 * h + 128)
         copy(q, ["ps%d" % b], ["%su%d" % (x, h)], u[:, c], bank(b)[:, 0:128])
-        mm(["%su%d" % (x, h), "i2f"], ["ps%d" % b2], bank(b2)[:, 0:128], u[:, c], T.i2f[:, :])
+        mm(["%su%d" % (x, h), "i2f"], ["ps%d" % b2], bank(b2)[:, 0:128], u[:, c], T.i2f[:, 0:128])
         copy(q, ["ps%d" % b2], ["%sy%d" % (x, h)], y3[:, c], bank(b2)[:, 0:128])
         dma(dq, sem, ["%sy%d" % (x, h)], [], y[:, 1024 * h:1024 * h + 1024], y3[:, c])
 
     slot_sums("p1", "1", T.ma, T.pr1, T.sg1, T.G1, T.r1, T.lp1)
 
     following(["xbl", "xbl1"], T.xbl, 7)
-    scopy(["fra", "lnu"], ["fas"], T.fas[:, :], T.fra[:, :].indirect(T.lnu[:, :]))
     scopy(["w2", "obu"], ["wp"], T.wp[:, :], T.w2[:, :].indirect(T.obu[:, :]))
-    ts(["ki", "pif"], ["pu"], T.pu[:, :], T.ki[:, 0:16:2], T.col[:, 6:7], OP.add)
-    vcopy(["xtl"], ["laf"], T.xf[:, 72:88], T.xt[:, 32:48])
     vcopy(["xbl"], ["bi"], T.bi[:, :], T.xbl[:, 0:32])
-    tt(["laf", "pu", "gf"], ["ly"], T.ly[:, :], T.xf[:, 72:88].indirect(T.pu[:, :]), T.gf[:, :], OP.mult)
-    mm(["d16", "ly"], ["ps3"], bank(3)[:, 0:128], T.d16[:, :], T.ly[:, :])
+    vcopy(["xal"], ["ai"], T.ai[:, :], T.xal[:, :])
     turned("bi", T.bi[:, :], T.bq[:, :], T.bs[:, :], T.bc[:, :], "bc", 128)
-    vcopy(["ps3"], ["lru"], T.lru[:, :], bank(3)[:, 0:128])
-    ends("2", ["xbl", "xbl1"], T.xbl, 7, "bc", T.bc[:, :], T.mb)
-    ts(["ki", "pif"], ["ru"], T.ru[:, :], T.ki[:, :], T.col[:, 6:7], OP.add)
-    invert("2", T.su2, 0, 16)
+    vcopy(["ef4"], ["eu4"], T.eu4[:, :], T.ef4[:, :])
+    ends("2", ["xbl", "xbl1"], T.xbl, 7, "bc", T.bc[:, :])
+    same("2", T.mb)
+    a = [T.aw[:, 32 * k:32 * k + 32] for k in range(10)]
+    ts(["ai"], ["a1"], a[1], T.ai[:, :], 4, OP.logical_shift_right, 6, OP.bitwise_and)
+    ts(["ai"], ["a2"], a[2], T.ai[:, :], 7, OP.logical_shift_right, 1, OP.bitwise_and)
+    ts(["ai"], ["a3"], a[3], T.ai[:, :], 0x61F, OP.bitwise_and)
+    ts(["ai"], ["a4"], a[4], T.ai[:, :], 3, OP.logical_shift_right, 32, OP.bitwise_and)
+    tt(["a1", "a2"], ["a5"], a[5], a[1], a[2], OP.add)
+    tt(["a3", "a4"], ["a6"], a[6], a[3], a[4], OP.add)
+    ts(["a5", "rc4"], ["a7"], a[7], a[5], 64.0, OP.mult, T.col[:, 8:9], OP.add)
 
-    sums_in("p1", T.lp1, T.lq1, "ss")
-    for h in range(2):
-        tt(["p1t%d" % h, "fas", "lnu", "Z1"] + ["Z1s0"] * h, ["Z1s%d" % h], T.Z1[:, :].indirect(T.lnu[:, 8 * h:8 * h + 8]),
-           T.lq1[:, 128 * h:128 * h + 128], T.fas[:, 128 * h:128 * h + 128], OP.mult)
+    sums_in("p1", T.lp1, lambda h, b, key, c, ps: tt([b, "fas"], [key], T.lq1[:, c], ps, T.fas[:, c], OP.mult))
+    got = sums_out("a", ["p1t0", "p1t1", "lq10", "eu4"], T.lq1[:, :], T.eu4, T.G2, T.ra, T.lpa, early, by_call("a"),
+                   lambda c, h: slice(c + 16 * h, c + 16 * h + 16), 1)
+    invert("s", "2", T.su2, 0, 32)
+    relist("2", "s")
+    ts(["a7"], ["a8"], a[8], a[7], 448, OP.bitwise_and)
+    tt(["a6", "a8"], ["a9"], a[9], a[6], a[8], OP.add)
+    vcopy(["a9"], ["au"], T.au[:, :], a[9])
+
+    ka = []
+    for i, s in enumerate(sorted(got)):
+        c, n = 512 * (got[s][0] // 2), BY_PE[i]
+        run("v", V.transpose, ["land" + s, "ame"], ["ta%d" % c], T.ta[:, c:c + 64], T.lpa[:, c // 8:c // 8 + 64])
+        for d in range(n + 1, 8):
+            dma("y", "rota%d" % i, ["ta%d" % c], ["tad%d" % c], T.ta[0:128 - 16 * d, c + 64 * d:c + 64 * d + 64], T.ta[16 * d:128, c:c + 64])
+            dma("y", "rota%d" % i, ["ta%d" % c], ["tad%d" % c], T.ta[128 - 16 * d:128, c + 64 * d:c + 64 * d + 64], T.ta[0:16 * d, c:c + 64])
+        parts = [(d0, d1) for d0, d1 in ((1, min(n, 4) + 1), (5, n + 1)) if d1 > d0]
+        for j, (d0, d1) in enumerate(parts):
+            b = (2 * i + j) % 5
+            for d in range(d0, d1):
+                mm(["ta%d" % c, "i2f"], ["ps%d" % b], bank(b)[:, 64 * (d - d0):64 * (d - d0) + 64], T.i2f[:, 16 * d:16 * d + 128], T.ta[:, c:c + 64])
+        if i in (1, 2):
+            h = i - 1
+            vcopy(["p1t%d" % h, "lnu", "Z1"] + ["Z1s0"] * h, ["Z1s%d" % h], T.Z1[:, :].indirect(T.lnu[:, 8 * h:8 * h + 8]), T.lq1[:, 128 * h:128 * h + 128])
+        for j, (d0, d1) in enumerate(parts):
+            b = (2 * i + j) % 5
+            copy("sv"[j], ["ps%d" % b], ["tap%d" % (c + d0)], T.ta[:, c + 64 * d0:c + 64 * d1], bank(b)[:, 0:64 * (d1 - d0)])
+            ka.append("tap%d" % (c + d0))
+        ka += ["ta%d" % c, "tad%d" % c]
     kz = ["Z1", "Z1s0", "Z1s1"]
 
-    def own_a():
-        c = 256 * me
-        mm(["aG%d" % c, "aG%d" % (c + 128), "d16"], ["ps4"], bank(4)[:, 0:256], T.d16[:, :], T.G2[:, c:c + 256])
-
-    _, got = sums_out("a", kz + ["lru"], T.Z1[:, :], T.lru, T.G2, T.ra, T.lpa, early,
-                      lambda c, d, k: "arra%d" % (3 if topo.chip(c) == topo.chip(d) else k), own_a)
-    scopy(["ps4"], ["ta%d" % me], T.ta[:, 256 * me:256 * me + 256], bank(4)[:, 0:256])
-    invert("2", T.su2, 16, 32)
-    relist("2")
-    same("2", T.mb)
-    vcopy(["xal"], ["au"], T.au[:, :], T.xal[:, :])
-
-    landing = [(s, q) for s in ("arra3", "arra0", "arra1", "arra2") for q in got[s]]
-
-    def widen(i):
-        s, q = landing[i]
-        copy("vs"[i % 2], ["land" + s, "ru"], ["rp%d" % q], T.rp[:, 256 * q:256 * q + 256], T.lpa[:, 32 * q:32 * q + 32].indirect(T.ru[:, :]))
-
-    widen(0)
-    widen(1)
-    for i, (s, q) in enumerate(landing):
-        for h in range(2):
-            mm(["rp%d" % q, "i2f"], ["ps%d" % (i % 4)], bank(i % 4)[:, 128 * h:128 * h + 128], T.rp[:, 256 * q + h:256 * q + 256:2], T.i2f[:, :])
-        if i + 2 < len(landing):
-            widen(i + 2)
-        if i == 1:
-            turned("xtl", T.xt[:, 48:64], T.xq[:, 48:64], T.xs[:, 48:64], T.xc1[:, 48:64], "xc3", 128)
-            ts(["xc3"], ["su3"], T.lsu[:, 0:16], T.xc1[:, 48:64], 128.0, OP.mult)
-        if i == 3:
-            fill("mb0", T.mb[:, 0:1], 0.0)
-            fill("sg20", T.sg2[:, 512:520], 0.0)
-            fill("lq20", T.lq2[:, 256:264], 0.0)
-        if i == 5:
-            vcopy(["ef2"], ["eu2"], T.eu2[:, :], T.ef2[:, :])
-        copy("vs"[i % 2], ["ps%d" % (i % 4)], ["ta%d" % q], T.ta[:, 256 * q:256 * q + 256], bank(i % 4)[:, 0:256])
-
-    tt(["ta%d" % q for q in range(8)] + ["au", "wp"], ["pr2"], T.pr2[:, :], T.ta[:, :].indirect(T.au[:, :]), T.wp[:, :], OP.mult)
+    tt(ka + ["au", "wp"], ["pr2"], T.pr2[:, :], T.ta[:, :].indirect(T.au[:, :]), T.wp[:, :], OP.mult)
     columns("ya", lambda c: kz, T.Z1, 0, 5)
-    store("ya", 0, 5, 6, "s", T.ua, T.ya3, T.ya, "oya", "y")
+    listed("2")
     slot_sums("p2", "2", T.mb, T.pr2, T.sg2, T.G1, T.r2, T.lp2)
     columns("ya", lambda c: kz, T.Z1, 1, 7)
-    invert("3", T.lsu, 0, 16)
-    relist("3")
-    store("ya", 1, 7, 6, "s", T.ua, T.ya3, T.ya, "oya", "y")
-    vcopy(["ef3"], ["eu3"], T.eu3[:, :], T.ef3[:, :])
+    store("ya", 0, 5, 6, "s", T.ua, T.ya3, T.ya, "oya", "y")
+    store("ya", 1, 7, 4, "v", T.ua, T.ya3, T.ya, "oya", "y")
+    listed("3")
 
-    sums_in("p2", T.lp2, T.lq2, "vs")
+    sums_in("p2", T.lp2, lambda h, b, key, c, ps: copy("vs"[h], [b], [key], T.lq2[:, c], ps))
     for h in range(2):
         for j in range(8):
             c = 1024 * h + 128 * j

@@ -18,7 +18,7 @@ SCRATCH = {
     "pc": sb(8, I), "dj": sb(16, I), "jt": sb(32, I), "pi": sb(8, I), "pg": sb(8, I), "col": sb(16),
     "di": sb(16, I), "d16": sb(16), "one": sb(256), "i2f": sb(256), "i2b": sb(256, B),
     "sh0": sb(128), "gf0": sb(128), "sh1": sb(128), "sh2": sb(128), "b8": sb(128), "gf": sb(128), "jf": sb(32), "pos": sb(512), "pos0": sb(256),
-    "kt": sb(32, I), "pu": sb(8, U), "tu": sb(32, U), "mw": sb(8), "fl1": sb(128), "fl3": sb(128, B),
+    "kt": sb(32, I), "pu": sb(8, U), "tu": sb(32, U), "mw": sb(8), "fl1": sb(128), "fl3": sb(128, B), "fra": sb(2048, B),
     "W4": sb(2048, B), "cf": sb(256), "ef4": sb(128), "eu4": sb(128, U), "lnt": sb(16, U),
     "ai": sb(32, I), "aw": sb(320, I),
     "xf": sb(104), "xq": sb(64, I), "xs": sb(64), "xc1": sb(64), "lsu": sb(32, U), "lnu": sb(16, U),
@@ -26,7 +26,7 @@ SCRATCH = {
     "ma": sb(520), "mb": sb(520), "W1": sb(2688), "W2": sb(2688), "W3": sb(2048),
     "ef1": sb(128), "ef2": sb(128), "ef3": sb(128), "eu1": sb(128, U), "eu2": sb(128, U), "eu3": sb(128, U),
     "ly": sb(128),
-    "oq": sb(32, I), "os1": sb(32), "oc": sb(32), "otu": sb(32, U), "wx": sb(512), "q1": sb(512), "q2": sb(512),
+    "oq": sb(32, I), "os1": sb(32), "oc": sb(32), "otu": sb(32, U), "wx": sb(512, I), "q1": sb(512), "q2": sb(512),
     "xal": sb(32), "xbl": sb(40), "au": sb(32, U), "bi": sb(32, I), "bq": sb(32, I), "bs": sb(32), "bc": sb(32),
     "td": sb(2048, B), "tc": sb(2048, B), "tb": sb(2048, B), "ta": sb(2048),
     "w1": sb(512), "w2": sb(512), "wp": sb(512), "pr1": sb(512), "pr2": sb(512), "sg1": sb(520), "sg2": sb(520),
@@ -39,12 +39,14 @@ SCRATCH = {
 SEMAPHORES = (["c_g", "c_v", "c_s", "c_p", "ldw", "ldl", "ldx", "ldn", "ldo", "ldv", "ldy", "ldz", "fas", "fil1", "fil2", "fil3",
                "ef1", "ef2", "ef3", "wx", "xal", "xbl", "oya", "oyb", "arrp1", "arrp2", "fil4", "ef4", "inv",
                "rota0", "rota1", "rota2", "rota3"]
-              + [k + x for x in "dcb" for k in ("snd", "self", "arr", "loc", "cmp", "rot")]
+              + [k + x for x in "dcb" for k in ("self", "arr", "loc", "cmp", "rot")] + ["snd" + x + h for x in "dcb" for h in "01"]
               + ["loc" + x for x in ("p1", "a", "p2")] + ["arra%d" % k for k in range(7)])
-LATE, EARLY = ((2, 2, 1, 1), 2), ((2, 2, 2), 0)
-AHEAD = 2
+LATE, EARLY = ((1, 2, 2, 1), 3), ((1, 1, 2, 2), 1)
+AHEAD = (2, 2)
+YA = 4
 LIFT = 32
-BY_PE = (2, 4, 4, 7)
+HALF = ("vyy", "vyy", "sss", "vvs")
+SPREAD = (-1, 3)
 
 
 def long_call(src, cores, topo):
@@ -194,47 +196,54 @@ def rank_program(g, core, T, topo):
 
     factor(0, T.fd)
     factor(1, T.fc)
-    factor(2, T.fb)
-    for f, l in enumerate((T.ld, T.lc, T.lb, T.la)):
+    for f, l in enumerate((T.ld, T.lc, T.lb)):
         for u in range(4):
             dma("ys"[u % 2], "ldl", [], ["lt"], T.lt[32 * f:32 * f + 32, 16 * u:16 * u + 16], l[32 * u:32 * u + 32, :])
-    factor(3, T.fa)
+    factor(2, T.fb)
+    fill("win0", T.win[96:128, 0:16], 0.0)
+    fill("lt0", T.lt[96:128, :], 0)
     dma("y", "ldx", [], ["xta"], T.xt[:, 0:32], T.xa[:, :])
-    dma("s", "ldy", [], ["xtb"], T.xt[:, 64:96], T.xb[:, :])
+    dma("s", "ldo", [], ["obt"], T.obt[:, :], T.ob[:, :])
 
     fill("one", T.one[:, :], 1.0)
-    iota("pos", T.pos, [[1, 512]], LIFT, 0)
     iota("pc", T.pc, [[0, 8]], 0, 1)
+    iota("kt", T.kt, [[1, 16], [256, 2]], 0, 0)
+    iota("dj", T.dj, [[1, 16]], 128, -1)
     iota("jt", T.jt, [[16, 32]], 2048, 1)
     select("sh0", T.sh0, T.one, "one", [[-1, 128]], OP.is_equal, -1, 1)
     select("sh2", T.sh2, T.one, "one", [[-16, 8], [256, 16]], OP.is_equal, -256 * 15, 1)
     select("sh1", T.sh1, T.sh0, "sh0", [[0, 8], [1, 16]], OP.not_equal, -15, 0)
+    iota("pos", T.pos, [[1, 512]], LIFT, 0)
     select("b8", T.b8, T.one, "one", [[-1, 8], [0, 16]], OP.is_equal, 0, 1)
-    iota("kt", T.kt, [[1, 16], [256, 2]], 0, 0)
+    iota("pos0", T.pos0, [[1, 256]], 0, 0)
     fill("fl1", T.fl1[:, :], 512.0 + LIFT)
+    fill("wx", T.wx[:, :], 0)
     fill("fl3", T.fl3[:, :], 256.0)
     fill("xf", T.xf[:, 32:33], -1.0)
     fill("mw", T.mw[:, 0:1], 0.0)
     fill("mw", T.mw[:, 1:8], 1.0)
-    fill("wx", T.wx[:, :], 0.0)
-    fill("lq20", T.lq2[:, 256:520], 0.0)
     ts(["pc"], ["pi"], T.pi[:, 0:1], T.pc[:, 0:1], 15, OP.bitwise_and)
     ts(["pc"], ["pg"], T.pg[:, 0:1], T.pc[:, 0:1], 4, OP.logical_shift_right)
+    ts(["dj"], ["di"], T.di[:, :], T.dj[:, 0:16], 15, OP.bitwise_and)
     ts(["jt"], ["jf"], T.jf[:, :], T.jt[:, :], 1.0 / 128, OP.mult)
-    ts(["pg"], ["rc"], T.col[:, 5:6], T.pg[:, 0:1], -256.0, OP.mult, 2048.0, OP.add)
-    ts(["pg"], ["rc4"], T.col[:, 8:9], T.pg[:, 0:1], -64.0, OP.mult, 512.0, OP.add)
     ts(["pi"], ["p16"], T.col[:, 7:8], T.pi[:, 0:1], 16.0, OP.mult)
     vcopy(["pi"], ["pif"], T.col[:, 6:7], T.pi[:, 0:1])
+    ts(["pg"], ["rc"], T.col[:, 5:6], T.pg[:, 0:1], -256.0, OP.mult, 2048.0, OP.add)
+    ts(["pg"], ["rc4"], T.col[:, 8:9], T.pg[:, 0:1], -64.0, OP.mult, 512.0, OP.add)
+    ts(["di"], ["d16"], T.d16[:, :], T.di[:, :], 0.0, OP.is_equal)
+    ts(["kt", "p16"], ["tu"], T.tu[:, :], T.kt[:, :], T.col[:, 7:8], OP.add)
+    ts(["one", "pif"], ["pu"], T.pu[:, :], T.one[:, 0:8], T.col[:, 6:7], OP.mult)
     for key, ap in (("ma0", T.ma[:, 0:1]), ("mb0", T.mb[:, 0:1]), ("sg10", T.sg1[:, 512:520]), ("sg20", T.sg2[:, 512:520]), ("lq10", T.lq1[:, 256:264])):
         fill(key, ap, 0.0)
     fill("xbl1", T.xbl[:, 32:33], -1.0)
     vcopy(["lt", "lt0"], ["lu"], T.lu[:, :], T.lt[:, :])
 
-    dma("y", "fil1", ["fl1"], ["W1"], T.W1[0::16, 0:2048], T.fl1[:, :])
     dma("y", "ldz", [], ["xtl"], T.xt[:, 32:48], T.la[:, :])
     dma("y", "ldz", [], ["xtl"], T.xt[:, 48:64], T.lb[:, :])
-    dma("y", "ldo", [], ["obt"], T.obt[:, :], T.ob[:, :])
+    dma("y", "fil1", ["fl1"], ["W1"], T.W1[0::16, 0:2048], T.fl1[:, :])
     dma("y", "ldv", [], ["vin"], T.vin[0:8, :], T.v[:, :])
+    dma("y", "wx", [], ["wx"], T.wx[1::16, :], T.xa[:, :])
+    dma("y", "wx", [], ["wx"], T.wx[2::16, :], T.xb[:, :])
 
     for u in range(4):
         copy("vs"[u % 2], ["win", "win0", "lu"], ["g0%d" % u], T.g0[:, 256 * u:256 * u + 256], T.win[:, :].indirect(T.lu[:, 16 * u:16 * u + 16]))
@@ -244,7 +253,8 @@ def rank_program(g, core, T, topo):
     def stage(x, f, q):
         snd, land = T["snd" + x], T["land" + x]
         for u in range(4):
-            dma(q, "snd" + x, ["g0%d" % u], ["snd" + x], snd[256 * u:256 * u + 256, :], T.g0[32 * f:32 * f + 32, 256 * u:256 * u + 256])
+            k = "snd%s%d" % (x, u // 2)
+            dma(q, k, ["g0%d" % u], [k], snd[256 * u:256 * u + 256, :], T.g0[32 * f:32 * f + 32, 256 * u:256 * u + 256])
         p, u = 32 * f + 16 * (me % 2), me // 2
         dma(q, "self" + x, ["g0%d" % u], ["landarr" + x], land[128 * me:128 * me + 128, :], T.g0[p:p + 16, 256 * u:256 * u + 256])
 
@@ -252,11 +262,10 @@ def rank_program(g, core, T, topo):
     stage("c", 1, "s")
     stage("b", 2, "y")
     for x in "dcb":
-        send(x, wide[core][0], 0, ["snd" + x], lambda j, r: T["snd" + x][128 * r:128 * r + 128, :], T["land" + x][128 * me:128 * me + 128, :],
-             lambda c, d, k: "arr" + x)
+        for halves in ([0], [1]) if x == "d" else ([0, 1],):
+            send(x, [(d, es) for d, es in wide[core][0] if cores.index(d) // 4 in halves], 0, ["snd%s%d" % (x, h) for h in halves],
+                 lambda j, r: T["snd" + x][128 * r:128 * r + 128, :], T["land" + x][128 * me:128 * me + 128, :], lambda c, d, k: "arr" + x)
         arrivals(wide, lambda c, d, k: "arr" + x)
-    iota("pos0", T.pos0, [[1, 256]], 0, 0)
-    iota("dj", T.dj, [[1, 16]], 128, -1)
     select("gf0", T.gf0, T.one, "one", [[-16, 8], [0, 16]], OP.is_ge, 0, 1)
     run("g", g.affine_select, ["one"], ["i2b"], T.i2b[:, :], T.one[:, :], [[0, 2], [-1, 128]], OP.is_equal, 0.0, 0, 1)
     select("gf", T.gf, T.gf0, "gf0", [[16, 8], [0, 16]], OP.is_ge, 15, -1)
@@ -268,17 +277,22 @@ def rank_program(g, core, T, topo):
         mm(xkey + ["sh1"], [k], bank(b)[:, 0:32], T.sh1[:, :], x[:, 0:32], True, False)
         mm(xkey + ["sh2"], [k], bank(b)[:, 0:32], T.sh2[:, :], x[:, 1:33], False, True)
 
-    def turned(key, x, xq, xs, xc, out, m, more=()):
-        ts([key, *more], [out + "q"], xq, x, 4, OP.logical_shift_right)
-        ts([out + "q"], [out + "s"], xs, xq, 1.0 / m - 16, OP.mult)
-        tt([key, out + "s"], [out], xc, x, xs, OP.add)
+    def turned(*lists):
+        for key, x, xq, xs, xc, out, m, more in lists:
+            ts([key] + more, [out + "q"], xq, x, 4, OP.logical_shift_right)
+        for key, x, xq, xs, xc, out, m, more in lists:
+            ts([out + "q"], [out + "s"], xs, xq, 1.0 / m - 16, OP.mult)
+        for key, x, xq, xs, xc, out, m, more in lists:
+            tt([key, out + "s"], [out], xc, x, xs, OP.add)
 
-    def ends(n, xkey, x, b, ckey, c):
+    def ends(n, xkey, x, b, ckey, c, between):
         eq, equ, su = T["eq" + n], T["equ" + n], T["su" + n]
         tt(xkey + ["ps%d" % b], ["eq" + n], eq[:, :], x[:, 0:32], bank(b)[:, 0:32], OP.is_equal)
+        between[0]()
         tt(["eq" + n, "jf"], ["dm"], T.dm[:, :], eq[:, :], T.jf[:, :], OP.mult)
         vcopy(["eq" + n], ["equ" + n], equ[:, :], eq[:, :])
         tt(["dm", ckey], ["of"], T.of[:, :], T.dm[:, :], c, OP.max)
+        between[1]()
         ts(["of"], ["su" + n], su[:, :], T.of[:, :], 128.0, OP.mult)
 
     def invert(q, n, su, c0, c1):
@@ -294,50 +308,42 @@ def rank_program(g, core, T, topo):
     def listed(n):
         ts(["ef" + n], ["eu" + n], T["eu" + n][:, :], T["ef" + n][:, :], 0.25 - LIFT, OP.add)
 
-    def same(n, m):
-        scopy(["mw", "equ" + n], ["m" + n], m[:, 1:513], T.mw[:, :].indirect(T["equ" + n][:, :]))
+    def same(q, n, m):
+        copy(q, ["mw", "equ" + n], ["m" + n], m[:, 1:513], T.mw[:, :].indirect(T["equ" + n][:, :]))
 
-    vcopy(["xta"], ["xf"], T.xf[:, 0:32], T.xt[:, 0:32])
-    vcopy(["xtb"], ["xfb"], T.xf[:, 40:72], T.xt[:, 64:96])
-    dma("s", "wx", ["xf"], ["wx"], T.wx[1::16, :], T.xf[:, 0:32])
-    dma("s", "wx", ["xfb"], ["wx"], T.wx[2::16, :], T.xf[:, 40:72])
-    dma("y", "fil3", ["fl1"], ["W3"], T.W3[0::16, 0:2048], T.fl1[:, :])
+    dma("s", "fil4", ["fl3"], ["W4"], T.W4[0::16, :], T.fl3[:, :])
+    dma("y", "ldn", [], ["xtc"], T.xt[:, 64:96], T.xb[:, :])
     dma("y", "ldn", [], ["xtc"], T.xt[:, 96:128], T.xc[:, :])
     dma("y", "ldn", [], ["xtc"], T.xt[:, 128:160], T.xd[:, :])
-    dma("y", "fil4", ["fl3"], ["W4"], T.W4[0::16, :], T.fl3[:, :])
+    vcopy(["xta"], ["xf"], T.xf[:, 0:32], T.xt[:, 0:32])
     following(["xf"], T.xf, 7)
     mm(["b8", "vin"], ["ps6"], bank(6)[:, :], T.b8[0:8, :], T.vin[0:8, :])
-    turned("xta", T.xt[:, 0:64], T.xq[:, :], T.xs[:, :], T.xc1[:, :], "xc1", 128, ["xtl"])
-    ends("1", ["xf"], T.xf, 7, "xc1", T.xc1[:, 0:32])
-    ts(["xc1"], ["su3"], T.lsu[:, 0:16], T.xc1[:, 48:64], 128.0, OP.mult)
-    invert("v", "1", T.su1, 0, 32)
-    relist("1")
-    same("1", T.ma)
+    turned(("xta", T.xt[:, 0:64], T.xq[:, :], T.xs[:, :], T.xc1[:, :], "xc1", 128, ["xtl"]),
+           ("obt", T.obt[:, :], T.oq[:, :], T.os1[:, :], T.oc[:, :], "oc", 32, []))
+    ends("1", ["xf"], T.xf, 7, "xc1", T.xc1[:, 0:32], [
+        lambda: ts(["oc"], ["otu"], T.otu[:, :], T.oc[:, :], 32.0, OP.mult),
+        lambda: vcopy(["xtl"], ["lnu"], T.lnu[:, :], T.xt[:, 32:48])])
+    invert("s", "1", T.su1, 0, 32)
     scopy(["ps6"], ["vr"], T.vr[:, :], bank(6)[:, :])
-    invert("s", "3", T.lsu, 0, 16)
-    relist("3", "s")
-    turned("obt", T.obt[:, :], T.oq[:, :], T.os1[:, :], T.oc[:, :], "oc", 32)
-    ts(["oc"], ["otu"], T.otu[:, :], T.oc[:, :], 32.0, OP.mult)
-    ts(["kt", "p16"], ["tu"], T.tu[:, :], T.kt[:, :], T.col[:, 7:8], OP.add)
-    scopy(["wx", "otu"], ["q1"], T.q1[:, :], T.wx[:, :].indirect(T.otu[:, :]))
-    scopy(["q1", "tu"], ["q2"], T.q2[:, :], T.q1[:, :].indirect(T.tu[:, :]))
-    ts(["xtb", "xtc", "rc"], ["xr"], T.xr[:, :], T.xt[:, 64:160], T.col[:, 5:6], OP.add)
-    vcopy(["xtl"], ["lnu"], T.lnu[:, :], T.xt[:, 32:48])
-    ts(["xr"], ["xo"], T.xo[:, :], T.xr[:, :], 2047, OP.bitwise_and)
-    ts(["dj"], ["di"], T.di[:, :], T.dj[:, 0:16], 15, OP.bitwise_and)
-    vcopy(["xo"], ["xu"], T.xu[:, :], T.xo[:, :])
-    ts(["di"], ["d16"], T.d16[:, :], T.di[:, :], 0.0, OP.is_equal)
-    vcopy(["pos0", "lnu", "W4"], ["W4s"], T.W4[:, :].indirect(T.lnu[:, :]), T.pos0[:, :])
-    ts(["one", "pif"], ["pu"], T.pu[:, :], T.one[:, 0:8], T.col[:, 6:7], OP.mult)
     vcopy(["xtl"], ["laf"], T.xf[:, 72:88], T.xt[:, 32:48])
-    vcopy(["obt"], ["obu"], T.obu[:, :], T.obt[:, :])
+    vcopy(["wx", "otu"], ["q1"], T.q1[:, :], T.wx[:, :].indirect(T.otu[:, :]))
+    vcopy(["pos0", "lnu", "W4"], ["W4s"], T.W4[:, :].indirect(T.lnu[:, :]), T.pos0[:, :])
+    dma("y", "fil2", ["fl1", "W4s"], ["W2"], T.W2[0::16, 0:2048], T.fl1[:, :])
+    dma("y", "fil3", ["fl1"], ["W3"], T.W3[0::16, 0:2048], T.fl1[:, :])
+    ts(["xtc", "rc"], ["xr"], T.xr[:, :], T.xt[:, 64:160], T.col[:, 5:6], OP.add)
+    ts(["xc1"], ["su3"], T.lsu[:, 0:16], T.xc1[:, 48:64], 128.0, OP.mult)
+    ts(["xr"], ["xo"], T.xo[:, :], T.xr[:, :], 2047, OP.bitwise_and)
     tt(["laf", "pu", "gf"], ["ly"], T.ly[:, :], T.xf[:, 72:88].indirect(T.pu[:, :]), T.gf[:, :], OP.mult)
     mm(["d16", "ly"], ["ps5"], bank(5)[:, 0:16], T.ly[:, :], T.d16[:, :])
+    vcopy(["xo"], ["xu"], T.xu[:, :], T.xo[:, :])
+    vcopy(["obt"], ["obu"], T.obu[:, :], T.obt[:, :])
     vcopy(["ps5"], ["lnt"], T.lnt[:, :], bank(5)[:, 0:16])
+    same("v", "1", T.ma)
 
-    def table(x, t, groups):
+    def table(x, t, first, groups):
         land, key, w = T["land" + x], "landarr" + x, 256
-        dma("y", "cmp" + x, [key], [x + "0"], t[:, 0:w], land[:, :])
+        for z in first:
+            dma("y", "cmp" + z, ["landarr" + z], [z + "0"], T["t" + z][:, 0:w], T["land" + z][:, :])
         byp = [d for _, ds, _ in groups for d in ds]
         for d in range(1, 8):
             if d not in byp:
@@ -350,23 +356,24 @@ def rank_program(g, core, T, topo):
             copy(q, ["ps%d" % b], ["%s%d" % (x, d) for d in ds], t[:, ds[0] * w:(ds[0] + n) * w], bank(b)[:, 0:n * w])
         return ["%s%d" % (x, d) for d in range(8)]
 
-    kd = table("d", T.td, ((0, (1, 2), "s"), (1, (3, 4), "v"), (2, (5,), "s")))
+    kd = table("d", T.td, "d", ((0, (1,), "s"), (1, (2,), "v"), (2, (3,), "s"), (4, (4,), "v"), (5, (5,), "s")))
     tt(kd + ["xu", "vr"], ["w1"], T.w1[:, :], T.td[:, :].indirect(T.xu[:, 64:96]), T.vr[:, :], OP.mult)
-    kc = table("c", T.tc, ((3, (1, 2), "s"), (7, (3, 4), "s")))
-    listed("1")
+    kc = table("c", T.tc, "cb", ((3, (1, 2), "s"), (7, (3,), "s")))
     tt(kc + ["xu", "w1"], ["w2"], T.w2[:, :], T.tc[:, :].indirect(T.xu[:, 32:64]), T.w1[:, :], OP.mult)
-    kb = table("b", T.tb, ((0, (1, 2), "s"), (1, (3, 4), "s")))
-    dma("y", "xal", ["q2"], ["xal"], T.xal[:, :], T.q2[1::16, :])
-    dma("y", "xbl", ["q2"], ["xbl"], T.xbl[:, 0:32], T.q2[2::16, :])
+    kb = table("b", T.tb, "", ((0, (1, 2), "s"), (1, (3, 4), "s")))
+    relist("1")
     for k in range(8):
-        dma("y", "inv", ["W4", "W4s"], ["win"], T.win[16 * k:16 * k + 8, :], T.W4[0::16, :])
-    for u in range(4):
-        dma("y", "fas", ["g0%d" % u], ["fas"], T.fas[32 * u:32 * u + 32, :], T.g0[96:128, 256 * u:256 * u + 256])
-    dma("y", "fil2", ["fl1"], ["W2"], T.W2[0::16, 0:2048], T.fl1[:, :])
+        dma("y", "inv", ["W4", "W4s"], kd + ["wi"], T.td[16 * k:16 * k + 8, :], T.W4[0::16, :])
+    for k in range(8):
+        dma("y", "fas", [], ["fra"], T.fra[16 * k:16 * k + 16, :], T.fa[:, :])
     tt(kb + ["xu", "w2"], ["pr1"], T.pr1[:, :], T.tb[:, :].indirect(T.xu[:, 0:32]), T.w2[:, :], OP.mult)
-    scopy(["win", "lnt"], ["cf"], T.cf[:, :], T.win[:, :].indirect(T.lnt[:, :]))
+    listed("1")
+    scopy(["q1", "tu"], ["q2"], T.q2[:, :], T.q1[:, :].indirect(T.tu[:, :]))
+    scopy(["wi", "lnt"], ["cf"], T.cf[:, :], T.td[:, :].indirect(T.lnt[:, :]))
     for k in range(8):
         dma("y", "ef4", ["cf"], ["ef4"], T.ef4[:, 16 * k:16 * k + 16], T.cf[16 * k:16 * k + 8, :])
+    dma("y", "xbl", ["q2"], ["xbl"], T.xbl[:, 0:32], T.q2[2::16, :])
+    dma("y", "xal", ["q2"], ["xal"], T.xal[:, :], T.q2[1::16, :])
 
     def sums_out(x, keys, src, lst, G, r, lp, calls, sem, cols, home):
         def pick(q, h):
@@ -379,28 +386,27 @@ def rank_program(g, core, T, topo):
                    G[:, 256 * q + 128 * h:256 * q + 128 * h + 128], T.d16[:, 0:16])
         steps = list(enumerate(calls[core]))
         steps.insert(home, (None, [(core, [])]))
-        order = [[cores.index(d) for d, _ in call] for _, call in steps] + [[]]
-        for q in order[0]:
-            pick(q, 0)
-            pick(q, 1)
-        pos = 0
+        order = [cores.index(d) for _, call in steps for d, _ in call]
+        picked = done = pos = 0
         for i, (k, call) in enumerate(steps):
-            n = 32 * len(call)
-            for j, q in enumerate(order[i]):
-                add(q, i, 32 * j)
-            for q in order[i + 1][:AHEAD]:
+            n, b = len(call), i % 5
+            for q in order[picked:done + n]:
                 pick(q, 0)
                 pick(q, 1)
+            picked = max(picked, done + n)
+            for j, q in enumerate(order[done:done + n]):
+                add(q, b, 32 * j)
+            done += n
+            for q in order[picked:done + AHEAD[min(i, 1)]]:
+                pick(q, 0)
+                pick(q, 1)
+            picked = max(picked, done + AHEAD[min(i, 1)])
             if k is None:
-                copy("vs"[i % 2], ["ps%d" % i], [x + "me"], lp[:, 32 * me:32 * me + 32], bank(i)[:, 0:32])
+                copy("vs"[i % 2], ["ps%d" % b], [x + "me"], lp[:, 32 * me:32 * me + 32], bank(b)[:, 0:32])
             else:
-                copy("vs"[i % 2], ["ps%d" % i], ["%sr%d" % (x, k)], r[:, pos:pos + n], bank(i)[:, 0:n])
-            for q in order[i + 1][AHEAD:]:
-                pick(q, 0)
-                pick(q, 1)
-            if k is not None:
+                copy("vs"[i % 2], ["ps%d" % b], ["%sr%d" % (x, k)], r[:, pos:pos + 32 * n], bank(b)[:, 0:32 * n])
                 send(x, call, k, ["%sr%d" % (x, k)], lambda j, q: r[:, pos + 32 * j:pos + 32 * j + 32], lp[:, 32 * me:32 * me + 32], sem)
-                pos += n
+                pos += 32 * n
         return arrivals(calls, sem)
 
     def slot_sums(x, n, m, pr, sg, G, r, lp):
@@ -413,8 +419,8 @@ def rank_program(g, core, T, topo):
             mm(["landarr" + x, x + "me", "i2f"], ["ps%d" % (5 + h)], bank(5 + h)[:, 0:128], lp[:, h::2], T.i2f[:, 0:128])
             out(h, "ps%d" % (5 + h), "%st%d" % (x, h), slice(128 * h, 128 * h + 128), bank(5 + h)[:, 0:128])
 
-    def columns(x, keys, z, h, b):
-        for j in range(8):
+    def columns(x, keys, z, h, b, j0=0, j1=8):
+        for j in range(j0, j1):
             c = 1024 * h + 128 * j
             mm(keys(c) + ["d16"], ["ps%d" % b], bank(b)[:, j:128:8], z[:, c:c + 128], T.d16[:, 0:16])
 
@@ -428,60 +434,80 @@ def rank_program(g, core, T, topo):
     slot_sums("p1", "1", T.ma, T.pr1, T.sg1, T.G1, T.r1, T.lp1)
 
     following(["xbl", "xbl1"], T.xbl, 7)
+    scopy(["fra", "lnu"], ["fas"], T.fas[:, :], T.fra[:, :].indirect(T.lnu[:, :]))
     scopy(["w2", "obu"], ["wp"], T.wp[:, :], T.w2[:, :].indirect(T.obu[:, :]))
+    a = [T.aw[:, 32 * k:32 * k + 32] for k in range(10)]
     vcopy(["xbl"], ["bi"], T.bi[:, :], T.xbl[:, 0:32])
     vcopy(["xal"], ["ai"], T.ai[:, :], T.xal[:, :])
-    turned("bi", T.bi[:, :], T.bq[:, :], T.bs[:, :], T.bc[:, :], "bc", 128)
-    vcopy(["ef4"], ["eu4"], T.eu4[:, :], T.ef4[:, :])
-    ends("2", ["xbl", "xbl1"], T.xbl, 7, "bc", T.bc[:, :])
-    same("2", T.mb)
-    a = [T.aw[:, 32 * k:32 * k + 32] for k in range(10)]
+    ts(["bi"], ["bq"], T.bq[:, :], T.bi[:, :], 4, OP.logical_shift_right)
     ts(["ai"], ["a1"], a[1], T.ai[:, :], 4, OP.logical_shift_right, 6, OP.bitwise_and)
+    ts(["bq"], ["bs"], T.bs[:, :], T.bq[:, :], 1.0 / 128 - 16, OP.mult)
     ts(["ai"], ["a2"], a[2], T.ai[:, :], 7, OP.logical_shift_right, 1, OP.bitwise_and)
-    ts(["ai"], ["a3"], a[3], T.ai[:, :], 0x61F, OP.bitwise_and)
-    ts(["ai"], ["a4"], a[4], T.ai[:, :], 3, OP.logical_shift_right, 32, OP.bitwise_and)
+    tt(["bi", "bs"], ["bc"], T.bc[:, :], T.bi[:, :], T.bs[:, :], OP.add)
+    ends("2", ["xbl", "xbl1"], T.xbl, 7, "bc", T.bc[:, :], [
+        lambda: ts(["ai"], ["a3"], a[3], T.ai[:, :], 0x61F, OP.bitwise_and),
+        lambda: ts(["ai"], ["a4"], a[4], T.ai[:, :], 3, OP.logical_shift_right, 32, OP.bitwise_and)])
+    invert("s", "2", T.su2, 0, 16)
     tt(["a1", "a2"], ["a5"], a[5], a[1], a[2], OP.add)
-    tt(["a3", "a4"], ["a6"], a[6], a[3], a[4], OP.add)
+    vcopy(["ef4"], ["eu4"], T.eu4[:, :], T.ef4[:, :])
     ts(["a5", "rc4"], ["a7"], a[7], a[5], 64.0, OP.mult, T.col[:, 8:9], OP.add)
+    tt(["a3", "a4"], ["a6"], a[6], a[3], a[4], OP.add)
+    ts(["a7"], ["a8"], a[8], a[7], 448, OP.bitwise_and)
 
     sums_in("p1", T.lp1, lambda h, b, key, c, ps: tt([b, "fas"], [key], T.lq1[:, c], ps, T.fas[:, c], OP.mult))
     got = sums_out("a", ["p1t0", "p1t1", "lq10", "eu4"], T.lq1[:, :], T.eu4, T.G2, T.ra, T.lpa, early, by_call("a"),
-                   lambda c, h: slice(c + 16 * h, c + 16 * h + 16), 1)
-    invert("s", "2", T.su2, 0, 32)
+                   lambda c, h: slice(c + 16 * h, c + 16 * h + 16), len(EARLY[0]))
+    invert("s", "2", T.su2, 16, 32)
     relist("2", "s")
-    ts(["a7"], ["a8"], a[8], a[7], 448, OP.bitwise_and)
+    same("s", "2", T.mb)
     tt(["a6", "a8"], ["a9"], a[9], a[6], a[8], OP.add)
     vcopy(["a9"], ["au"], T.au[:, :], a[9])
 
-    ka = []
-    for i, s in enumerate(sorted(got)):
-        c, n = 512 * (got[s][0] // 2), BY_PE[i]
-        run("v", V.transpose, ["land" + s, "ame"], ["ta%d" % c], T.ta[:, c:c + 64], T.lpa[:, c // 8:c // 8 + 64])
-        for d in range(n + 1, 8):
-            dma("y", "rota%d" % i, ["ta%d" % c], ["tad%d" % c], T.ta[0:128 - 16 * d, c + 64 * d:c + 64 * d + 64], T.ta[16 * d:128, c:c + 64])
-            dma("y", "rota%d" % i, ["ta%d" % c], ["tad%d" % c], T.ta[128 - 16 * d:128, c + 64 * d:c + 64 * d + 64], T.ta[0:16 * d, c:c + 64])
-        parts = [(d0, d1) for d0, d1 in ((1, min(n, 4) + 1), (5, n + 1)) if d1 > d0]
-        for j, (d0, d1) in enumerate(parts):
-            b = (2 * i + j) % 5
-            for d in range(d0, d1):
-                mm(["ta%d" % c, "i2f"], ["ps%d" % b], bank(b)[:, 64 * (d - d0):64 * (d - d0) + 64], T.i2f[:, 16 * d:16 * d + 128], T.ta[:, c:c + 64])
-        if i in (1, 2):
-            h = i - 1
+    def spread(i):
+        if i in SPREAD:
+            h = SPREAD.index(i)
             vcopy(["p1t%d" % h, "lnu", "Z1"] + ["Z1s0"] * h, ["Z1s%d" % h], T.Z1[:, :].indirect(T.lnu[:, 8 * h:8 * h + 8]), T.lq1[:, 128 * h:128 * h + 128])
-        for j, (d0, d1) in enumerate(parts):
-            b = (2 * i + j) % 5
-            copy("sv"[j], ["ps%d" % b], ["tap%d" % (c + d0)], T.ta[:, c + 64 * d0:c + 64 * d1], bank(b)[:, 0:64 * (d1 - d0)])
-            ka.append("tap%d" % (c + d0))
-        ka += ["ta%d" % c, "tad%d" % c]
+
+    def widen(i, c):
+        k0, k1 = "ta%d" % c, "tb%d" % c
+        copy(HALF[i][0], ["ps%d" % i], [k1], T.ta[:, c + 64:c + 256], bank(i)[:, 0:192])
+        for p, q in zip((0, 64), HALF[i][1:]):
+            out, in_ = T.ta[p:p + 64, c + 256:c + 512], T.ta[64 - p:128 - p, c:c + 256]
+            if q == "y":
+                dma(q, "rota%d" % i, [k0, k1], ["tc%d" % (c + p)], out, in_)
+            else:
+                copy(q, [k0, k1], ["tc%d" % (c + p)], out, in_)
+
+    ka = []
+    spread(-1)
+    pairs = {}
+    for s in sorted(got):
+        for q in got[s]:
+            pairs.setdefault(q // 2, []).append("land" + s)
+    for i, u in enumerate(sorted(pairs, key=lambda u: max(pairs[u]))):
+        c = 512 * u
+        run("v", V.transpose, pairs[u] + ["ame"] * (u == me // 2), ["ta%d" % c], T.ta[:, c:c + 64], T.lpa[:, c // 8:c // 8 + 64])
+        spread(i)
+        for d in range(1, 4):
+            mm(["ta%d" % c, "i2f"], ["ps%d" % i], bank(i)[:, 64 * d - 64:64 * d], T.i2f[:, 16 * d:16 * d + 128], T.ta[:, c:c + 64])
+        if ka:
+            widen(i - 1, ka[-1])
+        ka.append(c)
+    listed("2")
+    widen(len(ka) - 1, ka[-1])
+    ka = [k % (c + p) for c in ka for k, p in (("ta%d", 0), ("tb%d", 0), ("tc%d", 0), ("tc%d", 64))]
     kz = ["Z1", "Z1s0", "Z1s1"]
 
     tt(ka + ["au", "wp"], ["pr2"], T.pr2[:, :], T.ta[:, :].indirect(T.au[:, :]), T.wp[:, :], OP.mult)
     columns("ya", lambda c: kz, T.Z1, 0, 5)
-    listed("2")
+    columns("ya", lambda c: kz, T.Z1, 1, 7, 0, YA)
+    invert("s", "3", T.lsu, 0, 16)
+    relist("3")
     slot_sums("p2", "2", T.mb, T.pr2, T.sg2, T.G1, T.r2, T.lp2)
-    columns("ya", lambda c: kz, T.Z1, 1, 7)
+    columns("ya", lambda c: kz, T.Z1, 1, 7, YA, 8)
     store("ya", 0, 5, 6, "s", T.ua, T.ya3, T.ya, "oya", "y")
     store("ya", 1, 7, 4, "v", T.ua, T.ya3, T.ya, "oya", "y")
+    fill("lq20", T.lq2[:, 256:520], 0.0)
     listed("3")
 
     sums_in("p2", T.lp2, lambda h, b, key, c, ps: copy("vs"[h], [b], [key], T.lq2[:, c], ps))

from concourse.bass import DstId, RemoteDMATransfer
from concourse.mybir import AluOpType as OP, ActivationFunctionType as AF

F, B, I, U = "float32", "bfloat16", "int32", "uint16"


def sb(n, d=F):
    return ("sbuf", [128, n], d)


SCRATCH = {
    "win": sb(2048, B), "lt": sb(64, I), "lu": sb(64, U), "g0": sb(1024, B), "fas": sb(256, B),
    "xt": sb(160, I), "xr": sb(96, I), "xo": sb(96, I), "xu": sb(96, U),
    "obt": sb(32, I), "obu": sb(32, U), "vin": sb(512), "vr": sb(512),
    "sndd": ("dram", [1024, 32], B), "landd": ("dram", [1024, 32], B),
    "sndc": ("dram", [1024, 32], B), "landc": ("dram", [1024, 32], B),
    "sndb": ("dram", [1024, 32], B), "landb": ("dram", [1024, 32], B),
    "pc": sb(8, I), "dj": sb(16, I), "jt": sb(32, I), "pi": sb(8, I), "pg": sb(8, I), "col": sb(16),
    "di": sb(16, I), "d16": sb(16), "one": sb(256), "i2f": sb(256), "i2b": sb(256, B),
    "sh0": sb(128), "gf0": sb(128), "sh1": sb(128), "sh2": sb(128), "b8": sb(128), "gf": sb(128), "jf": sb(32), "pos": sb(512), "pos0": sb(256),
    "kt": sb(32, I), "pu": sb(8, U), "tu": sb(32, U), "mw": sb(8), "fl1": sb(128), "fl3": sb(128, B), "fra": sb(2048, B),
    "W4": sb(2048, B), "cf": sb(256), "ef4": sb(128), "eu4": sb(128, U), "lnt": sb(16, U),
    "ai": sb(32, I), "aw": sb(320, I),
    "xf": sb(104), "xq": sb(64, I), "xs": sb(64), "xc1": sb(64), "lsu": sb(32, U), "lnu": sb(16, U),
    "eq1": sb(32), "eq2": sb(32), "equ1": sb(32, U), "equ2": sb(32, U), "dm": sb(32), "of": sb(32), "su1": sb(32, U), "su2": sb(32, U),
    "ma": sb(520), "mb": sb(520), "W1": sb(2688), "W2": sb(2688), "W3": sb(2048),
    "ef1": sb(128), "ef2": sb(128), "ef3": sb(128), "eu1": sb(128, U), "eu2": sb(128, U), "eu3": sb(128, U),
    "ly": sb(128),
    "oq": sb(32, I), "os1": sb(32), "oc": sb(32), "otu": sb(32, U), "wx": sb(512, I), "q1": sb(512), "q2": sb(512),
    "xal": sb(32), "xbl": sb(40), "au": sb(32, U), "bi": sb(32, I), "bq": sb(32, I), "bs": sb(32), "bc": sb(32),
    "td": sb(2048, B), "tc": sb(2048, B), "tb": sb(2048, B), "ta": sb(2048),
    "w1": sb(512), "w2": sb(512), "wp": sb(512), "pr1": sb(512), "pr2": sb(512), "sg1": sb(520), "sg2": sb(520),
    "G1": sb(2048), "G2": sb(2048), "Z1": sb(2048),
    "r1": sb(256), "r2": sb(256), "ra": sb(256), "ua": sb(256), "ub": sb(256), "ya3": sb(256), "yb3": sb(256),
    "lp1": sb(256), "lq1": sb(264), "lp2": sb(256), "lq2": sb(520), "lpa": sb(256),
    "ps0": ("psum", [128, 512], F), "ps1": ("psum", [128, 512], F), "ps2": ("psum", [128, 512], F), "ps3": ("psum", [128, 512], F),
    "ps4": ("psum", [128, 512], F), "ps5": ("psum", [128, 512], F), "ps6": ("psum", [128, 512], F), "ps7": ("psum", [128, 512], F),
}
SEMAPHORES = (["c_g", "c_v", "c_s", "c_p", "ldw", "ldl", "ldx", "ldn", "ldo", "ldv", "ldy", "ldz", "fas", "fil1", "fil2", "fil3",
               "ef1", "ef2", "ef3", "wx", "xal", "xbl", "oya", "oyb", "arrp1", "arrp2", "fil4", "ef4", "inv",
               "rota0", "rota1", "rota2", "rota3"]
              + [k + x for x in "dcb" for k in ("self", "arr", "loc", "cmp", "rot")] + ["snd" + x + h for x in "dcb" for h in "01"]
              + ["loc" + x for x in ("p1", "a", "p2")] + ["arra%d" % k for k in range(7)])
LATE, EARLY = ((1, 2, 2, 1), 3), ((1, 1, 2, 2), 1)
AHEAD = (2, 2)
YA = 4
LIFT = 32
HALF = ("vyy", "vyy", "sss", "vvs")
SPREAD = (-1, 3)


def long_call(src, cores, topo):
    off = [d for d in cores if topo.chip(d) != topo.chip(src)]
    far = [d for d in off if not topo.mates(topo.chip(src), topo.chip(d)) and not topo.same_plane(topo.chip(src), topo.chip(d))]
    near = [d for d in off if d not in far]
    e = topo.engines(src, near[0])
    one, two = e[0::2], e[1::2]
    n = len(two) // len(far)
    call = [(d, [one[i]]) for i, d in enumerate(near)] + [(d, two[i * n:(i + 1) * n]) for i, d in enumerate(far)]
    on = [d for d in cores if d != src and d not in off]
    return call + [(d, [x for x in topo.engines(src, d) if x not in e][i:i + 1]) for i, d in enumerate(on)]


def plan_calls(src, cores, topo, sizes, home):
    off = [d for d in cores if topo.chip(d) != topo.chip(src)]
    on = [d for d in cores if d != src and topo.chip(d) == topo.chip(src)]
    off.sort(key=lambda d: (topo.same_plane(topo.chip(src), topo.chip(d)), topo.mates(topo.chip(src), topo.chip(d)), topo.die(d) != topo.die(src)))
    e = topo.engines(src, off[0])
    calls = []
    for m in sizes:
        n = len(e) // max(m, 1)
        calls.append([(off.pop(0), e[j * n:j * n + n]) for j in range(m)])
    for d in on:
        calls[home].append((d, [x for x in topo.engines(src, d) if x not in e][0:len(e) // 2]))
    return calls


def rank_program(g, core, T, topo):
    me = T.rank_of(core)
    if me is None:
        return
    cores = list(T.cores)
    eng = {"g": g, "v": g.vector, "s": g.scalar, "p": g.tensor, "y": g.sync}
    seen = {q: {} for q in eng}
    cnt, WR, RD = {}, {}, {}

    def need(q, toks):
        m = {}
        for s, n in toks:
            n = cnt[s] if n is None else n
            m[s] = max(m.get(s, 0), n)
        for s in m:
            if seen[q].get(s, 0) < m[s]:
                eng[q].wait_ge(T.sem[s], m[s])
                seen[q][s] = m[s]

    def before(q, rd, wr, own=None):
        own = own or q
        toks = []
        for k in rd:
            toks += [t for _, t in WR.get(k, [])]
            if k[:2] == "ps":
                toks += [t for o, t in RD.get(k, []) if o != own]
        for k in wr:
            toks += [t for o, t in WR.get(k, []) + RD.get(k, []) if o != own]
        need(q, toks)

    def after(o, tok, rd, wr):
        for k in rd:
            RD.setdefault(k, []).append((o, tok))
        for k in wr:
            WR.setdefault(k, []).append((o, tok))

    def run(q, fn, rd, wr, *a, **k):
        before(q, rd, wr)
        s = "c_" + q
        cnt[s] = cnt.get(s, 0) + 1
        fn(*a, **k).then_inc(T.sem[s], 1)
        after(q, (s, cnt[s]), rd, wr)

    def dma(q, sem, rd, wr, out, in_):
        before(q, rd, wr, "d" + sem)
        cnt[sem] = cnt.get(sem, 0) + 16
        eng[q].dma_start(out, in_).then_inc(T.sem[sem], 16)
        after("d" + sem, (sem, None), rd, wr)

    V, S, P = g.vector, g.scalar, g.tensor

    def ts(rd, wr, out, in0, s1, op0, s2=None, op1=None):
        if op1 is None:
            run("v", V.tensor_scalar, rd, wr, out, in0, s1, None, op0)
        else:
            run("v", V.tensor_scalar, rd, wr, out, in0, s1, s2, op0, op1)

    def tt(rd, wr, out, a, b, op):
        run("v", V.tensor_tensor, rd, wr, out, a, b, op)

    def vcopy(rd, wr, out, in_):
        run("v", V.tensor_copy, rd, wr, out, in_)

    def scopy(rd, wr, out, in_):
        run("s", S.activation, rd, wr, out, in_, AF.Copy)

    def copy(q, rd, wr, out, in_):
        (vcopy if q == "v" else scopy)(rd, wr, out, in_)

    def fill(key, ap, c):
        run("v", V.memset, [], [key], ap, c)

    def mm(rd, wr, out, lhsT, rhs, start=True, stop=True):
        run("p", P.matmul, rd, wr, out, lhsT, rhs, start, stop)

    def bank(i):
        return T["ps%d" % i]

    def iota(key, out, pattern, base, cm):
        if out.dtype == T.pos.dtype:
            run("g", g.iota, [], [key], out[:, :], pattern, base, cm, allow_small_or_imprecise_dtypes=True)
        else:
            run("g", g.iota, [], [key], out[:, :], pattern, base, cm)

    def select(key, out, src, skey, pattern, op, base, cm):
        run("g", g.affine_select, [skey], [key], out[:, :], src[:, 0:128], pattern, op, 0.0, base, cm)

    def send(x, call, k, key, src, dst, sem):
        trs = []
        for j, (d, es) in enumerate(call):
            rid, pid, _ = topo.addr(d)
            trs.append(RemoteDMATransfer(dst_ids=[DstId(rid=rid, pnc=pid)], dma_engine_mask=sum(1 << e for e in es),
                                         remote_sem=T.sem[sem(core, d, k)], src=src(j, cores.index(d)), dst=dst))
        before("g", key, [])
        g.remote_dma_fused(trs, local_sem=T.sem["loc" + x])
        cnt["loc" + x] = cnt.get("loc" + x, 0) + sum(len(es) for _, es in call)

    def arrivals(calls, sem):
        got = {}
        for c in cores:
            for k, call in enumerate(calls[c]):
                for d, es in call:
                    if d == core:
                        s = sem(c, d, k)
                        cnt[s] = cnt.get(s, 0) + len(es)
                        got.setdefault(s, []).append(cores.index(c))
        for s in got:
            after("remote", (s, None), [], ["land" + s])
        return got

    def by_call(x):
        return lambda c, d, k: "arr%s%d" % (x, 0 if topo.chip(c) == topo.chip(d) else k + 1)

    late, early = [{c: plan_calls(c, cores, topo, *p) for c in cores} for p in (LATE, EARLY)]

    def factor(f, x):
        for e in range(2):
            dma("ys"[e], "ldw", [], ["win"], T.win[32 * f + 16 * e:32 * f + 16 * e + 16, :], x[:, :])

    factor(0, T.fd)
    factor(1, T.fc)
    for f, l in enumerate((T.ld, T.lc, T.lb)):
        for u in range(4):
            dma("ys"[u % 2], "ldl", [], ["lt"], T.lt[32 * f:32 * f + 32, 16 * u:16 * u + 16], l[32 * u:32 * u + 32, :])
    factor(2, T.fb)
    fill("win0", T.win[96:128, 0:16], 0.0)
    fill("lt0", T.lt[96:128, :], 0)
    dma("y", "ldx", [], ["xta"], T.xt[:, 0:32], T.xa[:, :])
    dma("s", "ldo", [], ["obt"], T.obt[:, :], T.ob[:, :])

    fill("one", T.one[:, :], 1.0)
    iota("pc", T.pc, [[0, 8]], 0, 1)
    iota("kt", T.kt, [[1, 16], [256, 2]], 0, 0)
    iota("dj", T.dj, [[1, 16]], 128, -1)
    iota("jt", T.jt, [[16, 32]], 2048, 1)
    select("sh0", T.sh0, T.one, "one", [[-1, 128]], OP.is_equal, -1, 1)
    select("sh2", T.sh2, T.one, "one", [[-16, 8], [256, 16]], OP.is_equal, -256 * 15, 1)
    select("sh1", T.sh1, T.sh0, "sh0", [[0, 8], [1, 16]], OP.not_equal, -15, 0)
    iota("pos", T.pos, [[1, 512]], LIFT, 0)
    select("b8", T.b8, T.one, "one", [[-1, 8], [0, 16]], OP.is_equal, 0, 1)
    iota("pos0", T.pos0, [[1, 256]], 0, 0)
    fill("fl1", T.fl1[:, :], 512.0 + LIFT)
    fill("wx", T.wx[:, :], 0)
    fill("fl3", T.fl3[:, :], 256.0)
    fill("xf", T.xf[:, 32:33], -1.0)
    fill("mw", T.mw[:, 0:1], 0.0)
    fill("mw", T.mw[:, 1:8], 1.0)
    ts(["pc"], ["pi"], T.pi[:, 0:1], T.pc[:, 0:1], 15, OP.bitwise_and)
    ts(["pc"], ["pg"], T.pg[:, 0:1], T.pc[:, 0:1], 4, OP.logical_shift_right)
    ts(["dj"], ["di"], T.di[:, :], T.dj[:, 0:16], 15, OP.bitwise_and)
    ts(["jt"], ["jf"], T.jf[:, :], T.jt[:, :], 1.0 / 128, OP.mult)
    ts(["pi"], ["p16"], T.col[:, 7:8], T.pi[:, 0:1], 16.0, OP.mult)
    vcopy(["pi"], ["pif"], T.col[:, 6:7], T.pi[:, 0:1])
    ts(["pg"], ["rc"], T.col[:, 5:6], T.pg[:, 0:1], -256.0, OP.mult, 2048.0, OP.add)
    ts(["pg"], ["rc4"], T.col[:, 8:9], T.pg[:, 0:1], -64.0, OP.mult, 512.0, OP.add)
    ts(["di"], ["d16"], T.d16[:, :], T.di[:, :], 0.0, OP.is_equal)
    ts(["kt", "p16"], ["tu"], T.tu[:, :], T.kt[:, :], T.col[:, 7:8], OP.add)
    ts(["one", "pif"], ["pu"], T.pu[:, :], T.one[:, 0:8], T.col[:, 6:7], OP.mult)
    for key, ap in (("ma0", T.ma[:, 0:1]), ("mb0", T.mb[:, 0:1]), ("sg10", T.sg1[:, 512:520]), ("sg20", T.sg2[:, 512:520]), ("lq10", T.lq1[:, 256:264])):
        fill(key, ap, 0.0)
    fill("xbl1", T.xbl[:, 32:33], -1.0)
    vcopy(["lt", "lt0"], ["lu"], T.lu[:, :], T.lt[:, :])

    dma("y", "ldz", [], ["xtl"], T.xt[:, 32:48], T.la[:, :])
    dma("y", "ldz", [], ["xtl"], T.xt[:, 48:64], T.lb[:, :])
    dma("y", "fil1", ["fl1"], ["W1"], T.W1[0::16, 0:2048], T.fl1[:, :])
    dma("y", "ldv", [], ["vin"], T.vin[0:8, :], T.v[:, :])
    dma("y", "wx", [], ["wx"], T.wx[1::16, :], T.xa[:, :])
    dma("y", "wx", [], ["wx"], T.wx[2::16, :], T.xb[:, :])

    for u in range(4):
        copy("vs"[u % 2], ["win", "win0", "lu"], ["g0%d" % u], T.g0[:, 256 * u:256 * u + 256], T.win[:, :].indirect(T.lu[:, 16 * u:16 * u + 16]))

    wide = {c: [long_call(c, cores, topo)] for c in cores}

    def stage(x, f, q):
        snd, land = T["snd" + x], T["land" + x]
        for u in range(4):
            k = "snd%s%d" % (x, u // 2)
            dma(q, k, ["g0%d" % u], [k], snd[256 * u:256 * u + 256, :], T.g0[32 * f:32 * f + 32, 256 * u:256 * u + 256])
        p, u = 32 * f + 16 * (me % 2), me // 2
        dma(q, "self" + x, ["g0%d" % u], ["landarr" + x], land[128 * me:128 * me + 128, :], T.g0[p:p + 16, 256 * u:256 * u + 256])

    stage("d", 0, "y")
    stage("c", 1, "s")
    stage("b", 2, "y")
    for x in "dcb":
        for halves in ([0], [1]) if x == "d" else ([0, 1],):
            send(x, [(d, es) for d, es in wide[core][0] if cores.index(d) // 4 in halves], 0, ["snd%s%d" % (x, h) for h in halves],
                 lambda j, r: T["snd" + x][128 * r:128 * r + 128, :], T["land" + x][128 * me:128 * me + 128, :], lambda c, d, k: "arr" + x)
        arrivals(wide, lambda c, d, k: "arr" + x)
    select("gf0", T.gf0, T.one, "one", [[-16, 8], [0, 16]], OP.is_ge, 0, 1)
    run("g", g.affine_select, ["one"], ["i2b"], T.i2b[:, :], T.one[:, :], [[0, 2], [-1, 128]], OP.is_equal, 0.0, 0, 1)
    select("gf", T.gf, T.gf0, "gf0", [[16, 8], [0, 16]], OP.is_ge, 15, -1)
    run("g", g.affine_select, ["one"], ["i2f"], T.i2f[:, :], T.one[:, :], [[0, 2], [-1, 128]], OP.is_equal, 0.0, 0, 1)
    iota("Z1", T.Z1, [[0, 2048]], 0, 0)

    def following(xkey, x, b):
        k = "ps%d" % b
        mm(xkey + ["sh1"], [k], bank(b)[:, 0:32], T.sh1[:, :], x[:, 0:32], True, False)
        mm(xkey + ["sh2"], [k], bank(b)[:, 0:32], T.sh2[:, :], x[:, 1:33], False, True)

    def turned(*lists):
        for key, x, xq, xs, xc, out, m, more in lists:
            ts([key] + more, [out + "q"], xq, x, 4, OP.logical_shift_right)
        for key, x, xq, xs, xc, out, m, more in lists:
            ts([out + "q"], [out + "s"], xs, xq, 1.0 / m - 16, OP.mult)
        for key, x, xq, xs, xc, out, m, more in lists:
            tt([key, out + "s"], [out], xc, x, xs, OP.add)

    def ends(n, xkey, x, b, ckey, c, between):
        eq, equ, su = T["eq" + n], T["equ" + n], T["su" + n]
        tt(xkey + ["ps%d" % b], ["eq" + n], eq[:, :], x[:, 0:32], bank(b)[:, 0:32], OP.is_equal)
        between[0]()
        tt(["eq" + n, "jf"], ["dm"], T.dm[:, :], eq[:, :], T.jf[:, :], OP.mult)
        vcopy(["eq" + n], ["equ" + n], equ[:, :], eq[:, :])
        tt(["dm", ckey], ["of"], T.of[:, :], T.dm[:, :], c, OP.max)
        between[1]()
        ts(["of"], ["su" + n], su[:, :], T.of[:, :], 128.0, OP.mult)

    def invert(q, n, su, c0, c1):
        rd, wr, out, in_ = ["pos", "su" + n, "W" + n], ["W" + n + "s"], T["W" + n][:, :].indirect(su[:, c0:c1]), T.pos[:, 16 * c0:16 * c1]
        if q == "v":
            vcopy(rd, wr, out, in_)
        else:
            run("s", S.activation, rd, wr, out, in_, AF.Silu)

    def relist(n, q="y"):
        dma(q, "ef" + n, ["W" + n, "W" + n + "s"], ["ef" + n], T["ef" + n][:, :], T["W" + n][0::16, 0:2048])

    def listed(n):
        ts(["ef" + n], ["eu" + n], T["eu" + n][:, :], T["ef" + n][:, :], 0.25 - LIFT, OP.add)

    def same(q, n, m):
        copy(q, ["mw", "equ" + n], ["m" + n], m[:, 1:513], T.mw[:, :].indirect(T["equ" + n][:, :]))

    dma("s", "fil4", ["fl3"], ["W4"], T.W4[0::16, :], T.fl3[:, :])
    dma("y", "ldn", [], ["xtc"], T.xt[:, 64:96], T.xb[:, :])
    dma("y", "ldn", [], ["xtc"], T.xt[:, 96:128], T.xc[:, :])
    dma("y", "ldn", [], ["xtc"], T.xt[:, 128:160], T.xd[:, :])
    vcopy(["xta"], ["xf"], T.xf[:, 0:32], T.xt[:, 0:32])
    following(["xf"], T.xf, 7)
    mm(["b8", "vin"], ["ps6"], bank(6)[:, :], T.b8[0:8, :], T.vin[0:8, :])
    turned(("xta", T.xt[:, 0:64], T.xq[:, :], T.xs[:, :], T.xc1[:, :], "xc1", 128, ["xtl"]),
           ("obt", T.obt[:, :], T.oq[:, :], T.os1[:, :], T.oc[:, :], "oc", 32, []))
    ends("1", ["xf"], T.xf, 7, "xc1", T.xc1[:, 0:32], [
        lambda: ts(["oc"], ["otu"], T.otu[:, :], T.oc[:, :], 32.0, OP.mult),
        lambda: vcopy(["xtl"], ["lnu"], T.lnu[:, :], T.xt[:, 32:48])])
    invert("s", "1", T.su1, 0, 32)
    scopy(["ps6"], ["vr"], T.vr[:, :], bank(6)[:, :])
    vcopy(["xtl"], ["laf"], T.xf[:, 72:88], T.xt[:, 32:48])
    vcopy(["wx", "otu"], ["q1"], T.q1[:, :], T.wx[:, :].indirect(T.otu[:, :]))
    vcopy(["pos0", "lnu", "W4"], ["W4s"], T.W4[:, :].indirect(T.lnu[:, :]), T.pos0[:, :])
    dma("y", "fil2", ["fl1", "W4s"], ["W2"], T.W2[0::16, 0:2048], T.fl1[:, :])
    dma("y", "fil3", ["fl1"], ["W3"], T.W3[0::16, 0:2048], T.fl1[:, :])
    ts(["xtc", "rc"], ["xr"], T.xr[:, :], T.xt[:, 64:160], T.col[:, 5:6], OP.add)
    ts(["xc1"], ["su3"], T.lsu[:, 0:16], T.xc1[:, 48:64], 128.0, OP.mult)
    ts(["xr"], ["xo"], T.xo[:, :], T.xr[:, :], 2047, OP.bitwise_and)
    tt(["laf", "pu", "gf"], ["ly"], T.ly[:, :], T.xf[:, 72:88].indirect(T.pu[:, :]), T.gf[:, :], OP.mult)
    mm(["d16", "ly"], ["ps5"], bank(5)[:, 0:16], T.ly[:, :], T.d16[:, :])
    vcopy(["xo"], ["xu"], T.xu[:, :], T.xo[:, :])
    vcopy(["obt"], ["obu"], T.obu[:, :], T.obt[:, :])
    vcopy(["ps5"], ["lnt"], T.lnt[:, :], bank(5)[:, 0:16])
    same("v", "1", T.ma)

    def table(x, t, first, groups):
        land, key, w = T["land" + x], "landarr" + x, 256
        for z in first:
            dma("y", "cmp" + z, ["landarr" + z], [z + "0"], T["t" + z][:, 0:w], T["land" + z][:, :])
        byp = [d for _, ds, _ in groups for d in ds]
        for d in range(1, 8):
            if d not in byp:
                dma("y", "rot" + x, [key], ["%s%d" % (x, d)], t[0:128 - 16 * d, d * w:(d + 1) * w], land[128 * d:1024, :])
                dma("y", "rot" + x, [key], ["%s%d" % (x, d)], t[128 - 16 * d:128, d * w:(d + 1) * w], land[0:128 * d, :])
        for b, ds, q in groups:
            n = len(ds)
            for i, d in enumerate(ds):
                mm(["i2b", x + "0"], ["ps%d" % b], bank(b)[:, i * w:(i + 1) * w], T.i2b[:, 16 * d:16 * d + 128], t[:, 0:w])
            copy(q, ["ps%d" % b], ["%s%d" % (x, d) for d in ds], t[:, ds[0] * w:(ds[0] + n) * w], bank(b)[:, 0:n * w])
        return ["%s%d" % (x, d) for d in range(8)]

    kd = table("d", T.td, "d", ((0, (1,), "s"), (1, (2,), "v"), (2, (3,), "s"), (4, (4,), "v"), (5, (5,), "s")))
    tt(kd + ["xu", "vr"], ["w1"], T.w1[:, :], T.td[:, :].indirect(T.xu[:, 64:96]), T.vr[:, :], OP.mult)
    kc = table("c", T.tc, "cb", ((3, (1, 2), "s"), (7, (3,), "s")))
    tt(kc + ["xu", "w1"], ["w2"], T.w2[:, :], T.tc[:, :].indirect(T.xu[:, 32:64]), T.w1[:, :], OP.mult)
    kb = table("b", T.tb, "", ((0, (1, 2), "s"), (1, (3, 4), "s")))
    relist("1")
    for k in range(8):
        dma("y", "inv", ["W4", "W4s"], kd + ["wi"], T.td[16 * k:16 * k + 8, :], T.W4[0::16, :])
    for k in range(8):
        dma("y", "fas", [], ["fra"], T.fra[16 * k:16 * k + 16, :], T.fa[:, :])
    tt(kb + ["xu", "w2"], ["pr1"], T.pr1[:, :], T.tb[:, :].indirect(T.xu[:, 0:32]), T.w2[:, :], OP.mult)
    listed("1")
    scopy(["q1", "tu"], ["q2"], T.q2[:, :], T.q1[:, :].indirect(T.tu[:, :]))
    scopy(["wi", "lnt"], ["cf"], T.cf[:, :], T.td[:, :].indirect(T.lnt[:, :]))
    for k in range(8):
        dma("y", "ef4", ["cf"], ["ef4"], T.ef4[:, 16 * k:16 * k + 16], T.cf[16 * k:16 * k + 8, :])
    dma("y", "xbl", ["q2"], ["xbl"], T.xbl[:, 0:32], T.q2[2::16, :])
    dma("y", "xal", ["q2"], ["xal"], T.xal[:, :], T.q2[1::16, :])

    def sums_out(x, keys, src, lst, G, r, lp, calls, sem, cols, home):
        def pick(q, h):
            c = 256 * q + 128 * h
            copy("vs"[h], keys, ["%sG%d" % (x, c)], G[:, c:c + 128], src.indirect(lst[:, c // 16:c // 16 + 8]))

        def add(q, b, c):
            for h in range(2):
                mm(["%sG%d" % (x, 256 * q + 128 * h), "d16"], ["ps%d" % b], bank(b)[:, cols(c, h)],
                   G[:, 256 * q + 128 * h:256 * q + 128 * h + 128], T.d16[:, 0:16])
        steps = list(enumerate(calls[core]))
        steps.insert(home, (None, [(core, [])]))
        order = [cores.index(d) for _, call in steps for d, _ in call]
        picked = done = pos = 0
        for i, (k, call) in enumerate(steps):
            n, b = len(call), i % 5
            for q in order[picked:done + n]:
                pick(q, 0)
                pick(q, 1)
            picked = max(picked, done + n)
            for j, q in enumerate(order[done:done + n]):
                add(q, b, 32 * j)
            done += n
            for q in order[picked:done + AHEAD[min(i, 1)]]:
                pick(q, 0)
                pick(q, 1)
            picked = max(picked, done + AHEAD[min(i, 1)])
            if k is None:
                copy("vs"[i % 2], ["ps%d" % b], [x + "me"], lp[:, 32 * me:32 * me + 32], bank(b)[:, 0:32])
            else:
                copy("vs"[i % 2], ["ps%d" % b], ["%sr%d" % (x, k)], r[:, pos:pos + 32 * n], bank(b)[:, 0:32 * n])
                send(x, call, k, ["%sr%d" % (x, k)], lambda j, q: r[:, pos + 32 * j:pos + 32 * j + 32], lp[:, 32 * me:32 * me + 32], sem)
                pos += 32 * n
        return arrivals(calls, sem)

    def slot_sums(x, n, m, pr, sg, G, r, lp):
        run("v", V.tensor_tensor_scan, ["m" + n, {"1": "ma0", "2": "mb0"}[n], "pr" + n], ["sg" + n], sg[:, 0:512], m[:, 0:512], pr[:, :], 0.0, OP.mult, OP.add)
        sums_out(x, ["sg" + n, "sg" + n + "0", "eu" + n], sg[:, :], T["eu" + n], G, r, lp, late, lambda c, d, k: "arr" + x,
                 lambda c, h: slice(c + h, c + 32, 2), len(LATE[0]))

    def sums_in(x, lp, out):
        for h in range(2):
            mm(["landarr" + x, x + "me", "i2f"], ["ps%d" % (5 + h)], bank(5 + h)[:, 0:128], lp[:, h::2], T.i2f[:, 0:128])
            out(h, "ps%d" % (5 + h), "%st%d" % (x, h), slice(128 * h, 128 * h + 128), bank(5 + h)[:, 0:128])

    def columns(x, keys, z, h, b, j0=0, j1=8):
        for j in range(j0, j1):
            c = 1024 * h + 128 * j
            mm(keys(c) + ["d16"], ["ps%d" % b], bank(b)[:, j:128:8], z[:, c:c + 128], T.d16[:, 0:16])

    def store(x, h, b, b2, q, u, y3, y, sem, dq):
        c = slice(128 * h, 128 * h + 128)
        copy(q, ["ps%d" % b], ["%su%d" % (x, h)], u[:, c], bank(b)[:, 0:128])
        mm(["%su%d" % (x, h), "i2f"], ["ps%d" % b2], bank(b2)[:, 0:128], u[:, c], T.i2f[:, 0:128])
        copy(q, ["ps%d" % b2], ["%sy%d" % (x, h)], y3[:, c], bank(b2)[:, 0:128])
        dma(dq, sem, ["%sy%d" % (x, h)], [], y[:, 1024 * h:1024 * h + 1024], y3[:, c])

    slot_sums("p1", "1", T.ma, T.pr1, T.sg1, T.G1, T.r1, T.lp1)

    following(["xbl", "xbl1"], T.xbl, 7)
    scopy(["fra", "lnu"], ["fas"], T.fas[:, :], T.fra[:, :].indirect(T.lnu[:, :]))
    scopy(["w2", "obu"], ["wp"], T.wp[:, :], T.w2[:, :].indirect(T.obu[:, :]))
    a = [T.aw[:, 32 * k:32 * k + 32] for k in range(10)]
    vcopy(["xbl"], ["bi"], T.bi[:, :], T.xbl[:, 0:32])
    vcopy(["xal"], ["ai"], T.ai[:, :], T.xal[:, :])
    ts(["bi"], ["bq"], T.bq[:, :], T.bi[:, :], 4, OP.logical_shift_right)
    ts(["ai"], ["a1"], a[1], T.ai[:, :], 4, OP.logical_shift_right, 6, OP.bitwise_and)
    ts(["bq"], ["bs"], T.bs[:, :], T.bq[:, :], 1.0 / 128 - 16, OP.mult)
    ts(["ai"], ["a2"], a[2], T.ai[:, :], 7, OP.logical_shift_right, 1, OP.bitwise_and)
    tt(["bi", "bs"], ["bc"], T.bc[:, :], T.bi[:, :], T.bs[:, :], OP.add)
    ends("2", ["xbl", "xbl1"], T.xbl, 7, "bc", T.bc[:, :], [
        lambda: ts(["ai"], ["a3"], a[3], T.ai[:, :], 0x61F, OP.bitwise_and),
        lambda: ts(["ai"], ["a4"], a[4], T.ai[:, :], 3, OP.logical_shift_right, 32, OP.bitwise_and)])
    invert("s", "2", T.su2, 0, 16)
    tt(["a1", "a2"], ["a5"], a[5], a[1], a[2], OP.add)
    vcopy(["ef4"], ["eu4"], T.eu4[:, :], T.ef4[:, :])
    ts(["a5", "rc4"], ["a7"], a[7], a[5], 64.0, OP.mult, T.col[:, 8:9], OP.add)
    tt(["a3", "a4"], ["a6"], a[6], a[3], a[4], OP.add)
    ts(["a7"], ["a8"], a[8], a[7], 448, OP.bitwise_and)

    sums_in("p1", T.lp1, lambda h, b, key, c, ps: tt([b, "fas"], [key], T.lq1[:, c], ps, T.fas[:, c], OP.mult))
    got = sums_out("a", ["p1t0", "p1t1", "lq10", "eu4"], T.lq1[:, :], T.eu4, T.G2, T.ra, T.lpa, early, by_call("a"),
                   lambda c, h: slice(c + 16 * h, c + 16 * h + 16), len(EARLY[0]))
    invert("s", "2", T.su2, 16, 32)
    relist("2", "s")
    same("s", "2", T.mb)
    tt(["a6", "a8"], ["a9"], a[9], a[6], a[8], OP.add)
    vcopy(["a9"], ["au"], T.au[:, :], a[9])

    def spread(i):
        if i in SPREAD:
            h = SPREAD.index(i)
            vcopy(["p1t%d" % h, "lnu", "Z1"] + ["Z1s0"] * h, ["Z1s%d" % h], T.Z1[:, :].indirect(T.lnu[:, 8 * h:8 * h + 8]), T.lq1[:, 128 * h:128 * h + 128])

    def widen(i, c):
        k0, k1 = "ta%d" % c, "tb%d" % c
        copy(HALF[i][0], ["ps%d" % i], [k1], T.ta[:, c + 64:c + 256], bank(i)[:, 0:192])
        for p, q in zip((0, 64), HALF[i][1:]):
            out, in_ = T.ta[p:p + 64, c + 256:c + 512], T.ta[64 - p:128 - p, c:c + 256]
            if q == "y":
                dma(q, "rota%d" % i, [k0, k1], ["tc%d" % (c + p)], out, in_)
            else:
                copy(q, [k0, k1], ["tc%d" % (c + p)], out, in_)

    ka = []
    spread(-1)
    pairs = {}
    for s in sorted(got):
        for q in got[s]:
            pairs.setdefault(q // 2, []).append("land" + s)
    for i, u in enumerate(sorted(pairs, key=lambda u: max(pairs[u]))):
        c = 512 * u
        run("v", V.transpose, pairs[u] + ["ame"] * (u == me // 2), ["ta%d" % c], T.ta[:, c:c + 64], T.lpa[:, c // 8:c // 8 + 64])
        spread(i)
        for d in range(1, 4):
            mm(["ta%d" % c, "i2f"], ["ps%d" % i], bank(i)[:, 64 * d - 64:64 * d], T.i2f[:, 16 * d:16 * d + 128], T.ta[:, c:c + 64])
        if ka:
            widen(i - 1, ka[-1])
        ka.append(c)
    listed("2")
    widen(len(ka) - 1, ka[-1])
    ka = [k % (c + p) for c in ka for k, p in (("ta%d", 0), ("tb%d", 0), ("tc%d", 0), ("tc%d", 64))]
    kz = ["Z1", "Z1s0", "Z1s1"]

    tt(ka + ["au", "wp"], ["pr2"], T.pr2[:, :], T.ta[:, :].indirect(T.au[:, :]), T.wp[:, :], OP.mult)
    columns("ya", lambda c: kz, T.Z1, 0, 5)
    columns("ya", lambda c: kz, T.Z1, 1, 7, 0, YA)
    invert("s", "3", T.lsu, 0, 16)
    relist("3")
    slot_sums("p2", "2", T.mb, T.pr2, T.sg2, T.G1, T.r2, T.lp2)
    columns("ya", lambda c: kz, T.Z1, 1, 7, YA, 8)
    store("ya", 0, 5, 6, "s", T.ua, T.ya3, T.ya, "oya", "y")
    store("ya", 1, 7, 4, "v", T.ua, T.ya3, T.ya, "oya", "y")
    fill("lq20", T.lq2[:, 256:520], 0.0)
    listed("3")

    sums_in("p2", T.lp2, lambda h, b, key, c, ps: copy("vs"[h], [b], [key], T.lq2[:, c], ps))
    for h in range(2):
        for j in range(8):
            c = 1024 * h + 128 * j
            copy("vs"[j % 2], ["p2t0", "p2t1", "lq20", "eu3"], ["bG%d" % c, "aG%d" % c], T.G2[:, c:c + 128], T.lq2[:, :].indirect(T.eu3[:, c // 16:c // 16 + 8]))
    columns("yb", lambda c: ["bG%d" % c], T.G2, 0, 0)
    columns("yb", lambda c: ["bG%d" % c], T.G2, 1, 1)
    store("yb", 0, 0, 2, "s", T.ub, T.yb3, T.yb, "oyb", "y")
    store("yb", 1, 1, 3, "v", T.ub, T.yb3, T.yb, "oyb", "y")

    need("g", [(s, cnt[s]) for s in cnt])
